import numpy as np
import ml_dtypes


def mxq(x, axis, fmt="e4m3"):
    dtype, down = {"e4m3": (ml_dtypes.float8_e4m3fn, 7), "e5m2": (ml_dtypes.float8_e5m2, 14)}[fmt]
    v = np.moveaxis(np.asarray(x, np.float32).astype(ml_dtypes.bfloat16).astype(np.float64), axis, -1)
    blocks = v.reshape(v.shape[:-1] + (-1, 32))
    amax = np.abs(blocks).max(-1, keepdims=True)
    byte = np.maximum(np.where(amax > 0, np.frexp(amax)[1] - 1 + 127, 0) - down, 1)
    scale = np.exp2(byte - 127.0)
    codes = (blocks / scale).astype(np.float32).astype(dtype).astype(np.float64)
    return np.moveaxis((codes * scale).reshape(v.shape), -1, axis)


WIDE = False


def mx_kscale(k):
    if not WIDE:
        return np.ones(k)
    levels = np.array([10, -10, 5, -5, 0])
    if k % 512:
        return np.exp2(np.random.permutation(np.resize(levels, k // 32))).repeat(32)
    a = np.empty((k // 512, 16))
    for p in range(k // 512):
        a[p, :8] = np.random.permutation(np.resize(levels, 8))
        for g in range(8):
            far = levels[np.abs(levels - a[p, g]) >= 10]
            a[p, g + 8] = far[np.random.randint(len(far))]
    return np.exp2(a.ravel()).repeat(32)


def f64(x):
    return np.asarray(x).astype(np.float64)


def striped(idx):
    return np.tile(idx.reshape(-1, 16).T, (8, 1)).astype(np.uint16)


def unstriped(offs):
    return offs[:16].T.reshape(-1).astype(np.int64)


def striped8(idx):
    return np.concatenate([x.reshape(-1, 16).T for x in idx]).astype(np.uint16)


def runs(offs, k):
    lists = np.stack([offs[16 * r : 16 * r + 16].T.reshape(-1) for r in range(8)]).astype(np.int64)
    return lists[np.arange(k) % 512 // 64]


def pack_weight(w):
    k, n = w.shape
    w = f64(np.asarray(w, np.float32).astype(ml_dtypes.bfloat16)).reshape(k // 32, 32, n)
    amax = np.abs(w).max(1)
    byte = np.clip(np.where(amax > 0, np.frexp(amax)[1] - 1 + 127 - 7, 1), 1, 254)
    scaled = (w * np.exp2(127.0 - byte)[:, None, :]).reshape(k, n).astype(np.float32)
    words = np.ascontiguousarray(scaled.reshape(k // 512, 128, 4, n).transpose(0, 1, 3, 2)).astype(ml_dtypes.float8_e4m3fn).view(np.uint8)
    return words, np.ascontiguousarray(byte.astype(np.uint8).reshape(k // 512, 16, n))


def unpack_weight(words, scales):
    g, p, n, _ = words.shape
    vals = np.ascontiguousarray(words).view(ml_dtypes.float8_e4m3fn).astype(np.float64) * np.repeat(np.exp2(scales.astype(np.float64) - 127.0), 8, axis=1)[..., None]
    return vals.transpose(0, 1, 3, 2).reshape(g * 512, n)


K, T, S, N, H = 512, 2048, 512, 512, 512


def setup_inputs():
    n = np.random.standard_normal
    s = mx_kscale(K)[:, None]
    u = mx_kscale(H)
    packed_xT = pack_weight(n((K, T)) * s)
    return {
        "x_words": packed_xT[0],
        "x_scales": packed_xT[1],
        "w1": (n((K, H)) / np.sqrt(K) / s).astype(np.float32),
        "w2": (n((K, H)) / np.sqrt(K) / s * u).astype(np.float32),
        "w3": (n((H, N)) / np.sqrt(H) / u[:, None]).astype(np.float32),
        "offs": striped(np.random.permutation(T)[:S]),
        "p1": striped8(np.stack([np.random.permutation(S) for _ in range(8)])),
        "p2": striped8(np.stack([np.random.permutation(S) for _ in range(8)])),
    }


def reference(x_words, x_scales, w1, w2, w3, offs, p1, p2):
    xq = unpack_weight(x_words, x_scales)[:, unstriped(offs)]
    val = mxq(f64(w2), 0, "e4m3").T @ xq
    c = mxq(f64(w1), 0, "e4m3").T @ xq
    e1 = np.exp(-0.5 * ((c - (c[np.arange(H)[:, None], runs(p1, H)])) ** 2))
    e2 = np.exp(-0.5 * ((c - (c[np.arange(H)[:, None], runs(p2, H)])) ** 2))
    z = (val + e1 * (val[np.arange(H)[:, None], runs(p1, H)]) + e2 * (val[np.arange(H)[:, None], runs(p2, H)])) / (e1 + e2 + 1)
    return mxq(f64(w3), 0, "e4m3").T @ mxq(z, 0, "e4m3")

@@ -1,0 +1,202 @@
+from contextlib import ExitStack
+
+import concourse.mybir as mybir
+from concourse.masks import make_identity
+
+K, T, S, H, N = 512, 2048, 512, 512, 512
+FLOPS = 2 * K * H * S * 2 + 2 * H * N * S
+
+F32 = mybir.dt.float32
+BF16 = mybir.dt.bfloat16
+I32 = mybir.dt.int32
+U32 = mybir.dt.uint32
+U16 = mybir.dt.uint16
+U8 = mybir.dt.uint8
+FP8X4 = mybir.dt.float8_e4m3fn_x4
+ALU = mybir.AluOpType
+ACT = mybir.ActivationFunctionType
+
+P = 128
+PACK = 4
+HALF = S // 2
+SLICES = ((0, 128), (128, 256), (256, 384), (384, 512))
+W1_SPLIT = 88
+W2_SPLIT = 64
+W3_SPLIT = 64
+
+
+def tile_picked_nlmean_none_p_kernel(tc, x_words, x_scales, w1, w2, w3, offs, p1, p2, out):
+    nc = tc.nc
+    with ExitStack() as ctx:
+        lists = ctx.enter_context(tc.tile_pool(name="lists", bufs=1))
+        keep = ctx.enter_context(tc.tile_pool(name="keep", bufs=1))
+        psum = ctx.enter_context(tc.psum_pool(name="psum", bufs=1))
+
+        offs_sb = lists.tile([P, S // 16], U16, name="offs_sb")
+        p_sb = [lists.tile([P, S // 16], U16, name=f"p_sb{n}") for n in range(2)]
+
+        xs_all = keep.tile([P, T], U8, name="xs_all", align_bytes=64)
+        nc.vector.memset(xs_all[:].bitcast(I32), 0)
+        xw_all = keep.tile([P, T], U32, name="xw_all", align_bytes=64)
+        raw = [keep.tile([P, PACK, H], F32, name=f"raw{n}") for n in range(3)]
+
+        nc.sync.dma_start(raw[0][:], w1.rearrange("(p j) c -> p j c", j=PACK))
+        nc.sync.dma_start(offs_sb[:], offs)
+        for q in range(4):
+            nc.sync.dma_start(xs_all[32 * q : 32 * q + 4, :].bitcast(I32), x_scales[0, 4 * q : 4 * q + 4, :].bitcast(I32))
+        nc.sync.dma_start(xw_all[:].bitcast(I32), x_words[0].rearrange("p n t -> p (n t)").bitcast(I32))
+        nc.sync.dma_start(p_sb[0][:], p1)
+        nc.sync.dma_start(p_sb[1][:], p2)
+        nc.sync.dma_start(raw[1][:], w2.rearrange("(p j) c -> p j c", j=PACK))
+        nc.sync.dma_start(raw[2][:], w3.rearrange("(p j) c -> p j c", j=PACK))
+
+        ident = keep.tile([P, P], F32, name="ident")
+        make_identity(nc, ident[:])
+        c_win = [keep.tile([P, 2 * S], F32, name=f"c_win{t}") for t in range(PACK)]
+        for t in range(PACK):
+            nc.gpsimd.memset(c_win[t][:, S:], 0.0)
+        val = [keep.tile([P, 2 * S], F32, name=f"val{t}") for t in range(PACK)]
+        for t in range(PACK):
+            nc.gpsimd.memset(val[t][:, S:], 0.0)
+
+        wbf = [keep.tile([P, H * PACK], BF16, name=f"wbf{n}", align_bytes=64) for n in range(2)]
+        wc = [keep.tile([P, H], U32, name=f"wc{n}", align_bytes=64) for n in range(3)]
+        ws = [keep.tile([P, H], U8, name=f"ws{n}", align_bytes=64) for n in range(3)]
+
+        def cast_dealt(n, copy, m0, m1):
+            copy(wbf[n][:].rearrange("p (t m j) -> p m j t", t=PACK, j=PACK)[:, m0:m1], raw[n][:].rearrange("p j (m t) -> p m j t", t=PACK)[:, m0:m1])
+
+        def cast_plain(n, copy, c0, c1):
+            copy(wbf[n][:].rearrange("p (c i j) -> p c j i", i=4, j=PACK)[:, c0:c1], raw[n][:].rearrange("p j (c i) -> p c j i", i=4)[:, c0:c1])
+
+        def quant_w(n):
+            nc.vector.quantize_mx(out=wc[n][:].bitcast(FP8X4), scales=ws[n][:], in_=wbf[n][:])
+
+        cast_dealt(0, nc.vector.tensor_copy, 0, W1_SPLIT)
+        cast_dealt(0, nc.scalar.copy, W1_SPLIT, P)
+
+        xs = keep.tile([P, S], U8, name="xs", align_bytes=64)
+        xw = keep.tile([P, S], U32, name="xw", align_bytes=64)
+        nc.vector.tensor_copy(xs[:], xs_all[:].indirect(offs_sb[:]))
+        quant_w(0)
+        for h in range(2):
+            nc.vector.tensor_copy(xw[:, h * HALF : (h + 1) * HALF], xw_all[:].indirect(offs_sb[:, h * HALF // 16 : (h + 1) * HALF // 16]))
+
+        def first_product(n, t, dst, j0, j1):
+            acc = psum.tile([P, S], F32, name="acc", tag="acc", bufs=2)
+            cols = slice(t * P, (t + 1) * P)
+            nc.tensor.matmul_mx(out=acc[:, : j1 - j0], lhsT=wc[n][:, cols].bitcast(FP8X4), lhsT_scale=ws[n][:, cols],
+                                rhs=xw[:, j0:j1].bitcast(FP8X4), rhs_scale=xs[:, j0:j1], start=True, stop=True)
+            nc.scalar.copy(dst[:, j0:j1], acc[:, : j1 - j0])
+
+        e = [[keep.tile([P, S], F32, name=f"e{t}_{n}") for n in range(2)] for t in range(PACK)]
+        den2 = keep.tile([P, PACK, S], F32, name="den2", tag="den2", align_bytes=64)
+
+        c_own = [keep.tile([P, S], F32, name=f"c_own{t}", tag=f"c_own{t}", align_bytes=64) for t in range(PACK)]
+
+        def guide_of(t):
+            for j0, j1 in ((0, HALF), (HALF, S)) if t == 0 else ((0, S),):
+                first_product(0, t, c_win[t], j0, j1)
+                if t < 2:
+                    nc.vector.tensor_copy(c_own[t][:, j0:j1], c_win[t][:, j0:j1])
+                else:
+                    nc.sync.dma_start(c_own[t][:], c_win[t][:, :S])
+
+        def weights_of(t):
+            for n in range(2):
+                d = keep.tile([P, S], F32, name=f"d{t}_{n}")
+                nc.vector.tensor_tensor(d[:], c_win[t][:].indirect(p_sb[n][:]), c_own[t][:], ALU.subtract)
+                sq = keep.tile([P, S], F32, name="sq", tag="sq", bufs=2)
+                nc.scalar.activation(sq[:], d[:], ACT.Square)
+                nc.scalar.activation(e[t][n][:], sq[:], ACT.Exp, scale=-0.5)
+
+        def den_of(t):
+            den = psum.tile([P, S], F32, name="den", tag="den", bufs=2)
+            for n in range(2):
+                for b in range(S // P):
+                    cols = slice(b * P, (b + 1) * P)
+                    nc.tensor.matmul(den[:, cols], e[t][n][:, cols], ident[:], start=(n == 0 and b == 0), stop=(n == 1 and b == S // P - 1), is_transpose=True)
+            nc.scalar.activation(den2[:, t, :], den[:], ACT.Square, bias=1.0)
+
+        def values_of(t):
+            first_product(1, t, val[t], 0, S)
+
+        def add_terms(t, part, first, last):
+            for b in range(S // P):
+                nc.tensor.matmul(num[b][:, t * P : (t + 1) * P], part[:, b * P : (b + 1) * P], ident[:], start=first, stop=last, is_transpose=True)
+
+        def own_terms(t):
+            add_terms(t, val[t], t == 0, False)
+
+        num = [psum.tile([P, S], F32, name=f"num{b}", tag=f"num{b}") for b in range(S // P)]
+
+        def terms_of(t):
+            m = [keep.tile([P, S], F32, name=f"m{t}_{n}") for n in range(2)]
+            for n in range(2):
+                nc.vector.tensor_tensor(m[n][:], val[t][:].indirect(p_sb[n][:]), e[t][n][:], ALU.mult)
+                add_terms(t, m[n], False, t == PACK - 1 and n == 1)
+
+        guide_of(0)
+        cast_dealt(1, nc.vector.tensor_copy, 0, W2_SPLIT)
+        cast_dealt(1, nc.scalar.copy, W2_SPLIT, 96)
+        guide_of(1)
+        weights_of(0)
+        cast_dealt(1, nc.scalar.copy, 96, P)
+        guide_of(2)
+        guide_of(3)
+        quant_w(1)
+        weights_of(1)
+        den_of(0)
+        values_of(0)
+        own_terms(0)
+        weights_of(2)
+        den_of(1)
+        values_of(1)
+        own_terms(1)
+        weights_of(3)
+        den_of(2)
+        terms_of(0)
+        values_of(2)
+        own_terms(2)
+        den_of(3)
+        terms_of(1)
+        values_of(3)
+        own_terms(3)
+        terms_of(2)
+        terms_of(3)
+        r = [keep.tile([P, H], F32, name=f"r{b}") for b in range(S // P)]
+        for b in range(S // P):
+            nc.scalar.activation(r[b][:].rearrange("j (u p e) -> j u p e", u=2, e=2),
+                                 den2[:, :, b * P : (b + 1) * P].rearrange("j (u e) p -> j u p e", e=2), ACT.Abs_reciprocal_sqrt)
+        wbf.append(keep.tile([P, H * PACK], BF16, name="wbf2", tag="c_own3", align_bytes=64))
+        cast_plain(2, nc.vector.tensor_copy, 0, W3_SPLIT)
+        cast_plain(2, nc.scalar.copy, W3_SPLIT, P)
+        quant_w(2)
+        for s0, s1 in SLICES:
+            width = s1 - s0
+            blocks = width // P
+            back = psum.tile([P, blocks, 2, P], F32, name="back", tag="den", bufs=2)
+            for b in range(blocks):
+                j0 = s0 + b * P
+                zt = keep.tile([P, H], BF16, name=f"zt{j0}", align_bytes=64)
+                nc.vector.tensor_tensor(zt[:].rearrange("j (u p e) -> j u p e", u=2, e=2),
+                                        num[j0 // P][:].rearrange("j (u e p) -> j u p e", u=2, e=2),
+                                        r[j0 // P][:].rearrange("j (u p e) -> j u p e", u=2, e=2), ALU.mult)
+                words = zt[:].bitcast(F32)
+                for u in range(2):
+                    nc.tensor.transpose(back[:, b, u, :], words[:, u * P : (u + 1) * P], ident[:])
+            zb = keep.tile([P, width * PACK], BF16, name=f"zb{s0}", align_bytes=64)
+            nc.scalar.copy(zb[:].bitcast(F32).rearrange("p (b j u) -> p b j u", b=blocks, u=2), back[:].rearrange("p b u j -> p b j u"))
+            zc = keep.tile([P, width], U32, name=f"zc{s0}", align_bytes=64)
+            zs = keep.tile([P, width], U8, name=f"zs{s0}", align_bytes=64)
+            nc.vector.quantize_mx(out=zc[:].bitcast(FP8X4), scales=zs[:], in_=zb[:])
+            per_bank = S // width
+            for g in range(PACK // per_bank):
+                acc = psum.tile([P, S], F32, name="fin", tag=f"num{s0 // P}")
+                for a in range(per_bank):
+                    cols = slice((g * per_bank + a) * P, (g * per_bank + a + 1) * P)
+                    nc.tensor.matmul_mx(out=acc[:, a * width : (a + 1) * width], lhsT=wc[2][:, cols].bitcast(FP8X4), lhsT_scale=ws[2][:, cols],
+                                        rhs=zc[:].bitcast(FP8X4), rhs_scale=zs[:], start=True, stop=True)
+                res = keep.tile([P, per_bank, width], F32, name=f"res{s0}_{g}")
+                (nc.scalar.copy if (g + s0 // P) % 2 == 0 else nc.vector.tensor_copy)(res[:].rearrange("p a j -> p (a j)"), acc[:])
+                nc.sync.dma_start(out.rearrange("(a p) j -> p a j", p=P)[:, g * per_bank : (g + 1) * per_bank, s0:s1], res[:])

@@ -18,10 +18,11 @@ ACT = mybir.ActivationFunctionType
 
 P = 128
 PACK = 4
+HEADS = 8
 HALF = S // 2
-SLICES = ((0, 128), (128, 256), (256, 384), (384, 512))
-W1_SPLIT = 88
-W2_SPLIT = 64
+BLOCKS = S // P
+W1_SPLIT = 2
+W2_SPLIT = 3
 W3_SPLIT = 64
 
 
@@ -54,17 +55,18 @@ def tile_picked_nlmean_none_p_kernel(tc, x_words, x_scales, w1, w2, w3, offs, p1
         make_identity(nc, ident[:])
         c_win = [keep.tile([P, 2 * S], F32, name=f"c_win{t}") for t in range(PACK)]
         for t in range(PACK):
-            nc.gpsimd.memset(c_win[t][:, S:], 0.0)
-        val = [keep.tile([P, 2 * S], F32, name=f"val{t}") for t in range(PACK)]
-        for t in range(PACK):
-            nc.gpsimd.memset(val[t][:, S:], 0.0)
+            nc.vector.memset(c_win[t][:, S:], 0.0)
+        val = [keep.tile([P, 2 * S if t < PACK - 1 else S], F32, name=f"val{t}") for t in range(PACK)]
+        for t in range(PACK - 1):
+            nc.vector.memset(val[t][:, S:], 0.0)
 
         wbf = [keep.tile([P, H * PACK], BF16, name=f"wbf{n}", align_bytes=64) for n in range(2)]
         wc = [keep.tile([P, H], U32, name=f"wc{n}", align_bytes=64) for n in range(3)]
         ws = [keep.tile([P, H], U8, name=f"ws{n}", align_bytes=64) for n in range(3)]
 
-        def cast_dealt(n, copy, m0, m1):
-            copy(wbf[n][:].rearrange("p (t m j) -> p m j t", t=PACK, j=PACK)[:, m0:m1], raw[n][:].rearrange("p j (m t) -> p m j t", t=PACK)[:, m0:m1])
+        def cast_dealt(n, copy, t):
+            copy(wbf[n][:].rearrange("p (t g c i j) -> p t g c j i", t=PACK, g=HEADS, i=4, j=PACK)[:, t],
+                 raw[n][:].rearrange("p j (g t c i) -> p t g c j i", g=HEADS, t=PACK, i=4)[:, t])
 
         def cast_plain(n, copy, c0, c1):
             copy(wbf[n][:].rearrange("p (c i j) -> p c j i", i=4, j=PACK)[:, c0:c1], raw[n][:].rearrange("p j (c i) -> p c j i", i=4)[:, c0:c1])
@@ -72,8 +74,8 @@ def tile_picked_nlmean_none_p_kernel(tc, x_words, x_scales, w1, w2, w3, offs, p1
         def quant_w(n):
             nc.vector.quantize_mx(out=wc[n][:].bitcast(FP8X4), scales=ws[n][:], in_=wbf[n][:])
 
-        cast_dealt(0, nc.vector.tensor_copy, 0, W1_SPLIT)
-        cast_dealt(0, nc.scalar.copy, W1_SPLIT, P)
+        for t in range(PACK):
+            cast_dealt(0, nc.vector.tensor_copy if t < W1_SPLIT else nc.scalar.copy, t)
 
         xs = keep.tile([P, S], U8, name="xs", align_bytes=64)
         xw = keep.tile([P, S], U32, name="xw", align_bytes=64)
@@ -121,29 +123,69 @@ def tile_picked_nlmean_none_p_kernel(tc, x_words, x_scales, w1, w2, w3, offs, p1
         def values_of(t):
             first_product(1, t, val[t], 0, S)
 
-        def add_terms(t, part, first, last):
-            for b in range(S // P):
-                nc.tensor.matmul(num[b][:, t * P : (t + 1) * P], part[:, b * P : (b + 1) * P], ident[:], start=first, stop=last, is_transpose=True)
+        num = [psum.tile([P, S], F32, name=f"num{b}", tag=f"num{b}") for b in range(BLOCKS)]
+
+        def add_term(t, b, part, first=False, last=False):
+            nc.tensor.matmul(num[b][:, t * P : (t + 1) * P], part, ident[:], start=first, stop=last, is_transpose=True)
 
         def own_terms(t):
-            add_terms(t, val[t], t == 0, False)
+            for b in range(BLOCKS):
+                add_term(t, b, val[t][:, b * P : (b + 1) * P], first=(t == 0))
 
-        num = [psum.tile([P, S], F32, name=f"num{b}", tag=f"num{b}") for b in range(S // P)]
-
-        def terms_of(t):
-            m = [keep.tile([P, S], F32, name=f"m{t}_{n}") for n in range(2)]
+        def terms_of(t, b0=0, b1=BLOCKS, room=None):
+            j0, j1 = b0 * P, b1 * P
             for n in range(2):
-                nc.vector.tensor_tensor(m[n][:], val[t][:].indirect(p_sb[n][:]), e[t][n][:], ALU.mult)
-                add_terms(t, m[n], False, t == PACK - 1 and n == 1)
+                if room is None:
+                    m = keep.tile([P, j1 - j0], F32, name=f"m{t}_{b0}_{n}")[:]
+                else:
+                    m = room[:, n * P : (n + 1) * P]
+                nc.vector.tensor_tensor(m, val[t][:].indirect(p_sb[n][:, j0 // 16 : j1 // 16]), e[t][n][:, j0:j1], ALU.mult)
+                for b in range(b0, b1):
+                    add_term(t, b, m[:, (b - b0) * P : (b - b0 + 1) * P], last=(t == PACK - 1 and n == 1))
+
+        r = [keep.tile([P, H], F32, name=f"r{b}") for b in range(BLOCKS)]
+
+        def inverse_of(b):
+            nc.scalar.activation(r[b][:].rearrange("j (g t q) -> j g t q", g=HEADS, t=PACK),
+                                 den2[:, :, b * P : (b + 1) * P].rearrange("j t (g q) -> j g t q", g=HEADS), ACT.Abs_reciprocal_sqrt)
+
+        def finish(b):
+            zt = keep.tile([P, H], BF16, name=f"zt{b}", align_bytes=64)
+            nc.vector.tensor_tensor(zt[:].rearrange("j (g t q) -> j g t q", g=HEADS, t=PACK),
+                                    num[b][:].rearrange("j (t g q) -> j g t q", g=HEADS, t=PACK),
+                                    r[b][:].rearrange("j (g t q) -> j g t q", g=HEADS, t=PACK), ALU.mult)
+            words = zt[:].bitcast(F32)
+            back = psum.tile([P, 2, P], F32, name="back", tag="den", bufs=2)
+            for u in range(2):
+                nc.tensor.transpose(back[:, u, :], words[:, u::2], ident[:])
+            zb = keep.tile([P, P * PACK], BF16, name=f"zb{b}", align_bytes=64)
+            nc.scalar.copy(zb[:].bitcast(F32).rearrange("p (j u) -> p j u", u=2), back[:].rearrange("p u j -> p j u"))
+            zc = keep.tile([P, P], U32, name=f"zc{b}", align_bytes=64)
+            zs = keep.tile([P, P], U8, name=f"zs{b}", align_bytes=64)
+            nc.vector.quantize_mx(out=zc[:].bitcast(FP8X4), scales=zs[:], in_=zb[:])
+            parts = ((0, 2, nc.scalar.copy, nc.scalar), (2, 4, nc.vector.tensor_copy, nc.sync)) if b == BLOCKS - 1 else ((0, 4, nc.scalar.copy, nc.sync),)
+            for a0, a1, copy, queue in parts:
+                if a0 == 0:
+                    fin = psum.tile([P, S], F32, name="fin", tag=f"num{b}")
+                else:
+                    fin = psum.tile([P, S], F32, name="fin", tag="acc", bufs=2)
+                for a in range(a0, a1):
+                    cols = slice(a * P, (a + 1) * P)
+                    nc.tensor.matmul_mx(out=fin[:, (a - a0) * P : (a - a0 + 1) * P], lhsT=wc[2][:, cols].bitcast(FP8X4), lhsT_scale=ws[2][:, cols],
+                                        rhs=zc[:].bitcast(FP8X4), rhs_scale=zs[:], start=True, stop=True)
+                res = keep.tile([P, a1 - a0, P], F32, name=f"res{b}_{a0}")
+                copy(res[:].rearrange("p a j -> p (a j)"), fin[:, : (a1 - a0) * P])
+                queue.dma_start(out.rearrange("(a p) j -> p a j", p=P)[:, a0:a1, b * P : (b + 1) * P], res[:])
 
         guide_of(0)
-        cast_dealt(1, nc.vector.tensor_copy, 0, W2_SPLIT)
-        cast_dealt(1, nc.scalar.copy, W2_SPLIT, 96)
         guide_of(1)
-        weights_of(0)
-        cast_dealt(1, nc.scalar.copy, 96, P)
+        for t in range(W2_SPLIT):
+            cast_dealt(1, nc.vector.tensor_copy, t)
         guide_of(2)
         guide_of(3)
+        for t in range(W2_SPLIT, PACK):
+            cast_dealt(1, nc.scalar.copy, t)
+        weights_of(0)
         quant_w(1)
         weights_of(1)
         den_of(0)
@@ -158,45 +200,20 @@ def tile_picked_nlmean_none_p_kernel(tc, x_words, x_scales, w1, w2, w3, offs, p1
         terms_of(0)
         values_of(2)
         own_terms(2)
+        wbf.append(keep.tile([P, H * PACK], BF16, name="wbf2", tag="c_own3", align_bytes=64))
+        cast_plain(2, nc.scalar.copy, W3_SPLIT, P)
         den_of(3)
         terms_of(1)
         values_of(3)
         own_terms(3)
-        terms_of(2)
-        terms_of(3)
-        r = [keep.tile([P, H], F32, name=f"r{b}") for b in range(S // P)]
-        for b in range(S // P):
-            nc.scalar.activation(r[b][:].rearrange("j (u p e) -> j u p e", u=2, e=2),
-                                 den2[:, :, b * P : (b + 1) * P].rearrange("j (u e) p -> j u p e", e=2), ACT.Abs_reciprocal_sqrt)
-        wbf.append(keep.tile([P, H * PACK], BF16, name="wbf2", tag="c_own3", align_bytes=64))
         cast_plain(2, nc.vector.tensor_copy, 0, W3_SPLIT)
-        cast_plain(2, nc.scalar.copy, W3_SPLIT, P)
         quant_w(2)
-        for s0, s1 in SLICES:
-            width = s1 - s0
-            blocks = width // P
-            back = psum.tile([P, blocks, 2, P], F32, name="back", tag="den", bufs=2)
-            for b in range(blocks):
-                j0 = s0 + b * P
-                zt = keep.tile([P, H], BF16, name=f"zt{j0}", align_bytes=64)
-                nc.vector.tensor_tensor(zt[:].rearrange("j (u p e) -> j u p e", u=2, e=2),
-                                        num[j0 // P][:].rearrange("j (u e p) -> j u p e", u=2, e=2),
-                                        r[j0 // P][:].rearrange("j (u p e) -> j u p e", u=2, e=2), ALU.mult)
-                words = zt[:].bitcast(F32)
-                for u in range(2):
-                    nc.tensor.transpose(back[:, b, u, :], words[:, u * P : (u + 1) * P], ident[:])
-            zb = keep.tile([P, width * PACK], BF16, name=f"zb{s0}", align_bytes=64)
-            nc.scalar.copy(zb[:].bitcast(F32).rearrange("p (b j u) -> p b j u", b=blocks, u=2), back[:].rearrange("p b u j -> p b j u"))
-            zc = keep.tile([P, width], U32, name=f"zc{s0}", align_bytes=64)
-            zs = keep.tile([P, width], U8, name=f"zs{s0}", align_bytes=64)
-            nc.vector.quantize_mx(out=zc[:].bitcast(FP8X4), scales=zs[:], in_=zb[:])
-            per_bank = S // width
-            for g in range(PACK // per_bank):
-                acc = psum.tile([P, S], F32, name="fin", tag=f"num{s0 // P}")
-                for a in range(per_bank):
-                    cols = slice((g * per_bank + a) * P, (g * per_bank + a + 1) * P)
-                    nc.tensor.matmul_mx(out=acc[:, a * width : (a + 1) * width], lhsT=wc[2][:, cols].bitcast(FP8X4), lhsT_scale=ws[2][:, cols],
-                                        rhs=zc[:].bitcast(FP8X4), rhs_scale=zs[:], start=True, stop=True)
-                res = keep.tile([P, per_bank, width], F32, name=f"res{s0}_{g}")
-                (nc.scalar.copy if (g + s0 // P) % 2 == 0 else nc.vector.tensor_copy)(res[:].rearrange("p a j -> p (a j)"), acc[:])
-                nc.sync.dma_start(out.rearrange("(a p) j -> p a j", p=P)[:, g * per_bank : (g + 1) * per_bank, s0:s1], res[:])
+        terms_of(2)
+        for b in range(BLOCKS):
+            inverse_of(b)
+        terms_of(PACK - 1, 0, 1)
+        terms_of(PACK - 1, 1, 2)
+        for b in range(BLOCKS):
+            finish(b)
+            if b + 2 < BLOCKS:
+                terms_of(PACK - 1, b + 2, b + 3, r[b])

@@ -22,7 +22,6 @@ HEADS = 8
 HALF = S // 2
 BLOCKS = S // P
 W1_SPLIT = 2
-W2_SPLIT = 3
 W3_SPLIT = 64
 
 
@@ -39,7 +38,8 @@ def tile_picked_nlmean_none_p_kernel(tc, x_words, x_scales, w1, w2, w3, offs, p1
         xs_all = keep.tile([P, T], U8, name="xs_all", align_bytes=64)
         nc.vector.memset(xs_all[:].bitcast(I32), 0)
         xw_all = keep.tile([P, T], U32, name="xw_all", align_bytes=64)
-        raw = [keep.tile([P, PACK, H], F32, name=f"raw{n}") for n in range(3)]
+        raw = [keep.tile([P, PACK, H], F32, name=f"raw{n}") for n in (0, 2)]
+        raw_w2 = [keep.tile([P, PACK, H // 2], F32, name=f"raw_w2{h}") for h in range(2)]
 
         nc.sync.dma_start(raw[0][:], w1.rearrange("(p j) c -> p j c", j=PACK))
         nc.sync.dma_start(offs_sb[:], offs)
@@ -48,8 +48,9 @@ def tile_picked_nlmean_none_p_kernel(tc, x_words, x_scales, w1, w2, w3, offs, p1
         nc.sync.dma_start(xw_all[:].bitcast(I32), x_words[0].rearrange("p n t -> p (n t)").bitcast(I32))
         nc.sync.dma_start(p_sb[0][:], p1)
         nc.sync.dma_start(p_sb[1][:], p2)
-        nc.sync.dma_start(raw[1][:], w2.rearrange("(p j) c -> p j c", j=PACK))
-        nc.sync.dma_start(raw[2][:], w3.rearrange("(p j) c -> p j c", j=PACK))
+        for h in range(2):
+            nc.sync.dma_start(raw_w2[h][:], w2.rearrange("(p j) c -> p j c", j=PACK)[:, :, h * H // 2 : (h + 1) * H // 2])
+        nc.sync.dma_start(raw[1][:], w3.rearrange("(p j) c -> p j c", j=PACK))
 
         ident = keep.tile([P, P], F32, name="ident")
         make_identity(nc, ident[:])
@@ -57,25 +58,23 @@ def tile_picked_nlmean_none_p_kernel(tc, x_words, x_scales, w1, w2, w3, offs, p1
         for t in range(PACK):
             nc.vector.memset(c_win[t][:, S:], 0.0)
         val = [keep.tile([P, 2 * S if t < PACK - 1 else S], F32, name=f"val{t}") for t in range(PACK)]
-        for t in range(PACK - 1):
-            nc.vector.memset(val[t][:, S:], 0.0)
 
         wbf = [keep.tile([P, H * PACK], BF16, name=f"wbf{n}", align_bytes=64) for n in range(2)]
         wc = [keep.tile([P, H], U32, name=f"wc{n}", align_bytes=64) for n in range(3)]
         ws = [keep.tile([P, H], U8, name=f"ws{n}", align_bytes=64) for n in range(3)]
 
-        def cast_dealt(n, copy, t):
-            copy(wbf[n][:].rearrange("p (t g c i j) -> p t g c j i", t=PACK, g=HEADS, i=4, j=PACK)[:, t],
-                 raw[n][:].rearrange("p j (g t c i) -> p t g c j i", g=HEADS, t=PACK, i=4)[:, t])
+        def cast_dealt(n, copy, t, src, g0, g1):
+            copy(wbf[n][:].rearrange("p (t g c i j) -> p t g c j i", t=PACK, g=HEADS, i=4, j=PACK)[:, t, g0:g1],
+                 src[:].rearrange("p j (g t c i) -> p t g c j i", g=g1 - g0, t=PACK, i=4)[:, t])
 
         def cast_plain(n, copy, c0, c1):
-            copy(wbf[n][:].rearrange("p (c i j) -> p c j i", i=4, j=PACK)[:, c0:c1], raw[n][:].rearrange("p j (c i) -> p c j i", i=4)[:, c0:c1])
+            copy(wbf[n][:].rearrange("p (c i j) -> p c j i", i=4, j=PACK)[:, c0:c1], raw[1][:].rearrange("p j (c i) -> p c j i", i=4)[:, c0:c1])
 
         def quant_w(n):
             nc.vector.quantize_mx(out=wc[n][:].bitcast(FP8X4), scales=ws[n][:], in_=wbf[n][:])
 
         for t in range(PACK):
-            cast_dealt(0, nc.vector.tensor_copy if t < W1_SPLIT else nc.scalar.copy, t)
+            cast_dealt(0, nc.vector.tensor_copy if t < W1_SPLIT else nc.scalar.copy, t, raw[0], 0, HEADS)
 
         xs = keep.tile([P, S], U8, name="xs", align_bytes=64)
         xw = keep.tile([P, S], U32, name="xw", align_bytes=64)
@@ -94,7 +93,7 @@ def tile_picked_nlmean_none_p_kernel(tc, x_words, x_scales, w1, w2, w3, offs, p1
         e = [[keep.tile([P, S], F32, name=f"e{t}_{n}") for n in range(2)] for t in range(PACK)]
         den2 = keep.tile([P, PACK, S], F32, name="den2", tag="den2", align_bytes=64)
 
-        c_own = [keep.tile([P, S], F32, name=f"c_own{t}", tag=f"c_own{t}", align_bytes=64) for t in range(PACK)]
+        c_own = [val[t][:, S:] for t in range(PACK - 1)] + [keep.tile([P, S], F32, name="c_own3", tag="c_own3", align_bytes=64)[:]]
 
         def guide_of(t):
             for j0, j1 in ((0, HALF), (HALF, S)) if t == 0 else ((0, S),):
@@ -102,12 +101,12 @@ def tile_picked_nlmean_none_p_kernel(tc, x_words, x_scales, w1, w2, w3, offs, p1
                 if t < 2:
                     nc.vector.tensor_copy(c_own[t][:, j0:j1], c_win[t][:, j0:j1])
                 else:
-                    nc.sync.dma_start(c_own[t][:], c_win[t][:, :S])
+                    nc.sync.dma_start(c_own[t], c_win[t][:, :S])
 
         def weights_of(t):
             for n in range(2):
-                d = keep.tile([P, S], F32, name=f"d{t}_{n}")
-                nc.vector.tensor_tensor(d[:], c_win[t][:].indirect(p_sb[n][:]), c_own[t][:], ALU.subtract)
+                d = keep.tile([P, S], F32, name=f"d{t}_{n}", tag=f"d{t}_{n}")
+                nc.vector.tensor_tensor(d[:], c_win[t][:].indirect(p_sb[n][:]), c_own[t], ALU.subtract)
                 sq = keep.tile([P, S], F32, name="sq", tag="sq", bufs=2)
                 nc.scalar.activation(sq[:], d[:], ACT.Square)
                 nc.scalar.activation(e[t][n][:], sq[:], ACT.Exp, scale=-0.5)
@@ -132,13 +131,15 @@ def tile_picked_nlmean_none_p_kernel(tc, x_words, x_scales, w1, w2, w3, offs, p1
             for b in range(BLOCKS):
                 add_term(t, b, val[t][:, b * P : (b + 1) * P], first=(t == 0))
 
-        def terms_of(t, b0=0, b1=BLOCKS, room=None):
+        def terms_of(t, b0=0, b1=BLOCKS):
             j0, j1 = b0 * P, b1 * P
             for n in range(2):
-                if room is None:
-                    m = keep.tile([P, j1 - j0], F32, name=f"m{t}_{b0}_{n}")[:]
+                if t < 2:
+                    m = keep.tile([P, S], F32, name=f"m{t}_{n}", tag=f"d{t + 2}_{n}")[:]
+                elif t == 2:
+                    m = keep.tile([P, S], F32, name=f"m{t}_{n}", tag="sq", bufs=2)[:]
                 else:
-                    m = room[:, n * P : (n + 1) * P]
+                    m = keep.tile([P, j1 - j0], F32, name=f"m{t}_{b0}_{n}")[:]
                 nc.vector.tensor_tensor(m, val[t][:].indirect(p_sb[n][:, j0 // 16 : j1 // 16]), e[t][n][:, j0:j1], ALU.mult)
                 for b in range(b0, b1):
                     add_term(t, b, m[:, (b - b0) * P : (b - b0 + 1) * P], last=(t == PACK - 1 and n == 1))
@@ -149,7 +150,10 @@ def tile_picked_nlmean_none_p_kernel(tc, x_words, x_scales, w1, w2, w3, offs, p1
             nc.scalar.activation(r[b][:].rearrange("j (g t q) -> j g t q", g=HEADS, t=PACK),
                                  den2[:, :, b * P : (b + 1) * P].rearrange("j t (g q) -> j g t q", g=HEADS), ACT.Abs_reciprocal_sqrt)
 
-        def finish(b):
+        zc = [keep.tile([P, P], U32, name=f"zc{b}", align_bytes=64) for b in range(BLOCKS)]
+        zs = [keep.tile([P, P], U8, name=f"zs{b}", align_bytes=64) for b in range(BLOCKS)]
+
+        def average(b):
             zt = keep.tile([P, H], BF16, name=f"zt{b}", align_bytes=64)
             nc.vector.tensor_tensor(zt[:].rearrange("j (g t q) -> j g t q", g=HEADS, t=PACK),
                                     num[b][:].rearrange("j (t g q) -> j g t q", g=HEADS, t=PACK),
@@ -160,10 +164,10 @@ def tile_picked_nlmean_none_p_kernel(tc, x_words, x_scales, w1, w2, w3, offs, p1
                 nc.tensor.transpose(back[:, u, :], words[:, u::2], ident[:])
             zb = keep.tile([P, P * PACK], BF16, name=f"zb{b}", align_bytes=64)
             nc.scalar.copy(zb[:].bitcast(F32).rearrange("p (j u) -> p j u", u=2), back[:].rearrange("p u j -> p j u"))
-            zc = keep.tile([P, P], U32, name=f"zc{b}", align_bytes=64)
-            zs = keep.tile([P, P], U8, name=f"zs{b}", align_bytes=64)
-            nc.vector.quantize_mx(out=zc[:].bitcast(FP8X4), scales=zs[:], in_=zb[:])
-            parts = ((0, 2, nc.scalar.copy, nc.scalar), (2, 4, nc.vector.tensor_copy, nc.sync)) if b == BLOCKS - 1 else ((0, 4, nc.scalar.copy, nc.sync),)
+            nc.vector.quantize_mx(out=zc[b][:].bitcast(FP8X4), scales=zs[b][:], in_=zb[:])
+
+        def finish(b):
+            parts = ((0, 2, nc.scalar.copy, nc.sync), (2, 4, nc.vector.tensor_copy, nc.sync))
             for a0, a1, copy, queue in parts:
                 if a0 == 0:
                     fin = psum.tile([P, S], F32, name="fin", tag=f"num{b}")
@@ -172,19 +176,19 @@ def tile_picked_nlmean_none_p_kernel(tc, x_words, x_scales, w1, w2, w3, offs, p1
                 for a in range(a0, a1):
                     cols = slice(a * P, (a + 1) * P)
                     nc.tensor.matmul_mx(out=fin[:, (a - a0) * P : (a - a0 + 1) * P], lhsT=wc[2][:, cols].bitcast(FP8X4), lhsT_scale=ws[2][:, cols],
-                                        rhs=zc[:].bitcast(FP8X4), rhs_scale=zs[:], start=True, stop=True)
+                                        rhs=zc[b][:].bitcast(FP8X4), rhs_scale=zs[b][:], start=True, stop=True)
                 res = keep.tile([P, a1 - a0, P], F32, name=f"res{b}_{a0}")
                 copy(res[:].rearrange("p a j -> p (a j)"), fin[:, : (a1 - a0) * P])
                 queue.dma_start(out.rearrange("(a p) j -> p a j", p=P)[:, a0:a1, b * P : (b + 1) * P], res[:])
 
+        for t in range(PACK):
+            cast_dealt(1, nc.vector.tensor_copy, t, raw_w2[0], 0, HEADS // 2)
         guide_of(0)
         guide_of(1)
-        for t in range(W2_SPLIT):
-            cast_dealt(1, nc.vector.tensor_copy, t)
+        for t in range(PACK):
+            cast_dealt(1, nc.scalar.copy, t, raw_w2[1], HEADS // 2, HEADS)
         guide_of(2)
         guide_of(3)
-        for t in range(W2_SPLIT, PACK):
-            cast_dealt(1, nc.scalar.copy, t)
         weights_of(0)
         quant_w(1)
         weights_of(1)
@@ -196,24 +200,23 @@ def tile_picked_nlmean_none_p_kernel(tc, x_words, x_scales, w1, w2, w3, offs, p1
         values_of(1)
         own_terms(1)
         weights_of(3)
-        den_of(2)
         terms_of(0)
+        den_of(2)
         values_of(2)
         own_terms(2)
-        wbf.append(keep.tile([P, H * PACK], BF16, name="wbf2", tag="c_own3", align_bytes=64))
-        cast_plain(2, nc.scalar.copy, W3_SPLIT, P)
-        den_of(3)
-        terms_of(1)
         values_of(3)
         own_terms(3)
-        cast_plain(2, nc.vector.tensor_copy, 0, W3_SPLIT)
-        quant_w(2)
+        wbf.append(keep.tile([P, H * PACK], BF16, name="wbf2", tag="c_own3", align_bytes=64))
+        cast_plain(2, nc.scalar.copy, 0, 128)
+        den_of(3)
+        terms_of(1)
         terms_of(2)
         for b in range(BLOCKS):
             inverse_of(b)
-        terms_of(PACK - 1, 0, 1)
-        terms_of(PACK - 1, 1, 2)
+        for b0, b1 in ((0, 2), (2, 4)):
+            terms_of(PACK - 1, b0, b1)
+        quant_w(2)
+        for b in range(BLOCKS):
+            average(b)
         for b in range(BLOCKS):
             finish(b)
-            if b + 2 < BLOCKS:
-                terms_of(PACK - 1, b + 2, b + 3, r[b])

@@ -18,11 +18,13 @@ ACT = mybir.ActivationFunctionType
 
 P = 128
 PACK = 4
+TILES = H // P
 HEADS = 8
-HALF = S // 2
 BLOCKS = S // P
-W1_SPLIT = 2
-W3_SPLIT = 64
+HALF = S // 2
+PER_COLUMN = 16
+LINE = 4
+W1, W2, W3 = 0, 1, 2
 
 
 def tile_picked_nlmean_none_p_kernel(tc, x_words, x_scales, w1, w2, w3, offs, p1, p2, out):
@@ -32,191 +34,189 @@ def tile_picked_nlmean_none_p_kernel(tc, x_words, x_scales, w1, w2, w3, offs, p1
         keep = ctx.enter_context(tc.tile_pool(name="keep", bufs=1))
         psum = ctx.enter_context(tc.psum_pool(name="psum", bufs=1))
 
-        offs_sb = lists.tile([P, S // 16], U16, name="offs_sb")
-        p_sb = [lists.tile([P, S // 16], U16, name=f"p_sb{n}") for n in range(2)]
+        offs_sb = lists.tile([P, S // PER_COLUMN], U16, name="offs_sb")
+        p_sb = [lists.tile([P, S // PER_COLUMN], U16, name=f"p_sb{n}") for n in range(2)]
 
-        xs_all = keep.tile([P, T], U8, name="xs_all", align_bytes=64)
-        nc.vector.memset(xs_all[:].bitcast(I32), 0)
-        xw_all = keep.tile([P, T], U32, name="xw_all", align_bytes=64)
-        raw = [keep.tile([P, PACK, H], F32, name=f"raw{n}") for n in (0, 2)]
-        raw_w2 = [keep.tile([P, PACK, H // 2], F32, name=f"raw_w2{h}") for h in range(2)]
+        def entries(list_tile, j0, j1):
+            return list_tile[:, j0 // PER_COLUMN : j1 // PER_COLUMN]
 
-        nc.sync.dma_start(raw[0][:], w1.rearrange("(p j) c -> p j c", j=PACK))
+        x_scale_all = keep.tile([P, T], U8, name="x_scale_all", align_bytes=64)
+        nc.vector.memset(x_scale_all[:].bitcast(I32), 0)
+        x_word_all = keep.tile([P, T], U32, name="x_word_all", align_bytes=64)
+        w1_raw = keep.tile([P, PACK, H], F32, name="w1_raw")
+        w3_raw = keep.tile([P, PACK, N], F32, name="w3_raw")
+        w2_raw = [keep.tile([P, PACK, H // 2], F32, name=f"w2_raw{h}") for h in range(2)]
+
+        nc.sync.dma_start(w1_raw[:], w1.rearrange("(p s) c -> p s c", s=PACK))
         nc.sync.dma_start(offs_sb[:], offs)
-        for q in range(4):
-            nc.sync.dma_start(xs_all[32 * q : 32 * q + 4, :].bitcast(I32), x_scales[0, 4 * q : 4 * q + 4, :].bitcast(I32))
-        nc.sync.dma_start(xw_all[:].bitcast(I32), x_words[0].rearrange("p n t -> p (n t)").bitcast(I32))
+        for quad in range(4):
+            nc.sync.dma_start(x_scale_all[32 * quad : 32 * quad + 4, :].bitcast(I32), x_scales[0, 4 * quad : 4 * quad + 4, :].bitcast(I32))
+        nc.sync.dma_start(x_word_all[:].bitcast(I32), x_words[0].rearrange("p n s -> p (n s)").bitcast(I32))
         nc.sync.dma_start(p_sb[0][:], p1)
         nc.sync.dma_start(p_sb[1][:], p2)
         for h in range(2):
-            nc.sync.dma_start(raw_w2[h][:], w2.rearrange("(p j) c -> p j c", j=PACK)[:, :, h * H // 2 : (h + 1) * H // 2])
-        nc.sync.dma_start(raw[1][:], w3.rearrange("(p j) c -> p j c", j=PACK))
+            nc.sync.dma_start(w2_raw[h][:], w2.rearrange("(p s) c -> p s c", s=PACK)[:, :, h * H // 2 : (h + 1) * H // 2])
+        nc.sync.dma_start(w3_raw[:], w3.rearrange("(p s) c -> p s c", s=PACK))
 
         ident = keep.tile([P, P], F32, name="ident")
         make_identity(nc, ident[:])
-        c_win = [keep.tile([P, 2 * S], F32, name=f"c_win{t}") for t in range(PACK)]
-        for t in range(PACK):
+
+        c_win = [keep.tile([P, 2 * S], F32, name=f"c_win{t}") for t in range(TILES)]
+        for t in range(TILES):
             nc.vector.memset(c_win[t][:, S:], 0.0)
-        val = [keep.tile([P, 2 * S if t < PACK - 1 else S], F32, name=f"val{t}") for t in range(PACK)]
+        val = [keep.tile([P, 2 * S if t < TILES - 1 else S], F32, name=f"val{t}") for t in range(TILES)]
+        c_own_last = keep.tile([P, S], F32, name="c_own_last", tag="c_own_last", align_bytes=64)
+        c_own = [val[t][:, S:] for t in range(TILES - 1)] + [c_own_last[:]]
 
-        wbf = [keep.tile([P, H * PACK], BF16, name=f"wbf{n}", align_bytes=64) for n in range(2)]
-        wc = [keep.tile([P, H], U32, name=f"wc{n}", align_bytes=64) for n in range(3)]
-        ws = [keep.tile([P, H], U8, name=f"ws{n}", align_bytes=64) for n in range(3)]
+        w_bf16 = [keep.tile([P, H * PACK], BF16, name=f"w_bf16_{w}", align_bytes=64) for w in (W1, W2)]
+        w_word = [keep.tile([P, H], U32, name=f"w_word{w}", align_bytes=64) for w in (W1, W2, W3)]
+        w_scale = [keep.tile([P, H], U8, name=f"w_scale{w}", align_bytes=64) for w in (W1, W2, W3)]
 
-        def cast_dealt(n, copy, t, src, g0, g1):
-            copy(wbf[n][:].rearrange("p (t g c i j) -> p t g c j i", t=PACK, g=HEADS, i=4, j=PACK)[:, t, g0:g1],
-                 src[:].rearrange("p j (g t c i) -> p t g c j i", g=g1 - g0, t=PACK, i=4)[:, t])
+        def cast_tile_columns(w, copy, t, src, g0, g1):
+            copy(w_bf16[w][:].rearrange("p (t g c i s) -> p t g c s i", t=TILES, g=HEADS, i=LINE, s=PACK)[:, t, g0:g1],
+                 src[:].rearrange("p s (g t c i) -> p t g c s i", g=g1 - g0, t=TILES, i=LINE)[:, t])
 
-        def cast_plain(n, copy, c0, c1):
-            copy(wbf[n][:].rearrange("p (c i j) -> p c j i", i=4, j=PACK)[:, c0:c1], raw[1][:].rearrange("p j (c i) -> p c j i", i=4)[:, c0:c1])
+        def quantise_weights(w):
+            nc.vector.quantize_mx(out=w_word[w][:].bitcast(FP8X4), scales=w_scale[w][:], in_=w_bf16[w][:])
 
-        def quant_w(n):
-            nc.vector.quantize_mx(out=wc[n][:].bitcast(FP8X4), scales=ws[n][:], in_=wbf[n][:])
+        for t in range(TILES):
+            cast_tile_columns(W1, nc.vector.tensor_copy if t < TILES // 2 else nc.scalar.copy, t, w1_raw, 0, HEADS)
 
-        for t in range(PACK):
-            cast_dealt(0, nc.vector.tensor_copy if t < W1_SPLIT else nc.scalar.copy, t, raw[0], 0, HEADS)
+        x_scale = keep.tile([P, S], U8, name="x_scale", align_bytes=64)
+        x_word = keep.tile([P, S], U32, name="x_word", align_bytes=64)
+        nc.vector.tensor_copy(x_scale[:], x_scale_all[:].indirect(offs_sb[:]))
+        quantise_weights(W1)
+        for j0 in range(0, S, HALF):
+            nc.vector.tensor_copy(x_word[:, j0 : j0 + HALF], x_word_all[:].indirect(entries(offs_sb, j0, j0 + HALF)))
 
-        xs = keep.tile([P, S], U8, name="xs", align_bytes=64)
-        xw = keep.tile([P, S], U32, name="xw", align_bytes=64)
-        nc.vector.tensor_copy(xs[:], xs_all[:].indirect(offs_sb[:]))
-        quant_w(0)
-        for h in range(2):
-            nc.vector.tensor_copy(xw[:, h * HALF : (h + 1) * HALF], xw_all[:].indirect(offs_sb[:, h * HALF // 16 : (h + 1) * HALF // 16]))
-
-        def first_product(n, t, dst, j0, j1):
-            acc = psum.tile([P, S], F32, name="acc", tag="acc", bufs=2)
+        def product_with_x(w, t, dst, j0, j1, bank):
+            acc = psum.tile([P, S], F32, name="acc", tag=bank, bufs=2)
             cols = slice(t * P, (t + 1) * P)
-            nc.tensor.matmul_mx(out=acc[:, : j1 - j0], lhsT=wc[n][:, cols].bitcast(FP8X4), lhsT_scale=ws[n][:, cols],
-                                rhs=xw[:, j0:j1].bitcast(FP8X4), rhs_scale=xs[:, j0:j1], start=True, stop=True)
+            nc.tensor.matmul_mx(out=acc[:, : j1 - j0], lhsT=w_word[w][:, cols].bitcast(FP8X4), lhsT_scale=w_scale[w][:, cols],
+                                rhs=x_word[:, j0:j1].bitcast(FP8X4), rhs_scale=x_scale[:, j0:j1], start=True, stop=True)
             nc.scalar.copy(dst[:, j0:j1], acc[:, : j1 - j0])
 
-        e = [[keep.tile([P, S], F32, name=f"e{t}_{n}") for n in range(2)] for t in range(PACK)]
-        den2 = keep.tile([P, PACK, S], F32, name="den2", tag="den2", align_bytes=64)
-
-        c_own = [val[t][:, S:] for t in range(PACK - 1)] + [keep.tile([P, S], F32, name="c_own3", tag="c_own3", align_bytes=64)[:]]
-
-        def guide_of(t):
-            for j0, j1 in ((0, HALF), (HALF, S)) if t == 0 else ((0, S),):
-                first_product(0, t, c_win[t], j0, j1)
-                if t < 2:
-                    nc.vector.tensor_copy(c_own[t][:, j0:j1], c_win[t][:, j0:j1])
-                else:
+        def make_c(t):
+            if t == 0:
+                for j0 in range(0, S, HALF):
+                    product_with_x(W1, t, c_win[t], j0, j0 + HALF, "acc")
+                    nc.vector.tensor_copy(c_own[t][:, j0 : j0 + HALF], c_win[t][:, j0 : j0 + HALF])
+            else:
+                product_with_x(W1, t, c_win[t], 0, S, "den" if t == 1 else "acc")
+                if t > 1:
                     nc.sync.dma_start(c_own[t], c_win[t][:, :S])
 
-        def weights_of(t):
-            for n in range(2):
-                d = keep.tile([P, S], F32, name=f"d{t}_{n}", tag=f"d{t}_{n}")
-                nc.vector.tensor_tensor(d[:], c_win[t][:].indirect(p_sb[n][:]), c_own[t], ALU.subtract)
-                sq = keep.tile([P, S], F32, name="sq", tag="sq", bufs=2)
-                nc.scalar.activation(sq[:], d[:], ACT.Square)
-                nc.scalar.activation(e[t][n][:], sq[:], ACT.Exp, scale=-0.5)
+        e = [[keep.tile([P, S], F32, name=f"e{t}_{n}") for n in range(2)] for t in range(TILES)]
 
-        def den_of(t):
+        def make_e(t):
+            for n in range(2):
+                diff = keep.tile([P, S], F32, name=f"diff{t}_{n}", tag=f"diff{t}_{n}")
+                nc.vector.tensor_tensor(diff[:], c_win[t][:].indirect(p_sb[n][:]), c_own[t], ALU.subtract)
+                square = keep.tile([P, S], F32, name="square", tag="square", bufs=2)
+                nc.scalar.activation(square[:], diff[:], ACT.Square)
+                nc.scalar.activation(e[t][n][:], square[:], ACT.Exp, scale=-0.5)
+
+        den_sq = keep.tile([P, TILES, S], F32, name="den_sq")
+
+        def make_den(t):
             den = psum.tile([P, S], F32, name="den", tag="den", bufs=2)
             for n in range(2):
-                for b in range(S // P):
+                for b in range(BLOCKS):
                     cols = slice(b * P, (b + 1) * P)
-                    nc.tensor.matmul(den[:, cols], e[t][n][:, cols], ident[:], start=(n == 0 and b == 0), stop=(n == 1 and b == S // P - 1), is_transpose=True)
-            nc.scalar.activation(den2[:, t, :], den[:], ACT.Square, bias=1.0)
-
-        def values_of(t):
-            first_product(1, t, val[t], 0, S)
+                    nc.tensor.matmul(den[:, cols], e[t][n][:, cols], ident[:], start=(n == 0 and b == 0), stop=(n == 1 and b == BLOCKS - 1), is_transpose=True)
+            nc.scalar.activation(den_sq[:, t, :], den[:], ACT.Square, bias=1.0)
 
         num = [psum.tile([P, S], F32, name=f"num{b}", tag=f"num{b}") for b in range(BLOCKS)]
 
-        def add_term(t, b, part, first=False, last=False):
-            nc.tensor.matmul(num[b][:, t * P : (t + 1) * P], part, ident[:], start=first, stop=last, is_transpose=True)
+        def add_to_num(t, b, term, first=False, last=False):
+            nc.tensor.matmul(num[b][:, t * P : (t + 1) * P], term, ident[:], start=first, stop=last, is_transpose=True)
 
-        def own_terms(t):
+        def make_val(t):
+            product_with_x(W2, t, val[t], 0, S, "acc")
             for b in range(BLOCKS):
-                add_term(t, b, val[t][:, b * P : (b + 1) * P], first=(t == 0))
+                add_to_num(t, b, val[t][:, b * P : (b + 1) * P], first=(t == 0))
 
-        def terms_of(t, b0=0, b1=BLOCKS):
+        def make_terms(t, b0, b1):
             j0, j1 = b0 * P, b1 * P
             for n in range(2):
                 if t < 2:
-                    m = keep.tile([P, S], F32, name=f"m{t}_{n}", tag=f"d{t + 2}_{n}")[:]
+                    term = keep.tile([P, S], F32, name=f"term{t}_{n}", tag=f"diff{t + 2}_{n}")
                 elif t == 2:
-                    m = keep.tile([P, S], F32, name=f"m{t}_{n}", tag="sq", bufs=2)[:]
+                    term = keep.tile([P, S], F32, name=f"term{t}_{n}", tag="square", bufs=2)
                 else:
-                    m = keep.tile([P, j1 - j0], F32, name=f"m{t}_{b0}_{n}")[:]
-                nc.vector.tensor_tensor(m, val[t][:].indirect(p_sb[n][:, j0 // 16 : j1 // 16]), e[t][n][:, j0:j1], ALU.mult)
+                    term = keep.tile([P, j1 - j0], F32, name=f"term{t}_{b0}_{n}")
+                nc.vector.tensor_tensor(term[:], val[t][:].indirect(entries(p_sb[n], j0, j1)), e[t][n][:, j0:j1], ALU.mult)
                 for b in range(b0, b1):
-                    add_term(t, b, m[:, (b - b0) * P : (b - b0 + 1) * P], last=(t == PACK - 1 and n == 1))
+                    add_to_num(t, b, term[:, (b - b0) * P : (b - b0 + 1) * P], last=(t == TILES - 1 and n == 1))
 
-        r = [keep.tile([P, H], F32, name=f"r{b}") for b in range(BLOCKS)]
+        inv = [keep.tile([P, H], F32, name=f"inv{b}") for b in range(BLOCKS)]
 
-        def inverse_of(b):
-            nc.scalar.activation(r[b][:].rearrange("j (g t q) -> j g t q", g=HEADS, t=PACK),
-                                 den2[:, :, b * P : (b + 1) * P].rearrange("j t (g q) -> j g t q", g=HEADS), ACT.Abs_reciprocal_sqrt)
+        def make_inv(b):
+            nc.scalar.activation(inv[b][:].rearrange("j (g t q) -> j g t q", g=HEADS, t=TILES),
+                                 den_sq[:, :, b * P : (b + 1) * P].rearrange("j t (g q) -> j g t q", g=HEADS), ACT.Abs_reciprocal_sqrt)
 
-        zc = [keep.tile([P, P], U32, name=f"zc{b}", align_bytes=64) for b in range(BLOCKS)]
-        zs = [keep.tile([P, P], U8, name=f"zs{b}", align_bytes=64) for b in range(BLOCKS)]
+        z_word = [keep.tile([P, P], U32, name=f"z_word{b}", align_bytes=64) for b in range(BLOCKS)]
+        z_scale = [keep.tile([P, P], U8, name=f"z_scale{b}", align_bytes=64) for b in range(BLOCKS)]
 
-        def average(b):
-            zt = keep.tile([P, H], BF16, name=f"zt{b}", align_bytes=64)
-            nc.vector.tensor_tensor(zt[:].rearrange("j (g t q) -> j g t q", g=HEADS, t=PACK),
-                                    num[b][:].rearrange("j (t g q) -> j g t q", g=HEADS, t=PACK),
-                                    r[b][:].rearrange("j (g t q) -> j g t q", g=HEADS, t=PACK), ALU.mult)
-            words = zt[:].bitcast(F32)
+        def make_z(b):
+            z_rows = keep.tile([P, H], BF16, name=f"z_rows{b}", tag="z_bf16_0" if b == BLOCKS - 1 else f"z_rows{b}", align_bytes=64)
+            nc.vector.tensor_tensor(z_rows[:].rearrange("j (g t q) -> j g t q", g=HEADS, t=TILES),
+                                    num[b][:].rearrange("j (t g q) -> j g t q", g=HEADS, t=TILES),
+                                    inv[b][:].rearrange("j (g t q) -> j g t q", g=HEADS, t=TILES), ALU.mult)
+            pairs = z_rows[:].bitcast(F32)
             back = psum.tile([P, 2, P], F32, name="back", tag="den", bufs=2)
             for u in range(2):
-                nc.tensor.transpose(back[:, u, :], words[:, u::2], ident[:])
-            zb = keep.tile([P, P * PACK], BF16, name=f"zb{b}", align_bytes=64)
-            nc.scalar.copy(zb[:].bitcast(F32).rearrange("p (j u) -> p j u", u=2), back[:].rearrange("p u j -> p j u"))
-            nc.vector.quantize_mx(out=zc[b][:].bitcast(FP8X4), scales=zs[b][:], in_=zb[:])
+                nc.tensor.transpose(back[:, u, :], pairs[:, u::2], ident[:])
+            z_bf16 = keep.tile([P, P * PACK], BF16, name=f"z_bf16_{b}", tag=f"z_bf16_{b}", align_bytes=64)
+            nc.scalar.copy(z_bf16[:].bitcast(F32).rearrange("p (j u) -> p j u", u=2), back[:].rearrange("p u j -> p j u"))
+            nc.vector.quantize_mx(out=z_word[b][:].bitcast(FP8X4), scales=z_scale[b][:], in_=z_bf16[:])
 
-        def finish(b):
-            parts = ((0, 2, nc.scalar.copy, nc.sync), (2, 4, nc.vector.tensor_copy, nc.sync))
-            for a0, a1, copy, queue in parts:
-                if a0 == 0:
-                    fin = psum.tile([P, S], F32, name="fin", tag=f"num{b}")
+        def make_out(b):
+            for half in range(2):
+                if half == 0:
+                    acc = psum.tile([P, S], F32, name="out_acc", tag=f"num{b}")
                 else:
-                    fin = psum.tile([P, S], F32, name="fin", tag="acc", bufs=2)
-                for a in range(a0, a1):
-                    cols = slice(a * P, (a + 1) * P)
-                    nc.tensor.matmul_mx(out=fin[:, (a - a0) * P : (a - a0 + 1) * P], lhsT=wc[2][:, cols].bitcast(FP8X4), lhsT_scale=ws[2][:, cols],
-                                        rhs=zc[b][:].bitcast(FP8X4), rhs_scale=zs[b][:], start=True, stop=True)
-                res = keep.tile([P, a1 - a0, P], F32, name=f"res{b}_{a0}")
-                copy(res[:].rearrange("p a j -> p (a j)"), fin[:, : (a1 - a0) * P])
-                queue.dma_start(out.rearrange("(a p) j -> p a j", p=P)[:, a0:a1, b * P : (b + 1) * P], res[:])
+                    acc = psum.tile([P, S], F32, name="out_acc", tag="acc", bufs=2)
+                for a in range(2):
+                    cols = slice((2 * half + a) * P, (2 * half + a + 1) * P)
+                    nc.tensor.matmul_mx(out=acc[:, a * P : (a + 1) * P], lhsT=w_word[W3][:, cols].bitcast(FP8X4), lhsT_scale=w_scale[W3][:, cols],
+                                        rhs=z_word[b][:].bitcast(FP8X4), rhs_scale=z_scale[b][:], start=True, stop=True)
+                res = keep.tile([P, 2, P], F32, name=f"res{b}_{half}")
+                copy = nc.vector.tensor_copy if half == 1 and b >= BLOCKS // 2 else nc.scalar.copy
+                copy(res[:].rearrange("p a j -> p (a j)"), acc[:, : 2 * P])
+                nc.sync.dma_start(out.rearrange("(a p) j -> p a j", p=P)[:, 2 * half : 2 * half + 2, b * P : (b + 1) * P], res[:])
 
-        for t in range(PACK):
-            cast_dealt(1, nc.vector.tensor_copy, t, raw_w2[0], 0, HEADS // 2)
-        guide_of(0)
-        guide_of(1)
-        for t in range(PACK):
-            cast_dealt(1, nc.scalar.copy, t, raw_w2[1], HEADS // 2, HEADS)
-        guide_of(2)
-        guide_of(3)
-        weights_of(0)
-        quant_w(1)
-        weights_of(1)
-        den_of(0)
-        values_of(0)
-        own_terms(0)
-        weights_of(2)
-        den_of(1)
-        values_of(1)
-        own_terms(1)
-        weights_of(3)
-        terms_of(0)
-        den_of(2)
-        values_of(2)
-        own_terms(2)
-        values_of(3)
-        own_terms(3)
-        wbf.append(keep.tile([P, H * PACK], BF16, name="wbf2", tag="c_own3", align_bytes=64))
-        cast_plain(2, nc.scalar.copy, 0, 128)
-        den_of(3)
-        terms_of(1)
-        terms_of(2)
+        for t in range(TILES):
+            cast_tile_columns(W2, nc.vector.tensor_copy, t, w2_raw[0], 0, HEADS // 2)
+        make_c(0)
+        make_c(1)
+        for t in range(TILES):
+            cast_tile_columns(W2, nc.scalar.copy, t, w2_raw[1], HEADS // 2, HEADS)
+        make_c(2)
+        make_c(3)
+
+        make_e(0)
+        nc.vector.tensor_copy(c_own[1], c_win[1][:, :S])
+        quantise_weights(W2)
+        for t in range(1, TILES):
+            make_e(t)
+            make_den(t - 1)
+            make_val(t - 1)
+        make_terms(0, 0, BLOCKS)
+        make_val(TILES - 1)
+
+        w_bf16.append(keep.tile([P, N * PACK], BF16, name="w_bf16_2", tag="c_own_last", align_bytes=64))
+        nc.scalar.copy(w_bf16[W3][:].rearrange("p (c i s) -> p c s i", i=LINE, s=PACK), w3_raw[:].rearrange("p s (c i) -> p c s i", i=LINE))
+        make_den(TILES - 1)
+        for t in range(1, TILES - 1):
+            make_terms(t, 0, BLOCKS)
+
         for b in range(BLOCKS):
-            inverse_of(b)
-        for b0, b1 in ((0, 2), (2, 4)):
-            terms_of(PACK - 1, b0, b1)
-        quant_w(2)
+            make_inv(b)
+        for b0 in range(0, BLOCKS, BLOCKS // 2):
+            make_terms(TILES - 1, b0, b0 + BLOCKS // 2)
+        quantise_weights(W3)
         for b in range(BLOCKS):
-            average(b)
+            make_z(b)
         for b in range(BLOCKS):
-            finish(b)
+            make_out(b)

@@ -25,6 +25,7 @@ HALF = S // 2
 PER_COLUMN = 16
 LINE = 4
 W1, W2, W3 = 0, 1, 2
+W3_ON_VECTOR = 192
 
 
 def tile_picked_nlmean_none_p_kernel(tc, x_words, x_scales, w1, w2, w3, offs, p1, p2, out):
@@ -43,20 +44,21 @@ def tile_picked_nlmean_none_p_kernel(tc, x_words, x_scales, w1, w2, w3, offs, p1
         x_scale_all = keep.tile([P, T], U8, name="x_scale_all", align_bytes=64)
         nc.vector.memset(x_scale_all[:].bitcast(I32), 0)
         x_word_all = keep.tile([P, T], U32, name="x_word_all", align_bytes=64)
-        w1_raw = keep.tile([P, PACK, H], F32, name="w1_raw")
-        w3_raw = keep.tile([P, PACK, N], F32, name="w3_raw")
-        w2_raw = [keep.tile([P, PACK, H // 2], F32, name=f"w2_raw{h}") for h in range(2)]
+        w_raw = [[keep.tile([P, PACK, H // 2], F32, name=f"w_raw{w}_{h}", tag=f"w_raw{w}_{h}") for h in range(2)] for w in (W1, W2)]
 
-        nc.sync.dma_start(w1_raw[:], w1.rearrange("(p s) c -> p s c", s=PACK))
+        def load_half(w, src, h):
+            nc.sync.dma_start(w_raw[w][h][:], src.rearrange("(p s) c -> p s c", s=PACK)[:, :, h * H // 2 : (h + 1) * H // 2])
+
+        nc.sync.dma_start(x_word_all[:].bitcast(I32), x_words[0].rearrange("p n s -> p (n s)").bitcast(I32))
         nc.sync.dma_start(offs_sb[:], offs)
         for quad in range(4):
             nc.sync.dma_start(x_scale_all[32 * quad : 32 * quad + 4, :].bitcast(I32), x_scales[0, 4 * quad : 4 * quad + 4, :].bitcast(I32))
-        nc.sync.dma_start(x_word_all[:].bitcast(I32), x_words[0].rearrange("p n s -> p (n s)").bitcast(I32))
+        load_half(W1, w1, 0)
+        load_half(W1, w1, 1)
         nc.sync.dma_start(p_sb[0][:], p1)
         nc.sync.dma_start(p_sb[1][:], p2)
-        for h in range(2):
-            nc.sync.dma_start(w2_raw[h][:], w2.rearrange("(p s) c -> p s c", s=PACK)[:, :, h * H // 2 : (h + 1) * H // 2])
-        nc.sync.dma_start(w3_raw[:], w3.rearrange("(p s) c -> p s c", s=PACK))
+        load_half(W2, w2, 0)
+        load_half(W2, w2, 1)
 
         ident = keep.tile([P, P], F32, name="ident")
         make_identity(nc, ident[:])
@@ -65,86 +67,96 @@ def tile_picked_nlmean_none_p_kernel(tc, x_words, x_scales, w1, w2, w3, offs, p1
         for t in range(TILES):
             nc.vector.memset(c_win[t][:, S:], 0.0)
         val = [keep.tile([P, 2 * S if t < TILES - 1 else S], F32, name=f"val{t}") for t in range(TILES)]
-        c_own_last = keep.tile([P, S], F32, name="c_own_last", tag="c_own_last", align_bytes=64)
+        c_own_last = keep.tile([P, S], F32, name="c_own_last")
         c_own = [val[t][:, S:] for t in range(TILES - 1)] + [c_own_last[:]]
 
-        w_bf16 = [keep.tile([P, H * PACK], BF16, name=f"w_bf16_{w}", align_bytes=64) for w in (W1, W2)]
+        w_bf16 = [keep.tile([P, H * PACK], BF16, name=f"w_bf16_{w}", align_bytes=64) for w in (W1, W2, W3)]
         w_word = [keep.tile([P, H], U32, name=f"w_word{w}", align_bytes=64) for w in (W1, W2, W3)]
         w_scale = [keep.tile([P, H], U8, name=f"w_scale{w}", align_bytes=64) for w in (W1, W2, W3)]
 
-        def cast_tile_columns(w, copy, t, src, g0, g1):
-            copy(w_bf16[w][:].rearrange("p (t g c i s) -> p t g c s i", t=TILES, g=HEADS, i=LINE, s=PACK)[:, t, g0:g1],
-                 src[:].rearrange("p s (g t c i) -> p t g c s i", g=g1 - g0, t=TILES, i=LINE)[:, t])
+        def cast_tile_columns(w, copy, t, half):
+            g0 = half * HEADS // 2
+            copy(w_bf16[w][:].rearrange("p (t g c i s) -> p t g c s i", t=TILES, g=HEADS, i=LINE, s=PACK)[:, t, g0 : g0 + HEADS // 2],
+                 w_raw[w][half][:].rearrange("p s (g h u c i) -> p u h g c s i", g=HEADS // 2, h=2, u=2, i=LINE)[:, t // 2, t % 2])
 
-        def quantise_weights(w):
-            nc.vector.quantize_mx(out=w_word[w][:].bitcast(FP8X4), scales=w_scale[w][:], in_=w_bf16[w][:])
-
-        for t in range(TILES):
-            cast_tile_columns(W1, nc.vector.tensor_copy if t < TILES // 2 else nc.scalar.copy, t, w1_raw, 0, HEADS)
+        def quantise_weights(w, t0, t1):
+            nc.vector.quantize_mx(out=w_word[w][:, t0 * P : t1 * P].bitcast(FP8X4), scales=w_scale[w][:, t0 * P : t1 * P],
+                                  in_=w_bf16[w][:, t0 * P * PACK : t1 * P * PACK])
 
         x_scale = keep.tile([P, S], U8, name="x_scale", align_bytes=64)
         x_word = keep.tile([P, S], U32, name="x_word", align_bytes=64)
+        nc.vector.tensor_copy(x_word[:], x_word_all[:].indirect(offs_sb[:]))
         nc.vector.tensor_copy(x_scale[:], x_scale_all[:].indirect(offs_sb[:]))
-        quantise_weights(W1)
-        for j0 in range(0, S, HALF):
-            nc.vector.tensor_copy(x_word[:, j0 : j0 + HALF], x_word_all[:].indirect(entries(offs_sb, j0, j0 + HALF)))
 
-        def product_with_x(w, t, dst, j0, j1, bank):
-            acc = psum.tile([P, S], F32, name="acc", tag=bank, bufs=2)
+        for t in range(TILES):
+            cast_tile_columns(W1, nc.scalar.copy, t, 0)
+        for t in range(TILES):
+            cast_tile_columns(W1, nc.vector.tensor_copy if t == 0 else nc.scalar.copy, t, 1)
+        quantise_weights(W1, 0, 1)
+        quantise_weights(W1, 1, 2)
+        quantise_weights(W1, 2, TILES)
+
+        def product_with_x(w, t, j0, j1, bank, bufs):
+            acc = psum.tile([P, S], F32, name="acc", tag=bank, bufs=bufs)
             cols = slice(t * P, (t + 1) * P)
             nc.tensor.matmul_mx(out=acc[:, : j1 - j0], lhsT=w_word[w][:, cols].bitcast(FP8X4), lhsT_scale=w_scale[w][:, cols],
                                 rhs=x_word[:, j0:j1].bitcast(FP8X4), rhs_scale=x_scale[:, j0:j1], start=True, stop=True)
-            nc.scalar.copy(dst[:, j0:j1], acc[:, : j1 - j0])
+            return acc[:, : j1 - j0]
 
-        def make_c(t):
-            if t == 0:
-                for j0 in range(0, S, HALF):
-                    product_with_x(W1, t, c_win[t], j0, j0 + HALF, "acc")
-                    nc.vector.tensor_copy(c_own[t][:, j0 : j0 + HALF], c_win[t][:, j0 : j0 + HALF])
-            else:
-                product_with_x(W1, t, c_win[t], 0, S, "den" if t == 1 else "acc")
-                if t > 1:
-                    nc.sync.dma_start(c_own[t], c_win[t][:, :S])
+        def make_c(t, bank, bufs):
+            nc.scalar.copy(c_win[t][:, :S], product_with_x(W1, t, 0, S, bank, bufs))
+            nc.sync.dma_start(c_own[t], c_win[t][:, :S])
 
+        diff = [[keep.tile([P, S], F32, name=f"diff{t}_{n}", tag=f"diff{t}_{n}") for n in range(2)] for t in range(TILES)]
+        square = [[keep.tile([P, S], F32, name=f"square{t}_{n}", tag=f"square{t}_{n}") for n in range(2)] for t in range(TILES)]
         e = [[keep.tile([P, S], F32, name=f"e{t}_{n}") for n in range(2)] for t in range(TILES)]
 
-        def make_e(t):
-            for n in range(2):
-                diff = keep.tile([P, S], F32, name=f"diff{t}_{n}", tag=f"diff{t}_{n}")
-                nc.vector.tensor_tensor(diff[:], c_win[t][:].indirect(p_sb[n][:]), c_own[t], ALU.subtract)
-                square = keep.tile([P, S], F32, name="square", tag="square", bufs=2)
-                nc.scalar.activation(square[:], diff[:], ACT.Square)
-                nc.scalar.activation(e[t][n][:], square[:], ACT.Exp, scale=-0.5)
+        def make_diff(t, n, j0, j1):
+            nc.vector.tensor_tensor(diff[t][n][:, j0:j1], c_win[t][:].indirect(entries(p_sb[n], j0, j1)), c_own[t][:, j0:j1], ALU.subtract)
 
-        den_sq = keep.tile([P, TILES, S], F32, name="den_sq")
+        def make_square(t, n):
+            nc.scalar.activation(square[t][n][:], diff[t][n][:], ACT.Square)
 
-        def make_den(t):
-            den = psum.tile([P, S], F32, name="den", tag="den", bufs=2)
-            for n in range(2):
-                for b in range(BLOCKS):
-                    cols = slice(b * P, (b + 1) * P)
-                    nc.tensor.matmul(den[:, cols], e[t][n][:, cols], ident[:], start=(n == 0 and b == 0), stop=(n == 1 and b == BLOCKS - 1), is_transpose=True)
-            nc.scalar.activation(den_sq[:, t, :], den[:], ACT.Square, bias=1.0)
+        den = {}
 
-        num = [psum.tile([P, S], F32, name=f"num{b}", tag=f"num{b}") for b in range(BLOCKS)]
+        def make_e(t, n):
+            nc.scalar.activation(e[t][n][:], square[t][n][:], ACT.Exp, scale=-0.5)
+            if n == 0:
+                den[t] = psum.tile([P, S], F32, name="den", tag="den", bufs=2)
+            for b in range(BLOCKS):
+                cols = slice(b * P, (b + 1) * P)
+                nc.tensor.matmul(den[t][:, cols], e[t][n][:, cols], ident[:], start=(n == 0 and b == 0), stop=(n == 1 and b == BLOCKS - 1), is_transpose=True)
+
+        den_sq = keep.tile([P, BLOCKS, H], F32, name="den_sq")
+
+        def square_den(t):
+            nc.scalar.activation(den_sq[:].rearrange("j b (u g h q) -> j u h b g q", u=2, g=HEADS, h=2)[:, t // 2, t % 2],
+                                 den[t][:].rearrange("j (b g q) -> j b g q", b=BLOCKS, g=HEADS), ACT.Square, bias=1.0)
+
+        num = {}
 
         def add_to_num(t, b, term, first=False, last=False):
+            if first:
+                num[b] = psum.tile([P, S], F32, name=f"num{b}", tag=f"num{b}")
             nc.tensor.matmul(num[b][:, t * P : (t + 1) * P], term, ident[:], start=first, stop=last, is_transpose=True)
 
+        val_acc = {}
+
+        def multiply_val(t):
+            val_acc[t] = product_with_x(W2, t, 0, S, "acc", 2)
+
         def make_val(t):
-            product_with_x(W2, t, val[t], 0, S, "acc")
+            nc.scalar.copy(val[t][:, :S], val_acc[t])
+            if t + 2 < TILES:
+                multiply_val(t + 2)
             for b in range(BLOCKS):
                 add_to_num(t, b, val[t][:, b * P : (b + 1) * P], first=(t == 0))
 
         def make_terms(t, b0, b1):
             j0, j1 = b0 * P, b1 * P
             for n in range(2):
-                if t < 2:
-                    term = keep.tile([P, S], F32, name=f"term{t}_{n}", tag=f"diff{t + 2}_{n}")
-                elif t == 2:
-                    term = keep.tile([P, S], F32, name=f"term{t}_{n}", tag="square", bufs=2)
-                else:
-                    term = keep.tile([P, j1 - j0], F32, name=f"term{t}_{b0}_{n}")
+                held = [("diff2_1", "square2_0"), ("square2_1", "diff3_0"), ("square3_0", "square3_1")]
+                term = keep.tile([P, j1 - j0], F32, name=f"term{t}_{b0}_{n}", tag=held[t][n] if t < TILES - 1 else f"term{t}_{b0}_{n}")
                 nc.vector.tensor_tensor(term[:], val[t][:].indirect(entries(p_sb[n], j0, j1)), e[t][n][:, j0:j1], ALU.mult)
                 for b in range(b0, b1):
                     add_to_num(t, b, term[:, (b - b0) * P : (b - b0 + 1) * P], last=(t == TILES - 1 and n == 1))
@@ -152,26 +164,30 @@ def tile_picked_nlmean_none_p_kernel(tc, x_words, x_scales, w1, w2, w3, offs, p1
         inv = [keep.tile([P, H], F32, name=f"inv{b}") for b in range(BLOCKS)]
 
         def make_inv(b):
-            nc.scalar.activation(inv[b][:].rearrange("j (g t q) -> j g t q", g=HEADS, t=TILES),
-                                 den_sq[:, :, b * P : (b + 1) * P].rearrange("j t (g q) -> j g t q", g=HEADS), ACT.Abs_reciprocal_sqrt)
+            nc.scalar.activation(inv[b][:], den_sq[:, b, :], ACT.Abs_reciprocal_sqrt)
 
         z_word = [keep.tile([P, P], U32, name=f"z_word{b}", align_bytes=64) for b in range(BLOCKS)]
         z_scale = [keep.tile([P, P], U8, name=f"z_scale{b}", align_bytes=64) for b in range(BLOCKS)]
+        z_bf16 = [keep.tile([P, P * PACK], BF16, name=f"z_bf16_{b}", align_bytes=64) for b in range(BLOCKS)]
+        back = {}
 
-        def make_z(b):
-            z_rows = keep.tile([P, H], BF16, name=f"z_rows{b}", tag="z_bf16_0" if b == BLOCKS - 1 else f"z_rows{b}", align_bytes=64)
-            nc.vector.tensor_tensor(z_rows[:].rearrange("j (g t q) -> j g t q", g=HEADS, t=TILES),
-                                    num[b][:].rearrange("j (t g q) -> j g t q", g=HEADS, t=TILES),
-                                    inv[b][:].rearrange("j (g t q) -> j g t q", g=HEADS, t=TILES), ALU.mult)
-            pairs = z_rows[:].bitcast(F32)
-            back = psum.tile([P, 2, P], F32, name="back", tag="den", bufs=2)
-            for u in range(2):
-                nc.tensor.transpose(back[:, u, :], pairs[:, u::2], ident[:])
-            z_bf16 = keep.tile([P, P * PACK], BF16, name=f"z_bf16_{b}", tag=f"z_bf16_{b}", align_bytes=64)
-            nc.scalar.copy(z_bf16[:].bitcast(F32).rearrange("p (j u) -> p j u", u=2), back[:].rearrange("p u j -> p j u"))
-            nc.vector.quantize_mx(out=z_word[b][:].bitcast(FP8X4), scales=z_scale[b][:], in_=z_bf16[:])
+        def make_z(b, pieces):
+            z_rows = keep.tile([P, H], BF16, name=f"z_rows{b}", align_bytes=64)
+            back[b] = psum.tile([P, 2, P], F32, name="back", tag="den", bufs=2)
+            for u0 in range(0, 2, 2 // pieces):
+                for u in range(u0, u0 + 2 // pieces):
+                    nc.vector.tensor_tensor(z_rows[:].rearrange("j (u g h q) -> j u g h q", u=2, g=HEADS, h=2)[:, u],
+                                            num[b][:].rearrange("j (u h g q) -> j u g h q", u=2, g=HEADS, h=2)[:, u],
+                                            inv[b][:].rearrange("j (u g h q) -> j u g h q", u=2, g=HEADS, h=2)[:, u], ALU.mult)
+                    nc.tensor.transpose(back[b][:, u, :], z_rows[:].bitcast(F32)[:, u * P : (u + 1) * P], ident[:])
 
-        def make_out(b):
+        def interleave_z(b):
+            nc.scalar.copy(z_bf16[b][:].bitcast(F32).rearrange("p (j u) -> p j u", u=2), back[b][:].rearrange("p u j -> p j u"))
+
+        def quantise_z(b):
+            nc.vector.quantize_mx(out=z_word[b][:].bitcast(FP8X4), scales=z_scale[b][:], in_=z_bf16[b][:])
+
+        def make_out(b, copies):
             for half in range(2):
                 if half == 0:
                     acc = psum.tile([P, S], F32, name="out_acc", tag=f"num{b}")
@@ -182,41 +198,79 @@ def tile_picked_nlmean_none_p_kernel(tc, x_words, x_scales, w1, w2, w3, offs, p1
                     nc.tensor.matmul_mx(out=acc[:, a * P : (a + 1) * P], lhsT=w_word[W3][:, cols].bitcast(FP8X4), lhsT_scale=w_scale[W3][:, cols],
                                         rhs=z_word[b][:].bitcast(FP8X4), rhs_scale=z_scale[b][:], start=True, stop=True)
                 res = keep.tile([P, 2, P], F32, name=f"res{b}_{half}")
-                copy = nc.vector.tensor_copy if half == 1 and b >= BLOCKS // 2 else nc.scalar.copy
-                copy(res[:].rearrange("p a j -> p (a j)"), acc[:, : 2 * P])
+                copies[half](res[:].rearrange("p a j -> p (a j)"), acc[:, : 2 * P])
                 nc.sync.dma_start(out.rearrange("(a p) j -> p a j", p=P)[:, 2 * half : 2 * half + 2, b * P : (b + 1) * P], res[:])
 
+        for j0 in range(0, S, HALF):
+            nc.scalar.copy(c_win[0][:, j0 : j0 + HALF], product_with_x(W1, 0, j0, j0 + HALF, "acc", 2))
+        nc.vector.tensor_copy(c_own[0][:, :HALF], c_win[0][:, :HALF])
         for t in range(TILES):
-            cast_tile_columns(W2, nc.vector.tensor_copy, t, w2_raw[0], 0, HEADS // 2)
-        make_c(0)
-        make_c(1)
+            cast_tile_columns(W2, nc.vector.tensor_copy, t, 0)
+        make_diff(0, 0, 0, HALF)
+        nc.vector.tensor_copy(c_own[0][:, HALF:], c_win[0][:, HALF:S])
+        make_diff(0, 1, 0, HALF)
+        make_diff(0, 0, HALF, S)
+        make_diff(0, 1, HALF, S)
+        make_c(1, "den", 2)
+        make_c(2, "den", 2)
         for t in range(TILES):
-            cast_tile_columns(W2, nc.scalar.copy, t, w2_raw[1], HEADS // 2, HEADS)
-        make_c(2)
-        make_c(3)
+            cast_tile_columns(W2, nc.scalar.copy, t, 1)
+        quantise_weights(W2, 0, TILES)
+        multiply_val(0)
+        multiply_val(1)
 
-        make_e(0)
-        nc.vector.tensor_copy(c_own[1], c_win[1][:, :S])
-        quantise_weights(W2)
+        w3_raw = keep.tile([P, PACK, N], F32, name="w3_raw", tag="w_raw1_1")
+        for u in range(2):
+            nc.sync.dma_start(w3_raw[:, 2 * u : 2 * u + 2, :].rearrange("p e c -> p (e c)"),
+                              w3.rearrange("(blk u r e) c -> u blk r (e c)", u=2, r=8, e=2)[u])
+
+        def cast_w3(copy, c0, c1):
+            copy(w_bf16[W3][:, c0 * PACK : c1 * PACK].rearrange("p (c i s) -> p c s i", i=LINE, s=PACK), w3_raw[:, :, c0:c1].rearrange("p s (c i) -> p c s i", i=LINE))
+
+        make_square(0, 0)
+        make_c(3, "num0", 1)
+        make_square(0, 1)
+        make_e(0, 0)
+        make_e(0, 1)
         for t in range(1, TILES):
-            make_e(t)
-            make_den(t - 1)
+            for n in range(2):
+                make_diff(t, n, 0, S)
+        cast_w3(nc.vector.tensor_copy, 0, W3_ON_VECTOR)
+        for t in range(1, TILES):
             make_val(t - 1)
+            make_square(t, 0)
+            make_square(t, 1)
+            make_e(t, 0)
+            square_den(t - 1)
+            make_e(t, 1)
         make_terms(0, 0, BLOCKS)
+        make_terms(1, 0, BLOCKS)
         make_val(TILES - 1)
-
-        w_bf16.append(keep.tile([P, N * PACK], BF16, name="w_bf16_2", tag="c_own_last", align_bytes=64))
-        nc.scalar.copy(w_bf16[W3][:].rearrange("p (c i s) -> p c s i", i=LINE, s=PACK), w3_raw[:].rearrange("p s (c i) -> p c s i", i=LINE))
-        make_den(TILES - 1)
-        for t in range(1, TILES - 1):
-            make_terms(t, 0, BLOCKS)
-
-        for b in range(BLOCKS):
-            make_inv(b)
+        make_terms(2, 0, BLOCKS)
         for b0 in range(0, BLOCKS, BLOCKS // 2):
             make_terms(TILES - 1, b0, b0 + BLOCKS // 2)
-        quantise_weights(W3)
-        for b in range(BLOCKS):
-            make_z(b)
-        for b in range(BLOCKS):
-            make_out(b)
+        cast_w3(nc.scalar.copy, W3_ON_VECTOR, N)
+        square_den(TILES - 1)
+        quantise_weights(W3, 0, TILES)
+
+        sc, vc = nc.scalar.copy, nc.vector.tensor_copy
+        make_inv(0)
+        make_inv(1)
+        make_z(0, 2)
+        make_inv(2)
+        make_z(1, 2)
+        interleave_z(0)
+        make_inv(3)
+        make_z(2, 2)
+        quantise_z(0)
+        interleave_z(1)
+        make_z(3, 2)
+        quantise_z(1)
+        interleave_z(2)
+        make_out(0, (sc, vc))
+        interleave_z(3)
+        quantise_z(2)
+        quantise_z(3)
+        make_out(1, (sc, vc))
+        make_out(2, (sc, vc))
+        make_out(3, (sc, vc))

@@ -60,6 +60,11 @@ def tile_picked_nlmean_none_p_kernel(tc, x_words, x_scales, w1, w2, w3, offs, p1
         load_half(W2, w2, 0)
         load_half(W2, w2, 1)
 
+        w3_raw = keep.tile([P, PACK, N], F32, name="w3_raw")
+        for u in range(2):
+            nc.sync.dma_start(w3_raw[:, 2 * u : 2 * u + 2, :].rearrange("p e c -> p (e c)"),
+                              w3.rearrange("(blk u r e) c -> u blk r (e c)", u=2, r=8, e=2)[u])
+
         ident = keep.tile([P, P], F32, name="ident")
         make_identity(nc, ident[:])
 
@@ -105,9 +110,10 @@ def tile_picked_nlmean_none_p_kernel(tc, x_words, x_scales, w1, w2, w3, offs, p1
 
         def make_c(t, bank, bufs):
             nc.scalar.copy(c_win[t][:, :S], product_with_x(W1, t, 0, S, bank, bufs))
-            nc.sync.dma_start(c_own[t], c_win[t][:, :S])
+            if t > 1:
+                nc.sync.dma_start(c_own[t], c_win[t][:, :S])
 
-        diff = [[keep.tile([P, S], F32, name=f"diff{t}_{n}", tag=f"diff{t}_{n}") for n in range(2)] for t in range(TILES)]
+        diff = [[keep.tile([P, S], F32, name=f"diff{t}_{n}", tag=f"diff{t}_{n}")[:] for n in range(2)] if t != 1 else None for t in range(TILES)]
         square = [[keep.tile([P, S], F32, name=f"square{t}_{n}", tag=f"square{t}_{n}") for n in range(2)] for t in range(TILES)]
         e = [[keep.tile([P, S], F32, name=f"e{t}_{n}") for n in range(2)] for t in range(TILES)]
 
@@ -115,7 +121,7 @@ def tile_picked_nlmean_none_p_kernel(tc, x_words, x_scales, w1, w2, w3, offs, p1
             nc.vector.tensor_tensor(diff[t][n][:, j0:j1], c_win[t][:].indirect(entries(p_sb[n], j0, j1)), c_own[t][:, j0:j1], ALU.subtract)
 
         def make_square(t, n):
-            nc.scalar.activation(square[t][n][:], diff[t][n][:], ACT.Square)
+            nc.scalar.activation(square[t][n][:], diff[t][n], ACT.Square)
 
         den = {}
 
@@ -212,17 +218,15 @@ def tile_picked_nlmean_none_p_kernel(tc, x_words, x_scales, w1, w2, w3, offs, p1
         make_diff(0, 0, HALF, S)
         make_diff(0, 1, HALF, S)
         make_c(1, "den", 2)
+        nc.vector.tensor_copy(c_own[1], c_win[1][:, :S])
         make_c(2, "den", 2)
         for t in range(TILES):
             cast_tile_columns(W2, nc.scalar.copy, t, 1)
         quantise_weights(W2, 0, TILES)
         multiply_val(0)
         multiply_val(1)
-
-        w3_raw = keep.tile([P, PACK, N], F32, name="w3_raw", tag="w_raw1_1")
-        for u in range(2):
-            nc.sync.dma_start(w3_raw[:, 2 * u : 2 * u + 2, :].rearrange("p e c -> p (e c)"),
-                              w3.rearrange("(blk u r e) c -> u blk r (e c)", u=2, r=8, e=2)[u])
+        diff_pair = keep.tile([P, 2, S], F32, name="diff1", tag="w_raw1_1")
+        diff[1] = [diff_pair[:, n, :] for n in range(2)]
 
         def cast_w3(copy, c0, c1):
             copy(w_bf16[W3][:, c0 * PACK : c1 * PACK].rearrange("p (c i s) -> p c s i", i=LINE, s=PACK), w3_raw[:, :, c0:c1].rearrange("p s (c i) -> p c s i", i=LINE))

@@ -25,7 +25,6 @@ HALF = S // 2
 PER_COLUMN = 16
 LINE = 4
 W1, W2, W3 = 0, 1, 2
-W3_ON_VECTOR = 192
 
 
 def tile_picked_nlmean_none_p_kernel(tc, x_words, x_scales, w1, w2, w3, offs, p1, p2, out):
@@ -60,11 +59,6 @@ def tile_picked_nlmean_none_p_kernel(tc, x_words, x_scales, w1, w2, w3, offs, p1
         load_half(W2, w2, 0)
         load_half(W2, w2, 1)
 
-        w3_raw = keep.tile([P, PACK, N], F32, name="w3_raw")
-        for u in range(2):
-            nc.sync.dma_start(w3_raw[:, 2 * u : 2 * u + 2, :].rearrange("p e c -> p (e c)"),
-                              w3.rearrange("(blk u r e) c -> u blk r (e c)", u=2, r=8, e=2)[u])
-
         ident = keep.tile([P, P], F32, name="ident")
         make_identity(nc, ident[:])
 
@@ -75,7 +69,7 @@ def tile_picked_nlmean_none_p_kernel(tc, x_words, x_scales, w1, w2, w3, offs, p1
         c_own_last = keep.tile([P, S], F32, name="c_own_last")
         c_own = [val[t][:, S:] for t in range(TILES - 1)] + [c_own_last[:]]
 
-        w_bf16 = [keep.tile([P, H * PACK], BF16, name=f"w_bf16_{w}", align_bytes=64) for w in (W1, W2, W3)]
+        w_bf16 = [keep.tile([P, H * PACK], BF16, name=f"w_bf16_{w}", tag=f"w_bf16_{w}", align_bytes=64) for w in (W1, W2)]
         w_word = [keep.tile([P, H], U32, name=f"w_word{w}", align_bytes=64) for w in (W1, W2, W3)]
         w_scale = [keep.tile([P, H], U8, name=f"w_scale{w}", align_bytes=64) for w in (W1, W2, W3)]
 
@@ -113,8 +107,8 @@ def tile_picked_nlmean_none_p_kernel(tc, x_words, x_scales, w1, w2, w3, offs, p1
             if t > 1:
                 nc.sync.dma_start(c_own[t], c_win[t][:, :S])
 
-        diff = [[keep.tile([P, S], F32, name=f"diff{t}_{n}", tag=f"diff{t}_{n}")[:] for n in range(2)] if t != 1 else None for t in range(TILES)]
-        square = [[keep.tile([P, S], F32, name=f"square{t}_{n}", tag=f"square{t}_{n}") for n in range(2)] for t in range(TILES)]
+        diff = [[keep.tile([P, S], F32, name=f"diff{t}_{n}", tag=f"diff{t}_{n}", align_bytes=64)[:] for n in range(2)] if t != 1 else None for t in range(TILES)]
+        square = [[keep.tile([P, S], F32, name=f"square{t}_{n}", tag=f"square{t}_{n}", align_bytes=64) for n in range(2)] for t in range(TILES)]
         e = [[keep.tile([P, S], F32, name=f"e{t}_{n}") for n in range(2)] for t in range(TILES)]
 
         def make_diff(t, n, j0, j1):
@@ -133,11 +127,12 @@ def tile_picked_nlmean_none_p_kernel(tc, x_words, x_scales, w1, w2, w3, offs, p1
                 cols = slice(b * P, (b + 1) * P)
                 nc.tensor.matmul(den[t][:, cols], e[t][n][:, cols], ident[:], start=(n == 0 and b == 0), stop=(n == 1 and b == BLOCKS - 1), is_transpose=True)
 
-        den_sq = keep.tile([P, BLOCKS, H], F32, name="den_sq")
+        den_sq = [keep.tile([P, BLOCKS // 2, H], F32, name=f"den_sq{k}", tag=f"den_sq{k}", align_bytes=64) for k in range(2)]
 
         def square_den(t):
-            nc.scalar.activation(den_sq[:].rearrange("j b (u g h q) -> j u h b g q", u=2, g=HEADS, h=2)[:, t // 2, t % 2],
-                                 den[t][:].rearrange("j (b g q) -> j b g q", b=BLOCKS, g=HEADS), ACT.Square, bias=1.0)
+            for k in range(2):
+                nc.scalar.activation(den_sq[k][:].rearrange("j b (u g h q) -> j u h b g q", u=2, g=HEADS, h=2)[:, t // 2, t % 2],
+                                     den[t][:, k * HALF : (k + 1) * HALF].rearrange("j (b g q) -> j b g q", b=BLOCKS // 2, g=HEADS), ACT.Square, bias=1.0)
 
         num = {}
 
@@ -162,24 +157,24 @@ def tile_picked_nlmean_none_p_kernel(tc, x_words, x_scales, w1, w2, w3, offs, p1
             j0, j1 = b0 * P, b1 * P
             for n in range(2):
                 held = [("diff2_1", "square2_0"), ("square2_1", "diff3_0"), ("square3_0", "square3_1")]
-                term = keep.tile([P, j1 - j0], F32, name=f"term{t}_{b0}_{n}", tag=held[t][n] if t < TILES - 1 else f"term{t}_{b0}_{n}")
+                term = keep.tile([P, j1 - j0], F32, name=f"term{t}_{b0}_{n}", tag=held[t][n] if t < TILES - 1 else f"term{t}_{b0}_{n}", align_bytes=64)
                 nc.vector.tensor_tensor(term[:], val[t][:].indirect(entries(p_sb[n], j0, j1)), e[t][n][:, j0:j1], ALU.mult)
                 for b in range(b0, b1):
                     add_to_num(t, b, term[:, (b - b0) * P : (b - b0 + 1) * P], last=(t == TILES - 1 and n == 1))
 
-        inv = [keep.tile([P, H], F32, name=f"inv{b}") for b in range(BLOCKS)]
+        inv = [keep.tile([P, H], F32, name=f"inv{b}", tag=f"inv{b}", align_bytes=64) for b in range(BLOCKS)]
 
         def make_inv(b):
-            nc.scalar.activation(inv[b][:], den_sq[:, b, :], ACT.Abs_reciprocal_sqrt)
+            nc.scalar.activation(inv[b][:], den_sq[b // 2][:, b % 2, :], ACT.Abs_reciprocal_sqrt)
 
-        z_word = [keep.tile([P, P], U32, name=f"z_word{b}", align_bytes=64) for b in range(BLOCKS)]
-        z_scale = [keep.tile([P, P], U8, name=f"z_scale{b}", align_bytes=64) for b in range(BLOCKS)]
+        z_word = keep.tile([P, S], U32, name="z_word", align_bytes=64)
+        z_scale = keep.tile([P, S], U8, name="z_scale", align_bytes=64)
         z_bf16 = [keep.tile([P, P * PACK], BF16, name=f"z_bf16_{b}", align_bytes=64) for b in range(BLOCKS)]
         back = {}
 
         def make_z(b, pieces):
-            z_rows = keep.tile([P, H], BF16, name=f"z_rows{b}", align_bytes=64)
-            back[b] = psum.tile([P, 2, P], F32, name="back", tag="den", bufs=2)
+            z_rows = keep.tile([P, H], BF16, name=f"z_rows{b}", tag=f"z_rows{b}", align_bytes=64)
+            back[b] = psum.tile([P, 2, P], F32, name="back", tag="den" if b < 2 else "acc", bufs=2)
             for u0 in range(0, 2, 2 // pieces):
                 for u in range(u0, u0 + 2 // pieces):
                     nc.vector.tensor_tensor(z_rows[:].rearrange("j (u g h q) -> j u g h q", u=2, g=HEADS, h=2)[:, u],
@@ -191,21 +186,27 @@ def tile_picked_nlmean_none_p_kernel(tc, x_words, x_scales, w1, w2, w3, offs, p1
             nc.scalar.copy(z_bf16[b][:].bitcast(F32).rearrange("p (j u) -> p j u", u=2), back[b][:].rearrange("p u j -> p j u"))
 
         def quantise_z(b):
-            nc.vector.quantize_mx(out=z_word[b][:].bitcast(FP8X4), scales=z_scale[b][:], in_=z_bf16[b][:])
+            nc.vector.quantize_mx(out=z_word[:, b * P : (b + 1) * P].bitcast(FP8X4), scales=z_scale[:, b * P : (b + 1) * P], in_=z_bf16[b][:])
 
-        def make_out(b, copies):
-            for half in range(2):
-                if half == 0:
-                    acc = psum.tile([P, S], F32, name="out_acc", tag=f"num{b}")
-                else:
-                    acc = psum.tile([P, S], F32, name="out_acc", tag="acc", bufs=2)
-                for a in range(2):
-                    cols = slice((2 * half + a) * P, (2 * half + a + 1) * P)
-                    nc.tensor.matmul_mx(out=acc[:, a * P : (a + 1) * P], lhsT=w_word[W3][:, cols].bitcast(FP8X4), lhsT_scale=w_scale[W3][:, cols],
-                                        rhs=z_word[b][:].bitcast(FP8X4), rhs_scale=z_scale[b][:], start=True, stop=True)
-                res = keep.tile([P, 2, P], F32, name=f"res{b}_{half}")
-                copies[half](res[:].rearrange("p a j -> p (a j)"), acc[:, : 2 * P])
-                nc.sync.dma_start(out.rearrange("(a p) j -> p a j", p=P)[:, 2 * half : 2 * half + 2, b * P : (b + 1) * P], res[:])
+        out_acc = {}
+
+        def multiply_out(b, banks):
+            per_bank = TILES // len(banks)
+            out_acc[b] = []
+            for k, bank in enumerate(banks):
+                acc = psum.tile([P, per_bank, P], F32, name="out_acc", tag=bank, bufs=2 if bank == "den" else 1)
+                for a in range(per_bank):
+                    cols = slice((per_bank * k + a) * P, (per_bank * k + a + 1) * P)
+                    nc.tensor.matmul_mx(out=acc[:, a, :], lhsT=w_word[W3][:, cols].bitcast(FP8X4), lhsT_scale=w_scale[W3][:, cols],
+                                        rhs=z_word[:, b * P : (b + 1) * P].bitcast(FP8X4), rhs_scale=z_scale[:, b * P : (b + 1) * P], start=True, stop=True)
+                out_acc[b].append(acc)
+
+        def store_out(b, copies):
+            per_bank = TILES // len(copies)
+            for k, copy in enumerate(copies):
+                res = keep.tile([P, per_bank, P], F32, name=f"res{b}_{k}")
+                copy(res[:], out_acc[b][k][:])
+                nc.sync.dma_start(out.rearrange("(a p) j -> p a j", p=P)[:, per_bank * k : per_bank * (k + 1), b * P : (b + 1) * P], res[:])
 
         for j0 in range(0, S, HALF):
             nc.scalar.copy(c_win[0][:, j0 : j0 + HALF], product_with_x(W1, 0, j0, j0 + HALF, "acc", 2))
@@ -220,6 +221,7 @@ def tile_picked_nlmean_none_p_kernel(tc, x_words, x_scales, w1, w2, w3, offs, p1
         make_c(1, "den", 2)
         nc.vector.tensor_copy(c_own[1], c_win[1][:, :S])
         make_c(2, "den", 2)
+        make_c(3, "num0", 1)
         for t in range(TILES):
             cast_tile_columns(W2, nc.scalar.copy, t, 1)
         quantise_weights(W2, 0, TILES)
@@ -228,53 +230,68 @@ def tile_picked_nlmean_none_p_kernel(tc, x_words, x_scales, w1, w2, w3, offs, p1
         diff_pair = keep.tile([P, 2, S], F32, name="diff1", tag="w_raw1_1")
         diff[1] = [diff_pair[:, n, :] for n in range(2)]
 
-        def cast_w3(copy, c0, c1):
-            copy(w_bf16[W3][:, c0 * PACK : c1 * PACK].rearrange("p (c i s) -> p c s i", i=LINE, s=PACK), w3_raw[:, :, c0:c1].rearrange("p s (c i) -> p c s i", i=LINE))
+        w3_raw = keep.tile([P, PACK, N], F32, name="w3_raw", tag="w_bf16_1", align_bytes=64)
+        for u in range(2):
+            nc.sync.dma_start(w3_raw[:, 2 * u : 2 * u + 2, :].rearrange("p e c -> p (e c)"),
+                              w3.rearrange("(blk u r e) c -> u blk r (e c)", u=2, r=8, e=2)[u])
+
+        def cast_w3(k, tag):
+            half = keep.tile([P, N // 2 * PACK], BF16, name=f"w3_bf16_{k}", tag=tag, align_bytes=64)
+            nc.scalar.copy(half[:].rearrange("p (c i s) -> p c s i", i=LINE, s=PACK),
+                           w3_raw[:, :, k * N // 2 : (k + 1) * N // 2].rearrange("p s (c i) -> p c s i", i=LINE))
+            return half
+
+        def quantise_w3(k, half):
+            cols = slice(k * N // 2, (k + 1) * N // 2)
+            nc.vector.quantize_mx(out=w_word[W3][:, cols].bitcast(FP8X4), scales=w_scale[W3][:, cols], in_=half[:])
 
         make_square(0, 0)
-        make_c(3, "num0", 1)
         make_square(0, 1)
         make_e(0, 0)
         make_e(0, 1)
         for t in range(1, TILES):
             for n in range(2):
                 make_diff(t, n, 0, S)
-        cast_w3(nc.vector.tensor_copy, 0, W3_ON_VECTOR)
         for t in range(1, TILES):
             make_val(t - 1)
             make_square(t, 0)
             make_square(t, 1)
             make_e(t, 0)
-            square_den(t - 1)
+            if t < TILES - 1:
+                square_den(t - 1)
             make_e(t, 1)
+        square_den(TILES - 2)
         make_terms(0, 0, BLOCKS)
         make_terms(1, 0, BLOCKS)
         make_val(TILES - 1)
         make_terms(2, 0, BLOCKS)
-        for b0 in range(0, BLOCKS, BLOCKS // 2):
-            make_terms(TILES - 1, b0, b0 + BLOCKS // 2)
-        cast_w3(nc.scalar.copy, W3_ON_VECTOR, N)
+        make_terms(TILES - 1, 0, 2)
+        make_terms(TILES - 1, 2, 4)
+        w3_first = cast_w3(0, "w3_bf16_0")
         square_den(TILES - 1)
-        quantise_weights(W3, 0, TILES)
 
         sc, vc = nc.scalar.copy, nc.vector.tensor_copy
-        make_inv(0)
-        make_inv(1)
+        for b in range(BLOCKS):
+            make_inv(b)
+        w3_second = cast_w3(1, "den_sq0")
         make_z(0, 2)
-        make_inv(2)
         make_z(1, 2)
         interleave_z(0)
-        make_inv(3)
         make_z(2, 2)
-        quantise_z(0)
         interleave_z(1)
         make_z(3, 2)
-        quantise_z(1)
         interleave_z(2)
-        make_out(0, (sc, vc))
         interleave_z(3)
-        quantise_z(2)
-        quantise_z(3)
-        make_out(1, (sc, vc))
-        make_out(2, (sc, vc))
-        make_out(3, (sc, vc))
+        quantise_w3(0, w3_first)
+        quantise_z(0)
+        quantise_w3(1, w3_second)
+        for b in range(1, BLOCKS):
+            quantise_z(b)
+        multiply_out(0, ["num0", "den"])
+        multiply_out(1, ["num1", "den"])
+        store_out(0, [sc, vc])
+        multiply_out(2, ["num2", "den"])
+        store_out(1, [vc, sc])
+        multiply_out(3, ["num3", "den"])
+        store_out(2, [sc, vc])
+        store_out(3, [sc, vc])

@@ -50,8 +50,8 @@ def tile_picked_nlmean_none_p_kernel(tc, x_words, x_scales, w1, w2, w3, offs, p1
 
         nc.sync.dma_start(x_word_all[:].bitcast(I32), x_words[0].rearrange("p n s -> p (n s)").bitcast(I32))
         nc.sync.dma_start(offs_sb[:], offs)
-        for quad in range(4):
-            nc.sync.dma_start(x_scale_all[32 * quad : 32 * quad + 4, :].bitcast(I32), x_scales[0, 4 * quad : 4 * quad + 4, :].bitcast(I32))
+        for r in range(4):
+            nc.sync.dma_start(x_scale_all[r::32, :].bitcast(I32), x_scales[0, r::4, :].bitcast(I32))
         load_half(W1, w1, 0)
         load_half(W1, w1, 1)
         nc.sync.dma_start(p_sb[0][:], p1)
@@ -139,7 +139,7 @@ def tile_picked_nlmean_none_p_kernel(tc, x_words, x_scales, w1, w2, w3, offs, p1
         def add_to_num(t, b, term, first=False, last=False):
             if first:
                 num[b] = psum.tile([P, S], F32, name=f"num{b}", tag=f"num{b}")
-            nc.tensor.matmul(num[b][:, t * P : (t + 1) * P], term, ident[:], start=first, stop=last, is_transpose=True)
+            nc.tensor.matmul(num[b][:].rearrange("j (u g h q) -> j u h g q", u=2, g=HEADS, h=2)[:, t // 2, t % 2], term, ident[:], start=first, stop=last, is_transpose=True)
 
         val_acc = {}
 
@@ -175,11 +175,10 @@ def tile_picked_nlmean_none_p_kernel(tc, x_words, x_scales, w1, w2, w3, offs, p1
         def make_z(b, pieces):
             z_rows = keep.tile([P, H], BF16, name=f"z_rows{b}", tag=f"z_rows{b}", align_bytes=64)
             back[b] = psum.tile([P, 2, P], F32, name="back", tag="den" if b < 2 else "acc", bufs=2)
-            for u0 in range(0, 2, 2 // pieces):
-                for u in range(u0, u0 + 2 // pieces):
-                    nc.vector.tensor_tensor(z_rows[:].rearrange("j (u g h q) -> j u g h q", u=2, g=HEADS, h=2)[:, u],
-                                            num[b][:].rearrange("j (u h g q) -> j u g h q", u=2, g=HEADS, h=2)[:, u],
-                                            inv[b][:].rearrange("j (u g h q) -> j u g h q", u=2, g=HEADS, h=2)[:, u], ALU.mult)
+            width = H // pieces
+            for i0 in range(0, H, width):
+                nc.vector.tensor_tensor(z_rows[:, i0 : i0 + width], num[b][:, i0 : i0 + width], inv[b][:, i0 : i0 + width], ALU.mult)
+                for u in range(i0 // (2 * P), (i0 + width) // (2 * P)):
                     nc.tensor.transpose(back[b][:, u, :], z_rows[:].bitcast(F32)[:, u * P : (u + 1) * P], ident[:])
 
         def interleave_z(b):
@@ -190,23 +189,23 @@ def tile_picked_nlmean_none_p_kernel(tc, x_words, x_scales, w1, w2, w3, offs, p1
 
         out_acc = {}
 
-        def multiply_out(b, banks):
+        def multiply_out(j0, banks):
             per_bank = TILES // len(banks)
-            out_acc[b] = []
+            out_acc[j0] = []
             for k, bank in enumerate(banks):
-                acc = psum.tile([P, per_bank, P], F32, name="out_acc", tag=bank, bufs=2 if bank == "den" else 1)
+                acc = psum.tile([P, per_bank, HALF], F32, name="out_acc", tag=bank, bufs=2 if bank in ("den", "acc") else 1)
                 for a in range(per_bank):
                     cols = slice((per_bank * k + a) * P, (per_bank * k + a + 1) * P)
                     nc.tensor.matmul_mx(out=acc[:, a, :], lhsT=w_word[W3][:, cols].bitcast(FP8X4), lhsT_scale=w_scale[W3][:, cols],
-                                        rhs=z_word[:, b * P : (b + 1) * P].bitcast(FP8X4), rhs_scale=z_scale[:, b * P : (b + 1) * P], start=True, stop=True)
-                out_acc[b].append(acc)
+                                        rhs=z_word[:, j0 : j0 + HALF].bitcast(FP8X4), rhs_scale=z_scale[:, j0 : j0 + HALF], start=True, stop=True)
+                out_acc[j0].append(acc)
 
-        def store_out(b, copies):
+        def store_out(j0, copies):
             per_bank = TILES // len(copies)
             for k, copy in enumerate(copies):
-                res = keep.tile([P, per_bank, P], F32, name=f"res{b}_{k}")
-                copy(res[:], out_acc[b][k][:])
-                nc.sync.dma_start(out.rearrange("(a p) j -> p a j", p=P)[:, per_bank * k : per_bank * (k + 1), b * P : (b + 1) * P], res[:])
+                res = keep.tile([P, per_bank, HALF], F32, name=f"res{j0}_{k}")
+                copy(res[:], out_acc[j0][k][:])
+                nc.sync.dma_start(out.rearrange("(a p) j -> p a j", p=P)[:, per_bank * k : per_bank * (k + 1), j0 : j0 + HALF], res[:])
 
         for j0 in range(0, S, HALF):
             nc.scalar.copy(c_win[0][:, j0 : j0 + HALF], product_with_x(W1, 0, j0, j0 + HALF, "acc", 2))
@@ -274,10 +273,10 @@ def tile_picked_nlmean_none_p_kernel(tc, x_words, x_scales, w1, w2, w3, offs, p1
         for b in range(BLOCKS):
             make_inv(b)
         w3_second = cast_w3(1, "den_sq0")
-        make_z(0, 2)
-        make_z(1, 2)
+        make_z(0, 1)
+        make_z(1, 1)
         interleave_z(0)
-        make_z(2, 2)
+        make_z(2, 1)
         interleave_z(1)
         make_z(3, 2)
         interleave_z(2)
@@ -287,11 +286,7 @@ def tile_picked_nlmean_none_p_kernel(tc, x_words, x_scales, w1, w2, w3, offs, p1
         quantise_w3(1, w3_second)
         for b in range(1, BLOCKS):
             quantise_z(b)
-        multiply_out(0, ["num0", "den"])
-        multiply_out(1, ["num1", "den"])
-        store_out(0, [sc, vc])
-        multiply_out(2, ["num2", "den"])
-        store_out(1, [vc, sc])
-        multiply_out(3, ["num3", "den"])
-        store_out(2, [sc, vc])
-        store_out(3, [sc, vc])
+        multiply_out(0, ["num0", "num1", "num2", "num3"])
+        multiply_out(HALF, ["den", "den", "acc", "acc"])
+        store_out(0, [sc, vc, sc, vc])
+        store_out(HALF, [sc, vc, sc, vc])

@@ -70,7 +70,7 @@ def tile_picked_nlmean_none_p_kernel(tc, x_words, x_scales, w1, w2, w3, offs, p1
         c_own = [val[t][:, S:] for t in range(TILES - 1)] + [c_own_last[:]]
 
         w_bf16 = [keep.tile([P, H * PACK], BF16, name=f"w_bf16_{w}", tag=f"w_bf16_{w}", align_bytes=64) for w in (W1, W2)]
-        w_word = [keep.tile([P, H], U32, name=f"w_word{w}", align_bytes=64) for w in (W1, W2, W3)]
+        w_word = [keep.tile([P, H], U32, name=f"w_word{w}", align_bytes=64) for w in (W1, W2)]
         w_scale = [keep.tile([P, H], U8, name=f"w_scale{w}", align_bytes=64) for w in (W1, W2, W3)]
 
         def cast_tile_columns(w, copy, t, half):
@@ -90,7 +90,7 @@ def tile_picked_nlmean_none_p_kernel(tc, x_words, x_scales, w1, w2, w3, offs, p1
         for t in range(TILES):
             cast_tile_columns(W1, nc.scalar.copy, t, 0)
         for t in range(TILES):
-            cast_tile_columns(W1, nc.vector.tensor_copy if t == 0 else nc.scalar.copy, t, 1)
+            cast_tile_columns(W1, nc.vector.tensor_copy if t in (0, TILES - 1) else nc.scalar.copy, t, 1)
         quantise_weights(W1, 0, 1)
         quantise_weights(W1, 1, 2)
         quantise_weights(W1, 2, TILES)
@@ -109,7 +109,7 @@ def tile_picked_nlmean_none_p_kernel(tc, x_words, x_scales, w1, w2, w3, offs, p1
 
         diff = [[keep.tile([P, S], F32, name=f"diff{t}_{n}", tag=f"diff{t}_{n}", align_bytes=64)[:] for n in range(2)] if t != 1 else None for t in range(TILES)]
         square = [[keep.tile([P, S], F32, name=f"square{t}_{n}", tag=f"square{t}_{n}", align_bytes=64) for n in range(2)] for t in range(TILES)]
-        e = [[keep.tile([P, S], F32, name=f"e{t}_{n}") for n in range(2)] for t in range(TILES)]
+        e = [[keep.tile([P, S], F32, name=f"e{t}_{n}", tag=f"e{t}_{n}", align_bytes=64) for n in range(2)] for t in range(TILES)]
 
         def make_diff(t, n, j0, j1):
             nc.vector.tensor_tensor(diff[t][n][:, j0:j1], c_win[t][:].indirect(entries(p_sb[n], j0, j1)), c_own[t][:, j0:j1], ALU.subtract)
@@ -188,6 +188,7 @@ def tile_picked_nlmean_none_p_kernel(tc, x_words, x_scales, w1, w2, w3, offs, p1
             nc.vector.quantize_mx(out=z_word[:, b * P : (b + 1) * P].bitcast(FP8X4), scales=z_scale[:, b * P : (b + 1) * P], in_=z_bf16[b][:])
 
         out_acc = {}
+        w3_word = {}
 
         def multiply_out(j0, banks):
             per_bank = TILES // len(banks)
@@ -195,8 +196,8 @@ def tile_picked_nlmean_none_p_kernel(tc, x_words, x_scales, w1, w2, w3, offs, p1
             for k, bank in enumerate(banks):
                 acc = psum.tile([P, per_bank, HALF], F32, name="out_acc", tag=bank, bufs=2 if bank in ("den", "acc") else 1)
                 for a in range(per_bank):
-                    cols = slice((per_bank * k + a) * P, (per_bank * k + a + 1) * P)
-                    nc.tensor.matmul_mx(out=acc[:, a, :], lhsT=w_word[W3][:, cols].bitcast(FP8X4), lhsT_scale=w_scale[W3][:, cols],
+                    m = per_bank * k + a
+                    nc.tensor.matmul_mx(out=acc[:, a, :], lhsT=w3_word[m // 2][:, m % 2 * P : (m % 2 + 1) * P].bitcast(FP8X4), lhsT_scale=w_scale[W3][:, m * P : (m + 1) * P],
                                         rhs=z_word[:, j0 : j0 + HALF].bitcast(FP8X4), rhs_scale=z_scale[:, j0 : j0 + HALF], start=True, stop=True)
                 out_acc[j0].append(acc)
 
@@ -234,15 +235,12 @@ def tile_picked_nlmean_none_p_kernel(tc, x_words, x_scales, w1, w2, w3, offs, p1
             nc.sync.dma_start(w3_raw[:, 2 * u : 2 * u + 2, :].rearrange("p e c -> p (e c)"),
                               w3.rearrange("(blk u r e) c -> u blk r (e c)", u=2, r=8, e=2)[u])
 
-        def cast_w3(k, tag):
-            half = keep.tile([P, N // 2 * PACK], BF16, name=f"w3_bf16_{k}", tag=tag, align_bytes=64)
-            nc.scalar.copy(half[:].rearrange("p (c i s) -> p c s i", i=LINE, s=PACK),
-                           w3_raw[:, :, k * N // 2 : (k + 1) * N // 2].rearrange("p s (c i) -> p c s i", i=LINE))
-            return half
+        def w3_half_tile(k, tag):
+            return keep.tile([P, N // 2 * PACK], BF16, name=f"w3_bf16_{k}", tag=tag, align_bytes=64)
 
-        def quantise_w3(k, half):
-            cols = slice(k * N // 2, (k + 1) * N // 2)
-            nc.vector.quantize_mx(out=w_word[W3][:, cols].bitcast(FP8X4), scales=w_scale[W3][:, cols], in_=half[:])
+        def quantise_w3(k, half, tag):
+            w3_word[k] = keep.tile([P, N // 2], U32, name=f"w3_word{k}", tag=tag, align_bytes=64)
+            nc.vector.quantize_mx(out=w3_word[k][:].bitcast(FP8X4), scales=w_scale[W3][:, k * N // 2 : (k + 1) * N // 2], in_=half[:])
 
         make_square(0, 0)
         make_square(0, 1)
@@ -253,6 +251,8 @@ def tile_picked_nlmean_none_p_kernel(tc, x_words, x_scales, w1, w2, w3, offs, p1
                 make_diff(t, n, 0, S)
         for t in range(1, TILES):
             make_val(t - 1)
+            if t == TILES - 1:
+                make_terms(0, 0, BLOCKS)
             make_square(t, 0)
             make_square(t, 1)
             make_e(t, 0)
@@ -260,19 +260,20 @@ def tile_picked_nlmean_none_p_kernel(tc, x_words, x_scales, w1, w2, w3, offs, p1
                 square_den(t - 1)
             make_e(t, 1)
         square_den(TILES - 2)
-        make_terms(0, 0, BLOCKS)
         make_terms(1, 0, BLOCKS)
         make_val(TILES - 1)
         make_terms(2, 0, BLOCKS)
         make_terms(TILES - 1, 0, 2)
         make_terms(TILES - 1, 2, 4)
-        w3_first = cast_w3(0, "w3_bf16_0")
+        w3_first = w3_half_tile(0, "w3_bf16_0")
+        nc.scalar.copy(w3_first[:].rearrange("p (c i s) -> p c s i", i=LINE, s=PACK), w3_raw[:, :, : N // 2].rearrange("p s (c i) -> p c s i", i=LINE))
         square_den(TILES - 1)
 
         sc, vc = nc.scalar.copy, nc.vector.tensor_copy
         for b in range(BLOCKS):
             make_inv(b)
-        w3_second = cast_w3(1, "den_sq0")
+        w3_second = w3_half_tile(1, f"e{TILES - 1}_1")
+        nc.gpsimd.tensor_scalar(w3_second[:].rearrange("p (c s) -> p c s", s=PACK), w3_raw[:, :, N // 2 :].rearrange("p s c -> p c s"), 1.0, 0.0, ALU.mult, ALU.add)
         make_z(0, 1)
         make_z(1, 1)
         interleave_z(0)
@@ -281,12 +282,13 @@ def tile_picked_nlmean_none_p_kernel(tc, x_words, x_scales, w1, w2, w3, offs, p1
         make_z(3, 2)
         interleave_z(2)
         interleave_z(3)
-        quantise_w3(0, w3_first)
+        quantise_w3(0, w3_first, "w3_word0")
         quantise_z(0)
-        quantise_w3(1, w3_second)
-        for b in range(1, BLOCKS):
-            quantise_z(b)
+        quantise_z(1)
+        quantise_w3(1, w3_second, "inv2")
+        quantise_z(2)
+        quantise_z(3)
         multiply_out(0, ["num0", "num1", "num2", "num3"])
         multiply_out(HALF, ["den", "den", "acc", "acc"])
-        store_out(0, [sc, vc, sc, vc])
+        store_out(0, [sc, sc, sc, sc])
         store_out(HALF, [sc, vc, sc, vc])

@@ -90,7 +90,7 @@ def tile_picked_nlmean_none_p_kernel(tc, x_words, x_scales, w1, w2, w3, offs, p1
         for t in range(TILES):
             cast_tile_columns(W1, nc.scalar.copy, t, 0)
         for t in range(TILES):
-            cast_tile_columns(W1, nc.vector.tensor_copy if t in (0, TILES - 1) else nc.scalar.copy, t, 1)
+            cast_tile_columns(W1, nc.vector.tensor_copy if t == 0 else nc.scalar.copy, t, 1)
         quantise_weights(W1, 0, 1)
         quantise_weights(W1, 1, 2)
         quantise_weights(W1, 2, TILES)

@@ -43,7 +43,7 @@ def tile_picked_nlmean_none_p_kernel(tc, x_words, x_scales, w1, w2, w3, offs, p1
         x_scale_all = keep.tile([P, T], U8, name="x_scale_all", align_bytes=64)
         nc.vector.memset(x_scale_all[:].bitcast(I32), 0)
         x_word_all = keep.tile([P, T], U32, name="x_word_all", align_bytes=64)
-        w_raw = [[keep.tile([P, PACK, H // 2], F32, name=f"w_raw{w}_{h}", tag=f"w_raw{w}_{h}") for h in range(2)] for w in (W1, W2)]
+        w_raw = [[keep.tile([P, PACK, H // 2], F32, name=f"w_raw{w}_{h}", tag=f"w_raw{w}_{h}", align_bytes=64) for h in range(2)] for w in (W1, W2)]
 
         def load_half(w, src, h):
             nc.sync.dma_start(w_raw[w][h][:], src.rearrange("(p s) c -> p s c", s=PACK)[:, :, h * H // 2 : (h + 1) * H // 2])
@@ -103,11 +103,14 @@ def tile_picked_nlmean_none_p_kernel(tc, x_words, x_scales, w1, w2, w3, offs, p1
             return acc[:, : j1 - j0]
 
         def make_c(t, bank, bufs):
-            nc.scalar.copy(c_win[t][:, :S], product_with_x(W1, t, 0, S, bank, bufs))
-            if t > 1:
+            acc = product_with_x(W1, t, 0, S, bank, bufs)
+            nc.scalar.copy(c_win[t][:, :S], acc)
+            if t == 1:
+                nc.scalar.copy(c_own[t], acc)
+            else:
                 nc.sync.dma_start(c_own[t], c_win[t][:, :S])
 
-        diff = [[keep.tile([P, S], F32, name=f"diff{t}_{n}", tag=f"diff{t}_{n}", align_bytes=64)[:] for n in range(2)] if t != 1 else None for t in range(TILES)]
+        diff = [[keep.tile([P, S], F32, name=f"diff{t}_{n}", tag=f"diff{t}_{n}", align_bytes=64)[:] for n in range(2)] if t != 2 else None for t in range(TILES)]
         square = [[keep.tile([P, S], F32, name=f"square{t}_{n}", tag=f"square{t}_{n}", align_bytes=64) for n in range(2)] for t in range(TILES)]
         e = [[keep.tile([P, S], F32, name=f"e{t}_{n}", tag=f"e{t}_{n}", align_bytes=64) for n in range(2)] for t in range(TILES)]
 
@@ -156,7 +159,7 @@ def tile_picked_nlmean_none_p_kernel(tc, x_words, x_scales, w1, w2, w3, offs, p1
         def make_terms(t, b0, b1):
             j0, j1 = b0 * P, b1 * P
             for n in range(2):
-                held = [("diff2_1", "square2_0"), ("square2_1", "diff3_0"), ("square3_0", "square3_1")]
+                held = [("w_raw1_1", "w_bf16_1"), ("square2_0", "square2_1"), ("diff3_1", "square3_0")]
                 term = keep.tile([P, j1 - j0], F32, name=f"term{t}_{b0}_{n}", tag=held[t][n] if t < TILES - 1 else f"term{t}_{b0}_{n}", align_bytes=64)
                 nc.vector.tensor_tensor(term[:], val[t][:].indirect(entries(p_sb[n], j0, j1)), e[t][n][:, j0:j1], ALU.mult)
                 for b in range(b0, b1):
@@ -197,7 +200,7 @@ def tile_picked_nlmean_none_p_kernel(tc, x_words, x_scales, w1, w2, w3, offs, p1
                 acc = psum.tile([P, per_bank, HALF], F32, name="out_acc", tag=bank, bufs=2 if bank in ("den", "acc") else 1)
                 for a in range(per_bank):
                     m = per_bank * k + a
-                    nc.tensor.matmul_mx(out=acc[:, a, :], lhsT=w3_word[m // 2][:, m % 2 * P : (m % 2 + 1) * P].bitcast(FP8X4), lhsT_scale=w_scale[W3][:, m * P : (m + 1) * P],
+                    nc.tensor.matmul_mx(out=acc[:, a, :], lhsT=w3_word[m].bitcast(FP8X4), lhsT_scale=w_scale[W3][:, m * P : (m + 1) * P],
                                         rhs=z_word[:, j0 : j0 + HALF].bitcast(FP8X4), rhs_scale=z_scale[:, j0 : j0 + HALF], start=True, stop=True)
                 out_acc[j0].append(acc)
 
@@ -208,72 +211,71 @@ def tile_picked_nlmean_none_p_kernel(tc, x_words, x_scales, w1, w2, w3, offs, p1
                 copy(res[:], out_acc[j0][k][:])
                 nc.sync.dma_start(out.rearrange("(a p) j -> p a j", p=P)[:, per_bank * k : per_bank * (k + 1), j0 : j0 + HALF], res[:])
 
-        for j0 in range(0, S, HALF):
-            nc.scalar.copy(c_win[0][:, j0 : j0 + HALF], product_with_x(W1, 0, j0, j0 + HALF, "acc", 2))
+        halves = [product_with_x(W1, 0, j0, j0 + HALF, "acc", 2) for j0 in range(0, S, HALF)]
+        nc.scalar.copy(c_win[0][:, :HALF], halves[0])
+        nc.scalar.copy(c_win[0][:, HALF:S], halves[1])
+        nc.scalar.copy(c_own[0][:, HALF:], halves[1])
         nc.vector.tensor_copy(c_own[0][:, :HALF], c_win[0][:, :HALF])
         for t in range(TILES):
             cast_tile_columns(W2, nc.vector.tensor_copy, t, 0)
         make_diff(0, 0, 0, HALF)
-        nc.vector.tensor_copy(c_own[0][:, HALF:], c_win[0][:, HALF:S])
         make_diff(0, 1, 0, HALF)
         make_diff(0, 0, HALF, S)
         make_diff(0, 1, HALF, S)
         make_c(1, "den", 2)
-        nc.vector.tensor_copy(c_own[1], c_win[1][:, :S])
         make_c(2, "den", 2)
         make_c(3, "num0", 1)
+        make_diff(1, 0, 0, S)
+        make_diff(1, 1, 0, S)
         for t in range(TILES):
             cast_tile_columns(W2, nc.scalar.copy, t, 1)
         quantise_weights(W2, 0, TILES)
         multiply_val(0)
         multiply_val(1)
-        diff_pair = keep.tile([P, 2, S], F32, name="diff1", tag="w_raw1_1")
-        diff[1] = [diff_pair[:, n, :] for n in range(2)]
-
-        w3_raw = keep.tile([P, PACK, N], F32, name="w3_raw", tag="w_bf16_1", align_bytes=64)
-        for u in range(2):
-            nc.sync.dma_start(w3_raw[:, 2 * u : 2 * u + 2, :].rearrange("p e c -> p (e c)"),
-                              w3.rearrange("(blk u r e) c -> u blk r (e c)", u=2, r=8, e=2)[u])
-
-        def w3_half_tile(k, tag):
-            return keep.tile([P, N // 2 * PACK], BF16, name=f"w3_bf16_{k}", tag=tag, align_bytes=64)
-
-        def quantise_w3(k, half, tag):
-            w3_word[k] = keep.tile([P, N // 2], U32, name=f"w3_word{k}", tag=tag, align_bytes=64)
-            nc.vector.quantize_mx(out=w3_word[k][:].bitcast(FP8X4), scales=w_scale[W3][:, k * N // 2 : (k + 1) * N // 2], in_=half[:])
-
+        diff[2] = [keep.tile([P, S], F32, name="diff2_0", tag="w_raw1_1", align_bytes=64)[:], keep.tile([P, S], F32, name="diff2_1", tag="w_bf16_1", align_bytes=64)[:]]
         make_square(0, 0)
         make_square(0, 1)
         make_e(0, 0)
         make_e(0, 1)
-        for t in range(1, TILES):
+
+        w3_raw = keep.tile([P, PACK, N], F32, name="w3_raw", tag="square0_0", align_bytes=64)
+        for u in range(2):
+            nc.sync.dma_start(w3_raw[:, 2 * u : 2 * u + 2, :].rearrange("p e c -> p (e c)"),
+                              w3.rearrange("(blk u r e) c -> u blk r (e c)", u=2, r=8, e=2)[u])
+
+        def quantise_w3(words, values, m0, m1, base):
+            nc.vector.quantize_mx(out=words[:, (m0 - base) * P : (m1 - base) * P].bitcast(FP8X4), scales=w_scale[W3][:, m0 * P : m1 * P],
+                                  in_=values[:, (m0 - base) * P * PACK : (m1 - base) * P * PACK])
+            for m in range(m0, m1):
+                w3_word[m] = words[:, (m - base) * P : (m - base + 1) * P]
+
+        for t in range(2, TILES):
             for n in range(2):
                 make_diff(t, n, 0, S)
         for t in range(1, TILES):
-            make_val(t - 1)
-            if t == TILES - 1:
-                make_terms(0, 0, BLOCKS)
             make_square(t, 0)
             make_square(t, 1)
             make_e(t, 0)
-            if t < TILES - 1:
-                square_den(t - 1)
             make_e(t, 1)
-        square_den(TILES - 2)
-        make_terms(1, 0, BLOCKS)
-        make_val(TILES - 1)
+            make_val(t - 1)
+            if t > 1:
+                make_terms(t - 2, 0, BLOCKS)
+            square_den(t - 1)
+        make_val(3)
         make_terms(2, 0, BLOCKS)
         make_terms(TILES - 1, 0, 2)
         make_terms(TILES - 1, 2, 4)
-        w3_first = w3_half_tile(0, "w3_bf16_0")
-        nc.scalar.copy(w3_first[:].rearrange("p (c i s) -> p c s i", i=LINE, s=PACK), w3_raw[:, :, : N // 2].rearrange("p s (c i) -> p c s i", i=LINE))
+        w3_first = keep.tile([P, P * PACK], BF16, name="w3_first", align_bytes=64)
+        nc.scalar.copy(w3_first[:].rearrange("p (c i s) -> p c s i", i=LINE, s=PACK), w3_raw[:, :, :P].rearrange("p s (c i) -> p c s i", i=LINE))
         square_den(TILES - 1)
 
         sc, vc = nc.scalar.copy, nc.vector.tensor_copy
         for b in range(BLOCKS):
             make_inv(b)
-        w3_second = w3_half_tile(1, f"e{TILES - 1}_1")
-        nc.gpsimd.tensor_scalar(w3_second[:].rearrange("p (c s) -> p c s", s=PACK), w3_raw[:, :, N // 2 :].rearrange("p s c -> p c s"), 1.0, 0.0, ALU.mult, ALU.add)
+        w3_rest = keep.tile([P, (N - P) * PACK], BF16, name="w3_rest", tag=f"e{TILES - 1}_1", align_bytes=64)
+        for m0, m1 in ((1, 2), (2, TILES)):
+            nc.gpsimd.tensor_scalar(w3_rest[:, (m0 - 1) * P * PACK : (m1 - 1) * P * PACK].rearrange("p (c s) -> p c s", s=PACK),
+                                    w3_raw[:, :, m0 * P : m1 * P].rearrange("p s c -> p c s"), 1.0, 0.0, ALU.mult, ALU.add)
         make_z(0, 1)
         make_z(1, 1)
         interleave_z(0)
@@ -282,10 +284,12 @@ def tile_picked_nlmean_none_p_kernel(tc, x_words, x_scales, w1, w2, w3, offs, p1
         make_z(3, 2)
         interleave_z(2)
         interleave_z(3)
-        quantise_w3(0, w3_first, "w3_word0")
+        quantise_w3(keep.tile([P, P], U32, name="w3_word_first", align_bytes=64), w3_first, 0, 1, 0)
         quantise_z(0)
         quantise_z(1)
-        quantise_w3(1, w3_second, "inv2")
+        rest_words = keep.tile([P, N - P], U32, name="w3_word_rest", tag="inv2", align_bytes=64)
+        quantise_w3(rest_words, w3_rest, 1, 2, 1)
+        quantise_w3(rest_words, w3_rest, 2, TILES, 1)
         quantise_z(2)
         quantise_z(3)
         multiply_out(0, ["num0", "num1", "num2", "num3"])

@@ -110,7 +110,7 @@ def tile_picked_nlmean_none_p_kernel(tc, x_words, x_scales, w1, w2, w3, offs, p1
             else:
                 nc.sync.dma_start(c_own[t], c_win[t][:, :S])
 
-        diff = [[keep.tile([P, S], F32, name=f"diff{t}_{n}", tag=f"diff{t}_{n}", align_bytes=64)[:] for n in range(2)] if t != 2 else None for t in range(TILES)]
+        diff = [[keep.tile([P, S], F32, name=f"diff{t}_{n}", tag=f"diff{t}_{n}", align_bytes=64)[:] for n in range(2)] if t != 1 else None for t in range(TILES)]
         square = [[keep.tile([P, S], F32, name=f"square{t}_{n}", tag=f"square{t}_{n}", align_bytes=64) for n in range(2)] for t in range(TILES)]
         e = [[keep.tile([P, S], F32, name=f"e{t}_{n}", tag=f"e{t}_{n}", align_bytes=64) for n in range(2)] for t in range(TILES)]
 
@@ -159,7 +159,7 @@ def tile_picked_nlmean_none_p_kernel(tc, x_words, x_scales, w1, w2, w3, offs, p1
         def make_terms(t, b0, b1):
             j0, j1 = b0 * P, b1 * P
             for n in range(2):
-                held = [("w_raw1_1", "w_bf16_1"), ("square2_0", "square2_1"), ("diff3_1", "square3_0")]
+                held = [("diff2_0", "diff2_1"), ("square2_0", "square2_1"), ("diff3_1", "square3_0")]
                 term = keep.tile([P, j1 - j0], F32, name=f"term{t}_{b0}_{n}", tag=held[t][n] if t < TILES - 1 else f"term{t}_{b0}_{n}", align_bytes=64)
                 nc.vector.tensor_tensor(term[:], val[t][:].indirect(entries(p_sb[n], j0, j1)), e[t][n][:, j0:j1], ALU.mult)
                 for b in range(b0, b1):
@@ -225,14 +225,15 @@ def tile_picked_nlmean_none_p_kernel(tc, x_words, x_scales, w1, w2, w3, offs, p1
         make_c(1, "den", 2)
         make_c(2, "den", 2)
         make_c(3, "num0", 1)
+        diff[1] = [keep.tile([P, S], F32, name="diff1_0")[:]]
         make_diff(1, 0, 0, S)
-        make_diff(1, 1, 0, S)
         for t in range(TILES):
             cast_tile_columns(W2, nc.scalar.copy, t, 1)
         quantise_weights(W2, 0, TILES)
         multiply_val(0)
         multiply_val(1)
-        diff[2] = [keep.tile([P, S], F32, name="diff2_0", tag="w_raw1_1", align_bytes=64)[:], keep.tile([P, S], F32, name="diff2_1", tag="w_bf16_1", align_bytes=64)[:]]
+        diff[1].append(keep.tile([P, S], F32, name="diff1_1", tag="w_raw1_1", align_bytes=64)[:])
+        make_diff(1, 1, 0, S)
         make_square(0, 0)
         make_square(0, 1)
         make_e(0, 0)
@@ -253,15 +254,18 @@ def tile_picked_nlmean_none_p_kernel(tc, x_words, x_scales, w1, w2, w3, offs, p1
             for n in range(2):
                 make_diff(t, n, 0, S)
         for t in range(1, TILES):
+            make_val(t - 1)
+            if t == TILES - 1:
+                make_terms(0, 0, BLOCKS)
             make_square(t, 0)
             make_square(t, 1)
             make_e(t, 0)
+            if t < TILES - 1:
+                square_den(t - 1)
             make_e(t, 1)
-            make_val(t - 1)
-            if t > 1:
-                make_terms(t - 2, 0, BLOCKS)
-            square_den(t - 1)
-        make_val(3)
+        square_den(TILES - 2)
+        make_val(TILES - 1)
+        make_terms(1, 0, BLOCKS)
         make_terms(2, 0, BLOCKS)
         make_terms(TILES - 1, 0, 2)
         make_terms(TILES - 1, 2, 4)

@@ -105,10 +105,9 @@ def tile_picked_nlmean_none_p_kernel(tc, x_words, x_scales, w1, w2, w3, offs, p1
         def make_c(t, bank, bufs):
             acc = product_with_x(W1, t, 0, S, bank, bufs)
             nc.scalar.copy(c_win[t][:, :S], acc)
-            if t == 1:
-                nc.scalar.copy(c_own[t], acc)
-            else:
+            if t > 1:
                 nc.sync.dma_start(c_own[t], c_win[t][:, :S])
+            return acc
 
         diff = [[keep.tile([P, S], F32, name=f"diff{t}_{n}", tag=f"diff{t}_{n}", align_bytes=64)[:] for n in range(2)] if t != 1 else None for t in range(TILES)]
         square = [[keep.tile([P, S], F32, name=f"square{t}_{n}", tag=f"square{t}_{n}", align_bytes=64) for n in range(2)] for t in range(TILES)]
@@ -222,8 +221,9 @@ def tile_picked_nlmean_none_p_kernel(tc, x_words, x_scales, w1, w2, w3, offs, p1
         make_diff(0, 1, 0, HALF)
         make_diff(0, 0, HALF, S)
         make_diff(0, 1, HALF, S)
-        make_c(1, "den", 2)
+        c1_acc = make_c(1, "den", 2)
         make_c(2, "den", 2)
+        nc.scalar.copy(c_own[1], c1_acc)
         make_c(3, "num0", 1)
         diff[1] = [keep.tile([P, S], F32, name="diff1_0")[:]]
         make_diff(1, 0, 0, S)
@@ -276,24 +276,23 @@ def tile_picked_nlmean_none_p_kernel(tc, x_words, x_scales, w1, w2, w3, offs, p1
         sc, vc = nc.scalar.copy, nc.vector.tensor_copy
         for b in range(BLOCKS):
             make_inv(b)
-        w3_rest = keep.tile([P, (N - P) * PACK], BF16, name="w3_rest", tag=f"e{TILES - 1}_1", align_bytes=64)
-        for m0, m1 in ((1, 2), (2, TILES)):
-            nc.gpsimd.tensor_scalar(w3_rest[:, (m0 - 1) * P * PACK : (m1 - 1) * P * PACK].rearrange("p (c s) -> p c s", s=PACK),
-                                    w3_raw[:, :, m0 * P : m1 * P].rearrange("p s c -> p c s"), 1.0, 0.0, ALU.mult, ALU.add)
+        w3_rest = keep.tile([P, N // 2 * PACK], BF16, name="w3_rest", tag=f"e{TILES - 1}_1", align_bytes=64)
+        nc.gpsimd.tensor_scalar(w3_rest[:].rearrange("p (c s) -> p c s", s=PACK), w3_raw[:, :, P : N - P].rearrange("p s c -> p c s"), 1.0, 0.0, ALU.mult, ALU.add)
         make_z(0, 1)
         make_z(1, 1)
         interleave_z(0)
         make_z(2, 1)
         interleave_z(1)
+        w3_last = keep.tile([P, P * PACK], BF16, name="w3_last", tag="z_rows1", align_bytes=64)
+        nc.scalar.copy(w3_last[:].rearrange("p (c i s) -> p c s i", i=LINE, s=PACK), w3_raw[:, :, N - P :].rearrange("p s (c i) -> p c s i", i=LINE))
         make_z(3, 2)
         interleave_z(2)
         interleave_z(3)
         quantise_w3(keep.tile([P, P], U32, name="w3_word_first", align_bytes=64), w3_first, 0, 1, 0)
         quantise_z(0)
         quantise_z(1)
-        rest_words = keep.tile([P, N - P], U32, name="w3_word_rest", tag="inv2", align_bytes=64)
-        quantise_w3(rest_words, w3_rest, 1, 2, 1)
-        quantise_w3(rest_words, w3_rest, 2, TILES, 1)
+        quantise_w3(keep.tile([P, N // 2], U32, name="w3_word_rest", tag="inv2", align_bytes=64), w3_rest, 1, TILES - 1, 1)
+        quantise_w3(keep.tile([P, P], U32, name="w3_word_last", align_bytes=64), w3_last, TILES - 1, TILES, TILES - 1)
         quantise_z(2)
         quantise_z(3)
         multiply_out(0, ["num0", "num1", "num2", "num3"])

@@ -129,12 +129,11 @@ def tile_picked_nlmean_none_p_kernel(tc, x_words, x_scales, w1, w2, w3, offs, p1
                 cols = slice(b * P, (b + 1) * P)
                 nc.tensor.matmul(den[t][:, cols], e[t][n][:, cols], ident[:], start=(n == 0 and b == 0), stop=(n == 1 and b == BLOCKS - 1), is_transpose=True)
 
-        den_sq = [keep.tile([P, BLOCKS // 2, H], F32, name=f"den_sq{k}", tag=f"den_sq{k}", align_bytes=64) for k in range(2)]
+        den_sq = keep.tile([P, BLOCKS, H], F32, name="den_sq")
 
         def square_den(t):
-            for k in range(2):
-                nc.scalar.activation(den_sq[k][:].rearrange("j b (u g h q) -> j u h b g q", u=2, g=HEADS, h=2)[:, t // 2, t % 2],
-                                     den[t][:, k * HALF : (k + 1) * HALF].rearrange("j (b g q) -> j b g q", b=BLOCKS // 2, g=HEADS), ACT.Square, bias=1.0)
+            nc.scalar.activation(den_sq[:].rearrange("j b (u g h q) -> j u h b g q", u=2, g=HEADS, h=2)[:, t // 2, t % 2],
+                                 den[t][:].rearrange("j (b g q) -> j b g q", b=BLOCKS, g=HEADS), ACT.Square, bias=1.0)
 
         num = {}
 
@@ -158,7 +157,7 @@ def tile_picked_nlmean_none_p_kernel(tc, x_words, x_scales, w1, w2, w3, offs, p1
         def make_terms(t, b0, b1):
             j0, j1 = b0 * P, b1 * P
             for n in range(2):
-                held = [("diff2_0", "diff2_1"), ("square2_0", "square2_1"), ("diff3_1", "square3_0")]
+                held = [("w_raw1_1", "diff2_0"), ("diff2_1", "square2_0"), ("square2_1", "diff3_1")]
                 term = keep.tile([P, j1 - j0], F32, name=f"term{t}_{b0}_{n}", tag=held[t][n] if t < TILES - 1 else f"term{t}_{b0}_{n}", align_bytes=64)
                 nc.vector.tensor_tensor(term[:], val[t][:].indirect(entries(p_sb[n], j0, j1)), e[t][n][:, j0:j1], ALU.mult)
                 for b in range(b0, b1):
@@ -167,7 +166,7 @@ def tile_picked_nlmean_none_p_kernel(tc, x_words, x_scales, w1, w2, w3, offs, p1
         inv = [keep.tile([P, H], F32, name=f"inv{b}", tag=f"inv{b}", align_bytes=64) for b in range(BLOCKS)]
 
         def make_inv(b):
-            nc.scalar.activation(inv[b][:], den_sq[b // 2][:, b % 2, :], ACT.Abs_reciprocal_sqrt)
+            nc.scalar.activation(inv[b][:], den_sq[:, b, :], ACT.Abs_reciprocal_sqrt)
 
         z_word = keep.tile([P, S], U32, name="z_word", align_bytes=64)
         z_scale = keep.tile([P, S], U8, name="z_scale", align_bytes=64)
@@ -224,11 +223,11 @@ def tile_picked_nlmean_none_p_kernel(tc, x_words, x_scales, w1, w2, w3, offs, p1
         c1_acc = make_c(1, "den", 2)
         make_c(2, "den", 2)
         nc.scalar.copy(c_own[1], c1_acc)
-        make_c(3, "num0", 1)
         diff[1] = [keep.tile([P, S], F32, name="diff1_0")[:]]
         make_diff(1, 0, 0, S)
         for t in range(TILES):
             cast_tile_columns(W2, nc.scalar.copy, t, 1)
+        make_c(3, "num0", 1)
         quantise_weights(W2, 0, TILES)
         multiply_val(0)
         multiply_val(1)

@@ -43,21 +43,18 @@ def tile_picked_nlmean_none_p_kernel(tc, x_words, x_scales, w1, w2, w3, offs, p1
         x_scale_all = keep.tile([P, T], U8, name="x_scale_all", align_bytes=64)
         nc.vector.memset(x_scale_all[:].bitcast(I32), 0)
         x_word_all = keep.tile([P, T], U32, name="x_word_all", align_bytes=64)
-        w_raw = [[keep.tile([P, PACK, H // 2], F32, name=f"w_raw{w}_{h}", tag=f"w_raw{w}_{h}", align_bytes=64) for h in range(2)] for w in (W1, W2)]
-
-        def load_half(w, src, h):
-            nc.sync.dma_start(w_raw[w][h][:], src.rearrange("(p s) c -> p s c", s=PACK)[:, :, h * H // 2 : (h + 1) * H // 2])
+        w1_raw = keep.tile([P, PACK, H], F32, name="w1_raw")
+        w2_raw = [keep.tile([P, PACK, H // 2], F32, name=f"w2_raw{h}", tag=f"w_raw1_{h}", align_bytes=64) for h in range(2)]
 
         nc.sync.dma_start(x_word_all[:].bitcast(I32), x_words[0].rearrange("p n s -> p (n s)").bitcast(I32))
         nc.sync.dma_start(offs_sb[:], offs)
         for r in range(4):
             nc.sync.dma_start(x_scale_all[r::32, :].bitcast(I32), x_scales[0, r::4, :].bitcast(I32))
-        load_half(W1, w1, 0)
-        load_half(W1, w1, 1)
+        nc.sync.dma_start(w1_raw[:], w1.rearrange("(p s) c -> p s c", s=PACK))
         nc.sync.dma_start(p_sb[0][:], p1)
         nc.sync.dma_start(p_sb[1][:], p2)
-        load_half(W2, w2, 0)
-        load_half(W2, w2, 1)
+        for h in range(2):
+            nc.sync.dma_start(w2_raw[h][:], w2.rearrange("(p s) c -> p s c", s=PACK)[:, :, h * H // 2 : (h + 1) * H // 2])
 
         ident = keep.tile([P, P], F32, name="ident")
         make_identity(nc, ident[:])
@@ -73,10 +70,9 @@ def tile_picked_nlmean_none_p_kernel(tc, x_words, x_scales, w1, w2, w3, offs, p1
         w_word = [keep.tile([P, H], U32, name=f"w_word{w}", align_bytes=64) for w in (W1, W2)]
         w_scale = [keep.tile([P, H], U8, name=f"w_scale{w}", align_bytes=64) for w in (W1, W2, W3)]
 
-        def cast_tile_columns(w, copy, t, half):
-            g0 = half * HEADS // 2
-            copy(w_bf16[w][:].rearrange("p (t g c i s) -> p t g c s i", t=TILES, g=HEADS, i=LINE, s=PACK)[:, t, g0 : g0 + HEADS // 2],
-                 w_raw[w][half][:].rearrange("p s (g h u c i) -> p u h g c s i", g=HEADS // 2, h=2, u=2, i=LINE)[:, t // 2, t % 2])
+        def cast_tile_columns(w, copy, t, src, g0, g1):
+            copy(w_bf16[w][:].rearrange("p (t g c i s) -> p t g c s i", t=TILES, g=HEADS, i=LINE, s=PACK)[:, t, g0:g1],
+                 src[:].rearrange("p s (g h u c i) -> p u h g c s i", g=g1 - g0, h=2, u=2, i=LINE)[:, t // 2, t % 2])
 
         def quantise_weights(w, t0, t1):
             nc.vector.quantize_mx(out=w_word[w][:, t0 * P : t1 * P].bitcast(FP8X4), scales=w_scale[w][:, t0 * P : t1 * P],
@@ -88,12 +84,9 @@ def tile_picked_nlmean_none_p_kernel(tc, x_words, x_scales, w1, w2, w3, offs, p1
         nc.vector.tensor_copy(x_scale[:], x_scale_all[:].indirect(offs_sb[:]))
 
         for t in range(TILES):
-            cast_tile_columns(W1, nc.scalar.copy, t, 0)
+            cast_tile_columns(W1, nc.vector.tensor_copy if t % 2 == 0 else nc.scalar.copy, t, w1_raw, 0, HEADS)
         for t in range(TILES):
-            cast_tile_columns(W1, nc.vector.tensor_copy if t == 0 else nc.scalar.copy, t, 1)
-        quantise_weights(W1, 0, 1)
-        quantise_weights(W1, 1, 2)
-        quantise_weights(W1, 2, TILES)
+            quantise_weights(W1, t, t + 1)
 
         def product_with_x(w, t, j0, j1, bank, bufs):
             acc = psum.tile([P, S], F32, name="acc", tag=bank, bufs=bufs)
@@ -215,7 +208,7 @@ def tile_picked_nlmean_none_p_kernel(tc, x_words, x_scales, w1, w2, w3, offs, p1
         nc.scalar.copy(c_own[0][:, HALF:], halves[1])
         nc.vector.tensor_copy(c_own[0][:, :HALF], c_win[0][:, :HALF])
         for t in range(TILES):
-            cast_tile_columns(W2, nc.vector.tensor_copy, t, 0)
+            cast_tile_columns(W2, nc.vector.tensor_copy, t, w2_raw[0], 0, HEADS // 2)
         make_diff(0, 0, 0, HALF)
         make_diff(0, 1, 0, HALF)
         make_diff(0, 0, HALF, S)
@@ -226,7 +219,7 @@ def tile_picked_nlmean_none_p_kernel(tc, x_words, x_scales, w1, w2, w3, offs, p1
         diff[1] = [keep.tile([P, S], F32, name="diff1_0")[:]]
         make_diff(1, 0, 0, S)
         for t in range(TILES):
-            cast_tile_columns(W2, nc.scalar.copy, t, 1)
+            cast_tile_columns(W2, nc.scalar.copy, t, w2_raw[1], HEADS // 2, HEADS)
         make_c(3, "num0", 1)
         quantise_weights(W2, 0, TILES)
         multiply_val(0)

@@ -52,9 +52,10 @@ def tile_picked_nlmean_none_p_kernel(tc, x_words, x_scales, w1, w2, w3, offs, p1
             nc.sync.dma_start(x_scale_all[r::32, :].bitcast(I32), x_scales[0, r::4, :].bitcast(I32))
         nc.sync.dma_start(w1_raw[:], w1.rearrange("(p s) c -> p s c", s=PACK))
         nc.sync.dma_start(p_sb[0][:], p1)
+        w2_rows = w2.rearrange("(p s) c -> p s c", s=PACK)
+        nc.sync.dma_start(w2_raw[0][:], w2_rows[:, :, : H // 2])
         nc.sync.dma_start(p_sb[1][:], p2)
-        for h in range(2):
-            nc.sync.dma_start(w2_raw[h][:], w2.rearrange("(p s) c -> p s c", s=PACK)[:, :, h * H // 2 : (h + 1) * H // 2])
+        nc.sync.dma_start(w2_raw[1][:], w2_rows[:, :, H // 2 :])
 
         ident = keep.tile([P, P], F32, name="ident")
         make_identity(nc, ident[:])
@@ -210,9 +211,8 @@ def tile_picked_nlmean_none_p_kernel(tc, x_words, x_scales, w1, w2, w3, offs, p1
         for t in range(TILES):
             cast_tile_columns(W2, nc.vector.tensor_copy, t, w2_raw[0], 0, HEADS // 2)
         make_diff(0, 0, 0, HALF)
-        make_diff(0, 1, 0, HALF)
         make_diff(0, 0, HALF, S)
-        make_diff(0, 1, HALF, S)
+        make_diff(0, 1, 0, S)
         c1_acc = make_c(1, "den", 2)
         make_c(2, "den", 2)
         nc.scalar.copy(c_own[1], c1_acc)

@@ -44,7 +44,7 @@ def tile_picked_nlmean_none_p_kernel(tc, x_words, x_scales, w1, w2, w3, offs, p1
         nc.vector.memset(x_scale_all[:].bitcast(I32), 0)
         x_word_all = keep.tile([P, T], U32, name="x_word_all", align_bytes=64)
         w1_raw = keep.tile([P, PACK, H], F32, name="w1_raw")
-        w2_raw = [keep.tile([P, PACK, H // 2], F32, name=f"w2_raw{h}", tag=f"w_raw1_{h}", align_bytes=64) for h in range(2)]
+        w2_raw = [keep.tile([P, PACK, H // 2], F32, name=f"w2_raw{h}", tag=f"w2_raw{h}", align_bytes=64) for h in range(2)]
 
         nc.sync.dma_start(x_word_all[:].bitcast(I32), x_words[0].rearrange("p n s -> p (n s)").bitcast(I32))
         nc.sync.dma_start(offs_sb[:], offs)
@@ -64,8 +64,7 @@ def tile_picked_nlmean_none_p_kernel(tc, x_words, x_scales, w1, w2, w3, offs, p1
         for t in range(TILES):
             nc.vector.memset(c_win[t][:, S:], 0.0)
         val = [keep.tile([P, 2 * S if t < TILES - 1 else S], F32, name=f"val{t}") for t in range(TILES)]
-        c_own_last = keep.tile([P, S], F32, name="c_own_last")
-        c_own = [val[t][:, S:] for t in range(TILES - 1)] + [c_own_last[:]]
+        c_own = {t: val[t - 1][:, S:] for t in range(1, TILES)}
 
         w_bf16 = [keep.tile([P, H * PACK], BF16, name=f"w_bf16_{w}", tag=f"w_bf16_{w}", align_bytes=64) for w in (W1, W2)]
         w_word = [keep.tile([P, H], U32, name=f"w_word{w}", align_bytes=64) for w in (W1, W2)]
@@ -85,8 +84,8 @@ def tile_picked_nlmean_none_p_kernel(tc, x_words, x_scales, w1, w2, w3, offs, p1
         nc.vector.tensor_copy(x_scale[:], x_scale_all[:].indirect(offs_sb[:]))
 
         for t in range(TILES):
-            cast_tile_columns(W1, nc.vector.tensor_copy if t % 2 == 0 else nc.scalar.copy, t, w1_raw, 0, HEADS)
-        for t in range(TILES):
+            cast_tile_columns(W1, nc.vector.tensor_copy if t in (0, TILES - 1) else nc.scalar.copy, t, w1_raw, 0, HEADS)
+        for t in (0, 1, 3, 2):
             quantise_weights(W1, t, t + 1)
 
         def product_with_x(w, t, j0, j1, bank, bufs):
@@ -103,25 +102,52 @@ def tile_picked_nlmean_none_p_kernel(tc, x_words, x_scales, w1, w2, w3, offs, p1
                 nc.sync.dma_start(c_own[t], c_win[t][:, :S])
             return acc
 
-        diff = [[keep.tile([P, S], F32, name=f"diff{t}_{n}", tag=f"diff{t}_{n}", align_bytes=64)[:] for n in range(2)] if t != 1 else None for t in range(TILES)]
-        square = [[keep.tile([P, S], F32, name=f"square{t}_{n}", tag=f"square{t}_{n}", align_bytes=64) for n in range(2)] for t in range(TILES)]
+        diff, square = {}, {}
         e = [[keep.tile([P, S], F32, name=f"e{t}_{n}", tag=f"e{t}_{n}", align_bytes=64) for n in range(2)] for t in range(TILES)]
 
-        def make_diff(t, n, j0, j1):
-            nc.vector.tensor_tensor(diff[t][n][:, j0:j1], c_win[t][:].indirect(entries(p_sb[n], j0, j1)), c_own[t][:, j0:j1], ALU.subtract)
+        def make_diff(t, n, tag):
+            diff[t, n] = keep.tile([P, S], F32, name=f"diff{t}_{n}", tag=tag, align_bytes=64)
+            nc.vector.tensor_tensor(diff[t, n][:], c_win[t][:].indirect(p_sb[n][:]), c_own[t], ALU.subtract)
+
+        def block(b):
+            return slice(b * P, (b + 1) * P)
+
+        def fetch_negated(t, n, on_scalar=False):
+            diff[t, n] = keep.tile([P, S], F32, name=f"negated{t}_{n}", tag=f"diff{t}_{n}", align_bytes=64)
+            if on_scalar:
+                nc.scalar.activation(diff[t, n][:], c_win[t][:].indirect(p_sb[n][:]), ACT.Copy, scale=-1.0)
+            else:
+                nc.vector.tensor_scalar(diff[t, n][:], c_win[t][:].indirect(p_sb[n][:]), -1.0, 0.0, ALU.mult, ALU.add)
+
+        def turn_diff(t, n, bank):
+            negated = diff[t, n]
+            diff[t, n] = psum.tile([P, S], F32, name=f"turned{t}_{n}", tag=bank)
+            for b in range(BLOCKS):
+                nc.tensor.matmul(diff[t, n][:, block(b)], c_win[t][:, block(b)], ident[:], start=(b == 0), stop=False, is_transpose=True)
+            for b in range(BLOCKS):
+                nc.tensor.matmul(diff[t, n][:, block(b)], negated[:, block(b)], ident[:], start=False, stop=(b == BLOCKS - 1), is_transpose=True)
 
         def make_square(t, n):
-            nc.scalar.activation(square[t][n][:], diff[t][n], ACT.Square)
+            square[t, n] = keep.tile([P, S], F32, name=f"square{t}_{n}", tag=f"square{t}_{n}", align_bytes=64)
+            nc.scalar.activation(square[t, n][:], diff[t, n][:], ACT.Square)
+
+        def turn_square_back(t, n, bank, bufs):
+            turned = square[t, n]
+            square[t, n] = psum.tile([P, S], F32, name=f"square_back{t}_{n}", tag=bank, bufs=bufs)
+            for b in range(BLOCKS):
+                nc.tensor.transpose(square[t, n][:, block(b)], turned[:, block(b)], ident[:])
 
         den = {}
 
         def make_e(t, n):
-            nc.scalar.activation(e[t][n][:], square[t][n][:], ACT.Exp, scale=-0.5)
-            if n == 0:
+            nc.scalar.activation(e[t][n][:], square[t, n][:], ACT.Exp, scale=-0.5)
+
+        def add_to_den(t, n):
+            first = t not in den
+            if first:
                 den[t] = psum.tile([P, S], F32, name="den", tag="den", bufs=2)
             for b in range(BLOCKS):
-                cols = slice(b * P, (b + 1) * P)
-                nc.tensor.matmul(den[t][:, cols], e[t][n][:, cols], ident[:], start=(n == 0 and b == 0), stop=(n == 1 and b == BLOCKS - 1), is_transpose=True)
+                nc.tensor.matmul(den[t][:, block(b)], e[t][n][:, block(b)], ident[:], start=(first and b == 0), stop=(not first and b == BLOCKS - 1), is_transpose=True)
 
         den_sq = keep.tile([P, BLOCKS, H], F32, name="den_sq")
 
@@ -145,17 +171,17 @@ def tile_picked_nlmean_none_p_kernel(tc, x_words, x_scales, w1, w2, w3, offs, p1
             nc.scalar.copy(val[t][:, :S], val_acc[t])
             if t + 2 < TILES:
                 multiply_val(t + 2)
+
+        def add_val(t):
             for b in range(BLOCKS):
                 add_to_num(t, b, val[t][:, b * P : (b + 1) * P], first=(t == 0))
 
-        def make_terms(t, b0, b1):
+        def make_term(t, n, b0, b1, tag):
             j0, j1 = b0 * P, b1 * P
-            for n in range(2):
-                held = [("w_raw1_1", "diff2_0"), ("diff2_1", "square2_0"), ("square2_1", "diff3_1")]
-                term = keep.tile([P, j1 - j0], F32, name=f"term{t}_{b0}_{n}", tag=held[t][n] if t < TILES - 1 else f"term{t}_{b0}_{n}", align_bytes=64)
-                nc.vector.tensor_tensor(term[:], val[t][:].indirect(entries(p_sb[n], j0, j1)), e[t][n][:, j0:j1], ALU.mult)
-                for b in range(b0, b1):
-                    add_to_num(t, b, term[:, (b - b0) * P : (b - b0 + 1) * P], last=(t == TILES - 1 and n == 1))
+            term = keep.tile([P, j1 - j0], F32, name=f"term{t}_{b0}_{n}", tag=tag, align_bytes=64)
+            nc.vector.tensor_tensor(term[:], val[t][:].indirect(entries(p_sb[n], j0, j1)), e[t][n][:, j0:j1], ALU.mult)
+            for b in range(b0, b1):
+                add_to_num(t, b, term[:, block(b - b0)], last=(t == TILES - 1 and n == 0))
 
         inv = [keep.tile([P, H], F32, name=f"inv{b}", tag=f"inv{b}", align_bytes=64) for b in range(BLOCKS)]
 
@@ -206,29 +232,39 @@ def tile_picked_nlmean_none_p_kernel(tc, x_words, x_scales, w1, w2, w3, offs, p1
         halves = [product_with_x(W1, 0, j0, j0 + HALF, "acc", 2) for j0 in range(0, S, HALF)]
         nc.scalar.copy(c_win[0][:, :HALF], halves[0])
         nc.scalar.copy(c_win[0][:, HALF:S], halves[1])
-        nc.scalar.copy(c_own[0][:, HALF:], halves[1])
-        nc.vector.tensor_copy(c_own[0][:, :HALF], c_win[0][:, :HALF])
         for t in range(TILES):
             cast_tile_columns(W2, nc.vector.tensor_copy, t, w2_raw[0], 0, HEADS // 2)
-        make_diff(0, 0, 0, HALF)
-        make_diff(0, 0, HALF, S)
-        make_diff(0, 1, 0, S)
-        c1_acc = make_c(1, "den", 2)
-        make_c(2, "den", 2)
-        nc.scalar.copy(c_own[1], c1_acc)
-        diff[1] = [keep.tile([P, S], F32, name="diff1_0")[:]]
-        make_diff(1, 0, 0, S)
-        for t in range(TILES):
-            cast_tile_columns(W2, nc.scalar.copy, t, w2_raw[1], HEADS // 2, HEADS)
-        make_c(3, "num0", 1)
+        fetch_negated(0, 0)
+        fetch_negated(0, 1)
+        def cast_w2_on_gpsimd(u):
+            nc.gpsimd.tensor_scalar(w_bf16[W2][:].rearrange("p (u h g q s) -> p u g h q s", u=2, h=2, g=HEADS, s=PACK)[:, u, HEADS // 2 :],
+                                    w2_raw[1][:].rearrange("p s (g h u q) -> p u g h q s", g=HEADS // 2, h=2, u=2)[:, u], 1.0, 0.0, ALU.mult, ALU.add)
+
+        cast_w2_on_gpsimd(0)
+        cast_w2_on_gpsimd(1)
+        make_c(1, "den", 2)
+        nc.gpsimd.tensor_scalar(c_own[1], c_win[1][:, :S], 1.0, 0.0, ALU.mult, ALU.add)
+        make_c(3, "den", 2)
+        make_c(2, "num0", 1)
+        fetch_negated(3, 1, on_scalar=True)
         quantise_weights(W2, 0, TILES)
+        make_diff(1, 0, "diff1_0")
+        make_diff(1, 1, "diff1_1")
+        make_diff(2, 0, "diff2_0")
+        make_diff(2, 1, "diff2_1")
+        make_diff(3, 0, "diff3_0")
+        turn_diff(0, 0, "num1")
+        turn_diff(0, 1, "num2")
         multiply_val(0)
-        multiply_val(1)
-        diff[1].append(keep.tile([P, S], F32, name="diff1_1", tag="w_raw1_1", align_bytes=64)[:])
-        make_diff(1, 1, 0, S)
         make_square(0, 0)
+        turn_square_back(0, 0, "den", 2)
         make_square(0, 1)
+        turn_square_back(0, 1, "den", 2)
+        multiply_val(1)
+        turn_diff(3, 1, "num1")
+        make_val(0)
         make_e(0, 0)
+        make_square(1, 0)
         make_e(0, 1)
 
         w3_raw = keep.tile([P, PACK, N], F32, name="w3_raw", tag="square0_0", align_bytes=64)
@@ -242,34 +278,52 @@ def tile_picked_nlmean_none_p_kernel(tc, x_words, x_scales, w1, w2, w3, offs, p1
             for m in range(m0, m1):
                 w3_word[m] = words[:, (m - base) * P : (m - base + 1) * P]
 
-        for t in range(2, TILES):
-            for n in range(2):
-                make_diff(t, n, 0, S)
-        for t in range(1, TILES):
-            make_val(t - 1)
-            if t == TILES - 1:
-                make_terms(0, 0, BLOCKS)
-            make_square(t, 0)
-            make_square(t, 1)
-            make_e(t, 0)
-            if t < TILES - 1:
-                square_den(t - 1)
-            make_e(t, 1)
-        square_den(TILES - 2)
-        make_val(TILES - 1)
-        make_terms(1, 0, BLOCKS)
-        make_terms(2, 0, BLOCKS)
-        make_terms(TILES - 1, 0, 2)
-        make_terms(TILES - 1, 2, 4)
-        w3_first = keep.tile([P, P * PACK], BF16, name="w3_first", align_bytes=64)
-        nc.scalar.copy(w3_first[:].rearrange("p (c i s) -> p c s i", i=LINE, s=PACK), w3_raw[:, :, :P].rearrange("p s (c i) -> p c s i", i=LINE))
+        make_square(1, 1)
+        make_e(1, 0)
+        make_square(3, 1)
+        turn_square_back(3, 1, "num0", 1)
+        add_to_den(0, 0)
+        add_to_den(0, 1)
+        add_to_den(1, 0)
+        make_e(1, 1)
+        add_to_den(1, 1)
+        make_val(1)
+        make_square(2, 0)
+        make_e(3, 1)
+        add_val(0)
+        add_val(1)
+        square_den(0)
+        make_term(0, 0, 0, BLOCKS, "term0_0")
+        make_term(0, 1, 0, BLOCKS, "term0_1")
+        make_square(2, 1)
+        make_e(2, 0)
+        add_to_den(2, 0)
+        make_val(2)
+        add_val(2)
+        square_den(1)
+        add_to_den(3, 1)
+        make_term(1, 0, 0, BLOCKS, "term1_0")
+        make_square(3, 0)
+        make_e(2, 1)
+        add_to_den(2, 1)
+        make_e(3, 0)
+        add_to_den(3, 0)
+        make_val(3)
+        add_val(3)
+        make_term(1, 1, 0, BLOCKS, "term1_1")
+        make_term(2, 0, 0, BLOCKS, "term2_0")
+        make_term(2, 1, 0, BLOCKS, "term2_1")
+        square_den(2)
         square_den(TILES - 1)
+        for b0 in (0, 2):
+            for n in (1, 0):
+                make_term(TILES - 1, n, b0, b0 + 2, f"term3_{b0}_{n}")
 
         sc, vc = nc.scalar.copy, nc.vector.tensor_copy
         for b in range(BLOCKS):
             make_inv(b)
-        w3_rest = keep.tile([P, N // 2 * PACK], BF16, name="w3_rest", tag=f"e{TILES - 1}_1", align_bytes=64)
-        nc.gpsimd.tensor_scalar(w3_rest[:].rearrange("p (c s) -> p c s", s=PACK), w3_raw[:, :, P : N - P].rearrange("p s c -> p c s"), 1.0, 0.0, ALU.mult, ALU.add)
+        w3_rest = keep.tile([P, (N - P) * PACK], BF16, name="w3_rest", tag=f"e{TILES - 1}_0", align_bytes=64)
+        nc.gpsimd.tensor_scalar(w3_rest[:].rearrange("p (c s) -> p c s", s=PACK), w3_raw[:, :, : N - P].rearrange("p s c -> p c s"), 1.0, 0.0, ALU.mult, ALU.add)
         make_z(0, 1)
         make_z(1, 1)
         interleave_z(0)
@@ -280,10 +334,11 @@ def tile_picked_nlmean_none_p_kernel(tc, x_words, x_scales, w1, w2, w3, offs, p1
         make_z(3, 2)
         interleave_z(2)
         interleave_z(3)
-        quantise_w3(keep.tile([P, P], U32, name="w3_word_first", align_bytes=64), w3_first, 0, 1, 0)
+        w3_words = keep.tile([P, N - P], U32, name="w3_words", tag="inv2", align_bytes=64)
+        quantise_w3(w3_words, w3_rest, 0, 1, 0)
         quantise_z(0)
         quantise_z(1)
-        quantise_w3(keep.tile([P, N // 2], U32, name="w3_word_rest", tag="inv2", align_bytes=64), w3_rest, 1, TILES - 1, 1)
+        quantise_w3(w3_words, w3_rest, 1, TILES - 1, 0)
         quantise_w3(keep.tile([P, P], U32, name="w3_word_last", align_bytes=64), w3_last, TILES - 1, TILES, TILES - 1)
         quantise_z(2)
         quantise_z(3)

@@ -127,8 +127,8 @@ def tile_picked_nlmean_none_p_kernel(tc, x_words, x_scales, w1, w2, w3, offs, p1
             for b in range(BLOCKS):
                 nc.tensor.matmul(diff[t, n][:, block(b)], negated[:, block(b)], ident[:], start=False, stop=(b == BLOCKS - 1), is_transpose=True)
 
-        def make_square(t, n):
-            square[t, n] = keep.tile([P, S], F32, name=f"square{t}_{n}", tag=f"square{t}_{n}", align_bytes=64)
+        def make_square(t, n, tag=None):
+            square[t, n] = keep.tile([P, S], F32, name=f"square{t}_{n}", tag=tag or f"square{t}_{n}", align_bytes=64)
             nc.scalar.activation(square[t, n][:], diff[t, n][:], ACT.Square)
 
         def turn_square_back(t, n, bank, bufs):
@@ -183,10 +183,15 @@ def tile_picked_nlmean_none_p_kernel(tc, x_words, x_scales, w1, w2, w3, offs, p1
             for b in range(b0, b1):
                 add_to_num(t, b, term[:, block(b - b0)], last=(t == TILES - 1 and n == 0))
 
-        inv = [keep.tile([P, H], F32, name=f"inv{b}", tag=f"inv{b}", align_bytes=64) for b in range(BLOCKS)]
+        inv = {}
 
-        def make_inv(b):
-            nc.scalar.activation(inv[b][:], den_sq[:, b, :], ACT.Abs_reciprocal_sqrt)
+        def make_inv(b, part=lambda row: row):
+            if b not in inv:
+                inv[b] = keep.tile([P, H], F32, name=f"inv{b}", tag=f"inv{b}" if b else f"square{TILES - 1}_0", align_bytes=64)
+            nc.scalar.activation(part(inv[b][:]), part(den_sq[:, b, :]), ACT.Abs_reciprocal_sqrt)
+
+        def tile_columns(t):
+            return lambda row: row.rearrange("j (u g h q) -> j u h g q", u=2, g=HEADS, h=2)[:, t // 2, t % 2]
 
         z_word = keep.tile([P, S], U32, name="z_word", align_bytes=64)
         z_scale = keep.tile([P, S], U8, name="z_scale", align_bytes=64)
@@ -243,13 +248,13 @@ def tile_picked_nlmean_none_p_kernel(tc, x_words, x_scales, w1, w2, w3, offs, p1
         cast_w2_on_gpsimd(0)
         cast_w2_on_gpsimd(1)
         make_c(1, "den", 2)
-        nc.gpsimd.tensor_scalar(c_own[1], c_win[1][:, :S], 1.0, 0.0, ALU.mult, ALU.add)
         make_c(3, "den", 2)
         make_c(2, "num0", 1)
         fetch_negated(3, 1, on_scalar=True)
+        nc.vector.tensor_copy(c_own[1], c_win[1][:, :S])
         quantise_weights(W2, 0, TILES)
-        make_diff(1, 0, "diff1_0")
-        make_diff(1, 1, "diff1_1")
+        make_diff(1, 0, "w2_raw1")
+        make_diff(1, 1, "w_bf16_1")
         make_diff(2, 0, "diff2_0")
         make_diff(2, 1, "diff2_1")
         make_diff(3, 0, "diff3_0")
@@ -264,7 +269,7 @@ def tile_picked_nlmean_none_p_kernel(tc, x_words, x_scales, w1, w2, w3, offs, p1
         turn_diff(3, 1, "num1")
         make_val(0)
         make_e(0, 0)
-        make_square(1, 0)
+        make_square(1, 0, "square0_1")
         make_e(0, 1)
 
         w3_raw = keep.tile([P, PACK, N], F32, name="w3_raw", tag="square0_0", align_bytes=64)
@@ -278,10 +283,10 @@ def tile_picked_nlmean_none_p_kernel(tc, x_words, x_scales, w1, w2, w3, offs, p1
             for m in range(m0, m1):
                 w3_word[m] = words[:, (m - base) * P : (m - base + 1) * P]
 
-        make_square(1, 1)
-        make_e(1, 0)
+        make_square(1, 1, "w2_raw1")
         make_square(3, 1)
         turn_square_back(3, 1, "num0", 1)
+        make_e(1, 0)
         add_to_den(0, 0)
         add_to_den(0, 1)
         add_to_den(1, 0)
@@ -293,7 +298,7 @@ def tile_picked_nlmean_none_p_kernel(tc, x_words, x_scales, w1, w2, w3, offs, p1
         add_val(0)
         add_val(1)
         square_den(0)
-        make_term(0, 0, 0, BLOCKS, "term0_0")
+        make_term(0, 0, 0, BLOCKS, "square3_1")
         make_term(0, 1, 0, BLOCKS, "term0_1")
         make_square(2, 1)
         make_e(2, 0)
@@ -311,19 +316,25 @@ def tile_picked_nlmean_none_p_kernel(tc, x_words, x_scales, w1, w2, w3, offs, p1
         make_val(3)
         add_val(3)
         make_term(1, 1, 0, BLOCKS, "term1_1")
+        w3_first = keep.tile([P, P * PACK], BF16, name="w3_first", align_bytes=64)
+        nc.vector.tensor_copy(w3_first[:].rearrange("p (c i s) -> p c s i", i=LINE, s=PACK), w3_raw[:, :, :P].rearrange("p s (c i) -> p c s i", i=LINE))
+        quantise_w3(keep.tile([P, P], U32, name="w3_word_first", tag="diff2_1", align_bytes=64), w3_first, 0, 1, 0)
         make_term(2, 0, 0, BLOCKS, "term2_0")
         make_term(2, 1, 0, BLOCKS, "term2_1")
+        make_inv(0, lambda row: row[:, : H // 2])
         square_den(2)
         square_den(TILES - 1)
+        make_inv(0, tile_columns(2))
+        make_inv(0, tile_columns(3))
         for b0 in (0, 2):
             for n in (1, 0):
                 make_term(TILES - 1, n, b0, b0 + 2, f"term3_{b0}_{n}")
 
         sc, vc = nc.scalar.copy, nc.vector.tensor_copy
-        for b in range(BLOCKS):
+        for b in range(1, BLOCKS):
             make_inv(b)
-        w3_rest = keep.tile([P, (N - P) * PACK], BF16, name="w3_rest", tag=f"e{TILES - 1}_0", align_bytes=64)
-        nc.gpsimd.tensor_scalar(w3_rest[:].rearrange("p (c s) -> p c s", s=PACK), w3_raw[:, :, : N - P].rearrange("p s c -> p c s"), 1.0, 0.0, ALU.mult, ALU.add)
+        w3_rest = keep.tile([P, N // 2 * PACK], BF16, name="w3_rest", tag=f"e{TILES - 1}_0", align_bytes=64)
+        nc.gpsimd.tensor_scalar(w3_rest[:].rearrange("p (c s) -> p c s", s=PACK), w3_raw[:, :, P : N - P].rearrange("p s c -> p c s"), 1.0, 0.0, ALU.mult, ALU.add)
         make_z(0, 1)
         make_z(1, 1)
         interleave_z(0)
@@ -334,11 +345,9 @@ def tile_picked_nlmean_none_p_kernel(tc, x_words, x_scales, w1, w2, w3, offs, p1
         make_z(3, 2)
         interleave_z(2)
         interleave_z(3)
-        w3_words = keep.tile([P, N - P], U32, name="w3_words", tag="inv2", align_bytes=64)
-        quantise_w3(w3_words, w3_rest, 0, 1, 0)
         quantise_z(0)
         quantise_z(1)
-        quantise_w3(w3_words, w3_rest, 1, TILES - 1, 0)
+        quantise_w3(keep.tile([P, N // 2], U32, name="w3_word_rest", tag="inv2", align_bytes=64), w3_rest, 1, TILES - 1, 1)
         quantise_w3(keep.tile([P, P], U32, name="w3_word_last", align_bytes=64), w3_last, TILES - 1, TILES, TILES - 1)
         quantise_z(2)
         quantise_z(3)

@@ -57,6 +57,16 @@ def tile_picked_nlmean_none_p_kernel(tc, x_words, x_scales, w1, w2, w3, offs, p1
         nc.sync.dma_start(p_sb[1][:], p2)
         nc.sync.dma_start(w2_raw[1][:], w2_rows[:, :, H // 2 :])
 
+        w3_rows = w3.rearrange("(blk u r e) c -> u e blk r c", u=2, r=8, e=2)
+
+        def load_w3(name, c0, c1, tag):
+            raw = keep.tile([P, PACK, c1 - c0], F32, name=name, tag=tag, align_bytes=64)
+            for s in range(PACK):
+                nc.sync.dma_start(raw[:, s, :], w3_rows[s // 2, s % 2][:, :, c0:c1])
+            return raw
+
+        w3_raw_first = load_w3("w3_raw_first", 0, P, "w3_raw_first")
+
         ident = keep.tile([P, P], F32, name="ident")
         make_identity(nc, ident[:])
 
@@ -64,7 +74,8 @@ def tile_picked_nlmean_none_p_kernel(tc, x_words, x_scales, w1, w2, w3, offs, p1
         for t in range(TILES):
             nc.vector.memset(c_win[t][:, S:], 0.0)
         val = [keep.tile([P, 2 * S if t < TILES - 1 else S], F32, name=f"val{t}") for t in range(TILES)]
-        c_own = {t: val[t - 1][:, S:] for t in range(1, TILES)}
+        nc.vector.memset(val[2][:, S:], 0.0)
+        c_own = {t: val[t - 2][:, S:] for t in range(2, TILES)}
 
         w_bf16 = [keep.tile([P, H * PACK], BF16, name=f"w_bf16_{w}", tag=f"w_bf16_{w}", align_bytes=64) for w in (W1, W2)]
         w_word = [keep.tile([P, H], U32, name=f"w_word{w}", align_bytes=64) for w in (W1, W2)]
@@ -84,8 +95,8 @@ def tile_picked_nlmean_none_p_kernel(tc, x_words, x_scales, w1, w2, w3, offs, p1
         nc.vector.tensor_copy(x_scale[:], x_scale_all[:].indirect(offs_sb[:]))
 
         for t in range(TILES):
-            cast_tile_columns(W1, nc.vector.tensor_copy if t in (0, TILES - 1) else nc.scalar.copy, t, w1_raw, 0, HEADS)
-        for t in (0, 1, 3, 2):
+            cast_tile_columns(W1, nc.vector.tensor_copy if t % 2 == 0 else nc.scalar.copy, t, w1_raw, 0, HEADS)
+        for t in (0, 2, 1, 3):
             quantise_weights(W1, t, t + 1)
 
         def product_with_x(w, t, j0, j1, bank, bufs):
@@ -129,7 +140,10 @@ def tile_picked_nlmean_none_p_kernel(tc, x_words, x_scales, w1, w2, w3, offs, p1
 
         def make_square(t, n, tag=None):
             square[t, n] = keep.tile([P, S], F32, name=f"square{t}_{n}", tag=tag or f"square{t}_{n}", align_bytes=64)
-            nc.scalar.activation(square[t, n][:], diff[t, n][:], ACT.Square)
+            shared = HALF if (t, n) == (TILES - 1, 0) else 0
+            if shared:
+                nc.vector.tensor_tensor(square[t, n][:, :shared], diff[t, n][:, :shared], diff[t, n][:, :shared], ALU.mult)
+            nc.scalar.activation(square[t, n][:, shared:], diff[t, n][:, shared:], ACT.Square)
 
         def turn_square_back(t, n, bank, bufs):
             turned = square[t, n]
@@ -181,13 +195,13 @@ def tile_picked_nlmean_none_p_kernel(tc, x_words, x_scales, w1, w2, w3, offs, p1
             term = keep.tile([P, j1 - j0], F32, name=f"term{t}_{b0}_{n}", tag=tag, align_bytes=64)
             nc.vector.tensor_tensor(term[:], val[t][:].indirect(entries(p_sb[n], j0, j1)), e[t][n][:, j0:j1], ALU.mult)
             for b in range(b0, b1):
-                add_to_num(t, b, term[:, block(b - b0)], last=(t == TILES - 1 and n == 0))
+                add_to_num(t, b, term[:, block(b - b0)], last=(t == TILES - 1 and n == 1))
 
         inv = {}
 
         def make_inv(b, part=lambda row: row):
             if b not in inv:
-                inv[b] = keep.tile([P, H], F32, name=f"inv{b}", tag=f"inv{b}" if b else f"square{TILES - 1}_0", align_bytes=64)
+                inv[b] = keep.tile([P, H], F32, name=f"inv{b}", tag=f"inv{b}" if b else f"square{TILES - 1}_1", align_bytes=64)
             nc.scalar.activation(part(inv[b][:]), part(den_sq[:, b, :]), ACT.Abs_reciprocal_sqrt)
 
         def tile_columns(t):
@@ -247,35 +261,36 @@ def tile_picked_nlmean_none_p_kernel(tc, x_words, x_scales, w1, w2, w3, offs, p1
 
         cast_w2_on_gpsimd(0)
         cast_w2_on_gpsimd(1)
+        w3_first = keep.tile([P, P * PACK], BF16, name="w3_first", align_bytes=64)
+        nc.gpsimd.tensor_scalar(w3_first[:].rearrange("p (c s) -> p c s", s=PACK), w3_raw_first[:].rearrange("p s c -> p c s"), 1.0, 0.0, ALU.mult, ALU.add)
+        make_c(2, "den", 2)
         make_c(1, "den", 2)
-        make_c(3, "den", 2)
-        make_c(2, "num0", 1)
-        fetch_negated(3, 1, on_scalar=True)
-        nc.vector.tensor_copy(c_own[1], c_win[1][:, :S])
+        make_c(3, "num0", 1)
+        fetch_negated(1, 0)
+        fetch_negated(1, 1, on_scalar=True)
         quantise_weights(W2, 0, TILES)
-        make_diff(1, 0, "w2_raw1")
-        make_diff(1, 1, "w_bf16_1")
-        make_diff(2, 0, "diff2_0")
-        make_diff(2, 1, "diff2_1")
+        make_diff(2, 0, "w2_raw1")
+        make_diff(2, 1, "w_bf16_1")
         make_diff(3, 0, "diff3_0")
+        make_diff(3, 1, "diff3_1")
         turn_diff(0, 0, "num1")
         turn_diff(0, 1, "num2")
-        multiply_val(0)
+        turn_diff(1, 1, "num3")
         make_square(0, 0)
         turn_square_back(0, 0, "den", 2)
         make_square(0, 1)
         turn_square_back(0, 1, "den", 2)
+        multiply_val(0)
+        turn_diff(1, 0, "num1")
+        make_square(1, 1)
+        turn_square_back(1, 1, "num0", 1)
         multiply_val(1)
-        turn_diff(3, 1, "num1")
-        make_val(0)
         make_e(0, 0)
-        make_square(1, 0, "square0_1")
+        make_square(2, 0, "square0_0")
         make_e(0, 1)
+        make_val(0)
 
-        w3_raw = keep.tile([P, PACK, N], F32, name="w3_raw", tag="square0_0", align_bytes=64)
-        for u in range(2):
-            nc.sync.dma_start(w3_raw[:, 2 * u : 2 * u + 2, :].rearrange("p e c -> p (e c)"),
-                              w3.rearrange("(blk u r e) c -> u blk r (e c)", u=2, r=8, e=2)[u])
+        w3_raw = load_w3("w3_raw", P, N, "square0_1")
 
         def quantise_w3(words, values, m0, m1, base):
             nc.vector.quantize_mx(out=words[:, (m0 - base) * P : (m1 - base) * P].bitcast(FP8X4), scales=w_scale[W3][:, m0 * P : m1 * P],
@@ -283,42 +298,39 @@ def tile_picked_nlmean_none_p_kernel(tc, x_words, x_scales, w1, w2, w3, offs, p1
             for m in range(m0, m1):
                 w3_word[m] = words[:, (m - base) * P : (m - base + 1) * P]
 
-        make_square(1, 1, "w2_raw1")
-        make_square(3, 1)
-        turn_square_back(3, 1, "num0", 1)
-        make_e(1, 0)
+        make_square(1, 0)
+        turn_square_back(1, 0, "num2", 1)
+        make_square(2, 1, "w2_raw1")
+        make_e(1, 1)
         add_to_den(0, 0)
         add_to_den(0, 1)
-        add_to_den(1, 0)
-        make_e(1, 1)
         add_to_den(1, 1)
+        make_e(2, 0)
+        make_square(3, 0)
         make_val(1)
-        make_square(2, 0)
-        make_e(3, 1)
+        make_e(1, 0)
+        add_to_den(1, 0)
         add_val(0)
         add_val(1)
         square_den(0)
-        make_term(0, 0, 0, BLOCKS, "square3_1")
-        make_term(0, 1, 0, BLOCKS, "term0_1")
-        make_square(2, 1)
-        make_e(2, 0)
         add_to_den(2, 0)
-        make_val(2)
-        add_val(2)
-        square_den(1)
-        add_to_den(3, 1)
-        make_term(1, 0, 0, BLOCKS, "term1_0")
-        make_square(3, 0)
+        make_term(0, 0, 0, BLOCKS, "term0_0")
+        make_term(0, 1, 0, BLOCKS, "term0_1")
         make_e(2, 1)
         add_to_den(2, 1)
+        make_square(3, 1)
+        make_val(2)
+        add_val(2)
+        make_term(1, 0, 0, BLOCKS, "term1_0")
+        square_den(1)
         make_e(3, 0)
         add_to_den(3, 0)
+        make_e(3, 1)
+        add_to_den(3, 1)
         make_val(3)
         add_val(3)
         make_term(1, 1, 0, BLOCKS, "term1_1")
-        w3_first = keep.tile([P, P * PACK], BF16, name="w3_first", align_bytes=64)
-        nc.vector.tensor_copy(w3_first[:].rearrange("p (c i s) -> p c s i", i=LINE, s=PACK), w3_raw[:, :, :P].rearrange("p s (c i) -> p c s i", i=LINE))
-        quantise_w3(keep.tile([P, P], U32, name="w3_word_first", tag="diff2_1", align_bytes=64), w3_first, 0, 1, 0)
+        quantise_w3(keep.tile([P, P], U32, name="w3_word_first", tag="diff3_0", align_bytes=64), w3_first, 0, 1, 0)
         make_term(2, 0, 0, BLOCKS, "term2_0")
         make_term(2, 1, 0, BLOCKS, "term2_1")
         make_inv(0, lambda row: row[:, : H // 2])
@@ -327,21 +339,21 @@ def tile_picked_nlmean_none_p_kernel(tc, x_words, x_scales, w1, w2, w3, offs, p1
         make_inv(0, tile_columns(2))
         make_inv(0, tile_columns(3))
         for b0 in (0, 2):
-            for n in (1, 0):
+            for n in range(2):
                 make_term(TILES - 1, n, b0, b0 + 2, f"term3_{b0}_{n}")
 
         sc, vc = nc.scalar.copy, nc.vector.tensor_copy
         for b in range(1, BLOCKS):
             make_inv(b)
-        w3_rest = keep.tile([P, N // 2 * PACK], BF16, name="w3_rest", tag=f"e{TILES - 1}_0", align_bytes=64)
-        nc.gpsimd.tensor_scalar(w3_rest[:].rearrange("p (c s) -> p c s", s=PACK), w3_raw[:, :, P : N - P].rearrange("p s c -> p c s"), 1.0, 0.0, ALU.mult, ALU.add)
+        w3_rest = keep.tile([P, N // 2 * PACK], BF16, name="w3_rest", tag=f"e{TILES - 1}_1", align_bytes=64)
+        nc.gpsimd.tensor_scalar(w3_rest[:].rearrange("p (c s) -> p c s", s=PACK), w3_raw[:, :, : N // 2].rearrange("p s c -> p c s"), 1.0, 0.0, ALU.mult, ALU.add)
         make_z(0, 1)
         make_z(1, 1)
         interleave_z(0)
         make_z(2, 1)
         interleave_z(1)
         w3_last = keep.tile([P, P * PACK], BF16, name="w3_last", tag="z_rows1", align_bytes=64)
-        nc.scalar.copy(w3_last[:].rearrange("p (c i s) -> p c s i", i=LINE, s=PACK), w3_raw[:, :, N - P :].rearrange("p s (c i) -> p c s i", i=LINE))
+        nc.scalar.copy(w3_last[:].rearrange("p (c i s) -> p c s i", i=LINE, s=PACK), w3_raw[:, :, N // 2 :].rearrange("p s (c i) -> p c s i", i=LINE))
         make_z(3, 2)
         interleave_z(2)
         interleave_z(3)

@@ -25,6 +25,7 @@ HALF = S // 2
 PER_COLUMN = 16
 LINE = 4
 W1, W2, W3 = 0, 1, 2
+LAST = TILES - 1
 
 
 def tile_picked_nlmean_none_p_kernel(tc, x_words, x_scales, w1, w2, w3, offs, p1, p2, out):
@@ -55,7 +56,6 @@ def tile_picked_nlmean_none_p_kernel(tc, x_words, x_scales, w1, w2, w3, offs, p1
         w2_rows = w2.rearrange("(p s) c -> p s c", s=PACK)
         nc.sync.dma_start(w2_raw[0][:], w2_rows[:, :, : H // 2])
         nc.sync.dma_start(p_sb[1][:], p2)
-        nc.sync.dma_start(w2_raw[1][:], w2_rows[:, :, H // 2 :])
 
         w3_rows = w3.rearrange("(blk u r e) c -> u e blk r c", u=2, r=8, e=2)
 
@@ -66,6 +66,7 @@ def tile_picked_nlmean_none_p_kernel(tc, x_words, x_scales, w1, w2, w3, offs, p1
             return raw
 
         w3_raw_first = load_w3("w3_raw_first", 0, P, "w3_raw_first")
+        nc.sync.dma_start(w2_raw[1][:], w2_rows[:, :, H // 2 :])
 
         ident = keep.tile([P, P], F32, name="ident")
         make_identity(nc, ident[:])
@@ -114,10 +115,14 @@ def tile_picked_nlmean_none_p_kernel(tc, x_words, x_scales, w1, w2, w3, offs, p1
             return acc
 
         diff, square = {}, {}
-        e = [[keep.tile([P, S], F32, name=f"e{t}_{n}", tag=f"e{t}_{n}", align_bytes=64) for n in range(2)] for t in range(TILES)]
+        e = [[keep.tile([P, S], F32, name=f"e{t}_{n}", tag=f"e{t}_{n}", align_bytes=64)[:] for n in range(2)] for t in range(LAST)]
+        last_diff = keep.tile([P, 2 * S], F32, name="last_diff", tag="last_diff", align_bytes=64)
+        last_square = keep.tile([P, 2 * S], F32, name="last_square", tag="last_square", align_bytes=64)
+        last_e = keep.tile([P, 2 * S], F32, name="last_e", tag="last_e", align_bytes=64)
+        e.append([last_e[:, n * S : (n + 1) * S] for n in range(2)])
 
         def make_diff(t, n, tag):
-            diff[t, n] = keep.tile([P, S], F32, name=f"diff{t}_{n}", tag=tag, align_bytes=64)
+            diff[t, n] = keep.tile([P, S], F32, name=f"diff{t}_{n}", tag=tag, align_bytes=64) if tag else last_diff[:, n * S : (n + 1) * S]
             nc.vector.tensor_tensor(diff[t, n][:], c_win[t][:].indirect(p_sb[n][:]), c_own[t], ALU.subtract)
 
         def block(b):
@@ -140,10 +145,7 @@ def tile_picked_nlmean_none_p_kernel(tc, x_words, x_scales, w1, w2, w3, offs, p1
 
         def make_square(t, n, tag=None):
             square[t, n] = keep.tile([P, S], F32, name=f"square{t}_{n}", tag=tag or f"square{t}_{n}", align_bytes=64)
-            shared = HALF if (t, n) == (TILES - 1, 0) else 0
-            if shared:
-                nc.vector.tensor_tensor(square[t, n][:, :shared], diff[t, n][:, :shared], diff[t, n][:, :shared], ALU.mult)
-            nc.scalar.activation(square[t, n][:, shared:], diff[t, n][:, shared:], ACT.Square)
+            nc.scalar.activation(square[t, n][:], diff[t, n][:], ACT.Square)
 
         def turn_square_back(t, n, bank, bufs):
             turned = square[t, n]
@@ -201,7 +203,7 @@ def tile_picked_nlmean_none_p_kernel(tc, x_words, x_scales, w1, w2, w3, offs, p1
 
         def make_inv(b, part=lambda row: row):
             if b not in inv:
-                inv[b] = keep.tile([P, H], F32, name=f"inv{b}", tag=f"inv{b}" if b else f"square{TILES - 1}_1", align_bytes=64)
+                inv[b] = keep.tile([P, H], F32, name=f"inv{b}", tag=f"inv{b}" if b else "last_square", align_bytes=64)
             nc.scalar.activation(part(inv[b][:]), part(den_sq[:, b, :]), ACT.Abs_reciprocal_sqrt)
 
         def tile_columns(t):
@@ -259,10 +261,10 @@ def tile_picked_nlmean_none_p_kernel(tc, x_words, x_scales, w1, w2, w3, offs, p1
             nc.gpsimd.tensor_scalar(w_bf16[W2][:].rearrange("p (u h g q s) -> p u g h q s", u=2, h=2, g=HEADS, s=PACK)[:, u, HEADS // 2 :],
                                     w2_raw[1][:].rearrange("p s (g h u q) -> p u g h q s", g=HEADS // 2, h=2, u=2)[:, u], 1.0, 0.0, ALU.mult, ALU.add)
 
+        w3_first = keep.tile([P, P * PACK], BF16, name="w3_first", tag="w2_raw0", align_bytes=64)
+        nc.gpsimd.tensor_scalar(w3_first[:].rearrange("p (c s) -> p c s", s=PACK), w3_raw_first[:].rearrange("p s c -> p c s"), 1.0, 0.0, ALU.mult, ALU.add)
         cast_w2_on_gpsimd(0)
         cast_w2_on_gpsimd(1)
-        w3_first = keep.tile([P, P * PACK], BF16, name="w3_first", align_bytes=64)
-        nc.gpsimd.tensor_scalar(w3_first[:].rearrange("p (c s) -> p c s", s=PACK), w3_raw_first[:].rearrange("p s c -> p c s"), 1.0, 0.0, ALU.mult, ALU.add)
         make_c(2, "den", 2)
         make_c(1, "den", 2)
         make_c(3, "num0", 1)
@@ -271,8 +273,9 @@ def tile_picked_nlmean_none_p_kernel(tc, x_words, x_scales, w1, w2, w3, offs, p1
         quantise_weights(W2, 0, TILES)
         make_diff(2, 0, "w2_raw1")
         make_diff(2, 1, "w_bf16_1")
-        make_diff(3, 0, "diff3_0")
-        make_diff(3, 1, "diff3_1")
+        make_diff(3, 0, None)
+        make_diff(3, 1, None)
+        nc.vector.tensor_tensor(last_square[:, :HALF], last_diff[:, :HALF], last_diff[:, :HALF], ALU.mult)
         turn_diff(0, 0, "num1")
         turn_diff(0, 1, "num2")
         turn_diff(1, 1, "num3")
@@ -306,7 +309,7 @@ def tile_picked_nlmean_none_p_kernel(tc, x_words, x_scales, w1, w2, w3, offs, p1
         add_to_den(0, 1)
         add_to_den(1, 1)
         make_e(2, 0)
-        make_square(3, 0)
+        make_e(2, 1)
         make_val(1)
         make_e(1, 0)
         add_to_den(1, 0)
@@ -314,23 +317,21 @@ def tile_picked_nlmean_none_p_kernel(tc, x_words, x_scales, w1, w2, w3, offs, p1
         add_val(1)
         square_den(0)
         add_to_den(2, 0)
+        add_to_den(2, 1)
         make_term(0, 0, 0, BLOCKS, "term0_0")
         make_term(0, 1, 0, BLOCKS, "term0_1")
-        make_e(2, 1)
-        add_to_den(2, 1)
-        make_square(3, 1)
+        nc.scalar.activation(last_square[:, HALF:], last_diff[:, HALF:], ACT.Square)
         make_val(2)
         add_val(2)
         make_term(1, 0, 0, BLOCKS, "term1_0")
         square_den(1)
-        make_e(3, 0)
+        nc.scalar.activation(last_e[:], last_square[:], ACT.Exp, scale=-0.5)
         add_to_den(3, 0)
-        make_e(3, 1)
         add_to_den(3, 1)
         make_val(3)
         add_val(3)
         make_term(1, 1, 0, BLOCKS, "term1_1")
-        quantise_w3(keep.tile([P, P], U32, name="w3_word_first", tag="diff3_0", align_bytes=64), w3_first, 0, 1, 0)
+        quantise_w3(keep.tile([P, P], U32, name="w3_word_first", tag="last_diff", align_bytes=64), w3_first, 0, 1, 0)
         make_term(2, 0, 0, BLOCKS, "term2_0")
         make_term(2, 1, 0, BLOCKS, "term2_1")
         make_inv(0, lambda row: row[:, : H // 2])
@@ -345,7 +346,7 @@ def tile_picked_nlmean_none_p_kernel(tc, x_words, x_scales, w1, w2, w3, offs, p1
         sc, vc = nc.scalar.copy, nc.vector.tensor_copy
         for b in range(1, BLOCKS):
             make_inv(b)
-        w3_rest = keep.tile([P, N // 2 * PACK], BF16, name="w3_rest", tag=f"e{TILES - 1}_1", align_bytes=64)
+        w3_rest = keep.tile([P, N // 2 * PACK], BF16, name="w3_rest", tag="last_e", align_bytes=64)
         nc.gpsimd.tensor_scalar(w3_rest[:].rearrange("p (c s) -> p c s", s=PACK), w3_raw[:, :, : N // 2].rearrange("p s c -> p c s"), 1.0, 0.0, ALU.mult, ALU.add)
         make_z(0, 1)
         make_z(1, 1)

from contextlib import ExitStack

import concourse.mybir as mybir
from concourse.masks import make_identity

K, T, S, H, N = 512, 2048, 512, 512, 512
FLOPS = 2 * K * H * S * 2 + 2 * H * N * S

F32 = mybir.dt.float32
BF16 = mybir.dt.bfloat16
I32 = mybir.dt.int32
U32 = mybir.dt.uint32
U16 = mybir.dt.uint16
U8 = mybir.dt.uint8
FP8X4 = mybir.dt.float8_e4m3fn_x4
ALU = mybir.AluOpType
ACT = mybir.ActivationFunctionType

P = 128
PACK = 4
TILES = H // P
HEADS = 8
BLOCKS = S // P
HALF = S // 2
PER_COLUMN = 16
LINE = 4
W1, W2, W3 = 0, 1, 2
LAST = TILES - 1


def tile_picked_nlmean_none_p_kernel(tc, x_words, x_scales, w1, w2, w3, offs, p1, p2, out):
    nc = tc.nc
    with ExitStack() as ctx:
        lists = ctx.enter_context(tc.tile_pool(name="lists", bufs=1))
        keep = ctx.enter_context(tc.tile_pool(name="keep", bufs=1))
        psum = ctx.enter_context(tc.psum_pool(name="psum", bufs=1))

        offs_sb = lists.tile([P, S // PER_COLUMN], U16, name="offs_sb")
        p_sb = [lists.tile([P, S // PER_COLUMN], U16, name=f"p_sb{n}") for n in range(2)]

        def entries(list_tile, j0, j1):
            return list_tile[:, j0 // PER_COLUMN : j1 // PER_COLUMN]

        x_scale_all = keep.tile([P, T], U8, name="x_scale_all", align_bytes=64)
        nc.vector.memset(x_scale_all[:].bitcast(I32), 0)
        x_word_all = keep.tile([P, T], U32, name="x_word_all", align_bytes=64)
        w1_raw = keep.tile([P, PACK, H], F32, name="w1_raw")
        w2_raw = [keep.tile([P, PACK, H // 2], F32, name=f"w2_raw{h}", tag=f"w2_raw{h}", align_bytes=64) for h in range(2)]

        nc.sync.dma_start(x_word_all[:].bitcast(I32), x_words[0].rearrange("p n s -> p (n s)").bitcast(I32))
        nc.sync.dma_start(offs_sb[:], offs)
        for r in range(4):
            nc.sync.dma_start(x_scale_all[r::32, :].bitcast(I32), x_scales[0, r::4, :].bitcast(I32))
        nc.sync.dma_start(w1_raw[:], w1.rearrange("(p s) c -> p s c", s=PACK))
        nc.sync.dma_start(p_sb[0][:], p1)
        w2_rows = w2.rearrange("(p s) c -> p s c", s=PACK)
        nc.sync.dma_start(w2_raw[0][:], w2_rows[:, :, : H // 2])
        nc.sync.dma_start(p_sb[1][:], p2)

        w3_rows = w3.rearrange("(blk u r e) c -> u e blk r c", u=2, r=8, e=2)

        def load_w3(name, c0, c1, tag):
            raw = keep.tile([P, PACK, c1 - c0], F32, name=name, tag=tag, align_bytes=64)
            for s in range(PACK):
                nc.sync.dma_start(raw[:, s, :], w3_rows[s // 2, s % 2][:, :, c0:c1])
            return raw

        w3_raw_first = load_w3("w3_raw_first", 0, P, "w3_raw_first")
        nc.sync.dma_start(w2_raw[1][:], w2_rows[:, :, H // 2 :])

        ident = keep.tile([P, P], F32, name="ident")
        make_identity(nc, ident[:])

        c_win = [keep.tile([P, 2 * S], F32, name=f"c_win{t}") for t in range(TILES)]
        for t in range(TILES):
            nc.vector.memset(c_win[t][:, S:], 0.0)
        val = [keep.tile([P, 2 * S if t < TILES - 1 else S], F32, name=f"val{t}") for t in range(TILES)]
        nc.vector.memset(val[2][:, S:], 0.0)
        c_own = {t: val[t - 2][:, S:] for t in range(2, TILES)}

        w_bf16 = [keep.tile([P, H * PACK], BF16, name=f"w_bf16_{w}", tag=f"w_bf16_{w}", align_bytes=64) for w in (W1, W2)]
        w_word = [keep.tile([P, H], U32, name=f"w_word{w}", align_bytes=64) for w in (W1, W2)]
        w_scale = [keep.tile([P, H], U8, name=f"w_scale{w}", align_bytes=64) for w in (W1, W2, W3)]

        def cast_tile_columns(w, copy, t, src, g0, g1):
            copy(w_bf16[w][:].rearrange("p (t g c i s) -> p t g c s i", t=TILES, g=HEADS, i=LINE, s=PACK)[:, t, g0:g1],
                 src[:].rearrange("p s (g h u c i) -> p u h g c s i", g=g1 - g0, h=2, u=2, i=LINE)[:, t // 2, t % 2])

        def quantise_weights(w, t0, t1):
            nc.vector.quantize_mx(out=w_word[w][:, t0 * P : t1 * P].bitcast(FP8X4), scales=w_scale[w][:, t0 * P : t1 * P],
                                  in_=w_bf16[w][:, t0 * P * PACK : t1 * P * PACK])

        x_scale = keep.tile([P, S], U8, name="x_scale", align_bytes=64)
        x_word = keep.tile([P, S], U32, name="x_word", align_bytes=64)
        nc.vector.tensor_copy(x_word[:], x_word_all[:].indirect(offs_sb[:]))
        nc.vector.tensor_copy(x_scale[:], x_scale_all[:].indirect(offs_sb[:]))

        for t in range(TILES):
            cast_tile_columns(W1, nc.vector.tensor_copy if t % 2 == 0 else nc.scalar.copy, t, w1_raw, 0, HEADS)
        for t in (0, 2, 1, 3):
            quantise_weights(W1, t, t + 1)

        def product_with_x(w, t, j0, j1, bank, bufs):
            acc = psum.tile([P, S], F32, name="acc", tag=bank, bufs=bufs)
            cols = slice(t * P, (t + 1) * P)
            nc.tensor.matmul_mx(out=acc[:, : j1 - j0], lhsT=w_word[w][:, cols].bitcast(FP8X4), lhsT_scale=w_scale[w][:, cols],
                                rhs=x_word[:, j0:j1].bitcast(FP8X4), rhs_scale=x_scale[:, j0:j1], start=True, stop=True)
            return acc[:, : j1 - j0]

        def make_c(t, bank, bufs):
            acc = product_with_x(W1, t, 0, S, bank, bufs)
            nc.scalar.copy(c_win[t][:, :S], acc)
            if t > 1:
                nc.sync.dma_start(c_own[t], c_win[t][:, :S])
            return acc

        diff, square = {}, {}
        e = [[keep.tile([P, S], F32, name=f"e{t}_{n}", tag=f"e{t}_{n}", align_bytes=64)[:] for n in range(2)] for t in range(LAST)]
        last_diff = keep.tile([P, 2 * S], F32, name="last_diff", tag="last_diff", align_bytes=64)
        last_square = keep.tile([P, 2 * S], F32, name="last_square", tag="last_square", align_bytes=64)
        last_e = keep.tile([P, 2 * S], F32, name="last_e", tag="last_e", align_bytes=64)
        e.append([last_e[:, n * S : (n + 1) * S] for n in range(2)])

        def make_diff(t, n, tag):
            diff[t, n] = keep.tile([P, S], F32, name=f"diff{t}_{n}", tag=tag, align_bytes=64) if tag else last_diff[:, n * S : (n + 1) * S]
            nc.vector.tensor_tensor(diff[t, n][:], c_win[t][:].indirect(p_sb[n][:]), c_own[t], ALU.subtract)

        def block(b):
            return slice(b * P, (b + 1) * P)

        def fetch_negated(t, n, on_scalar=False):
            diff[t, n] = keep.tile([P, S], F32, name=f"negated{t}_{n}", tag=f"diff{t}_{n}", align_bytes=64)
            if on_scalar:
                nc.scalar.activation(diff[t, n][:], c_win[t][:].indirect(p_sb[n][:]), ACT.Copy, scale=-1.0)
            else:
                nc.vector.tensor_scalar(diff[t, n][:], c_win[t][:].indirect(p_sb[n][:]), -1.0, 0.0, ALU.mult, ALU.add)

        def turn_diff(t, n, bank):
            negated = diff[t, n]
            diff[t, n] = psum.tile([P, S], F32, name=f"turned{t}_{n}", tag=bank)
            for b in range(BLOCKS):
                nc.tensor.matmul(diff[t, n][:, block(b)], c_win[t][:, block(b)], ident[:], start=(b == 0), stop=False, is_transpose=True)
            for b in range(BLOCKS):
                nc.tensor.matmul(diff[t, n][:, block(b)], negated[:, block(b)], ident[:], start=False, stop=(b == BLOCKS - 1), is_transpose=True)

        def make_square(t, n, tag=None):
            square[t, n] = keep.tile([P, S], F32, name=f"square{t}_{n}", tag=tag or f"square{t}_{n}", align_bytes=64)
            nc.scalar.activation(square[t, n][:], diff[t, n][:], ACT.Square)

        def turn_square_back(t, n, bank, bufs):
            turned = square[t, n]
            square[t, n] = psum.tile([P, S], F32, name=f"square_back{t}_{n}", tag=bank, bufs=bufs)
            for b in range(BLOCKS):
                nc.tensor.transpose(square[t, n][:, block(b)], turned[:, block(b)], ident[:])

        den = {}

        def make_e(t, n):
            nc.scalar.activation(e[t][n][:], square[t, n][:], ACT.Exp, scale=-0.5)

        def add_to_den(t, n):
            first = t not in den
            if first:
                den[t] = psum.tile([P, S], F32, name="den", tag="den", bufs=2)
            for b in range(BLOCKS):
                nc.tensor.matmul(den[t][:, block(b)], e[t][n][:, block(b)], ident[:], start=(first and b == 0), stop=(not first and b == BLOCKS - 1), is_transpose=True)

        den_sq = keep.tile([P, BLOCKS, H], F32, name="den_sq")

        def square_den(t):
            nc.scalar.activation(den_sq[:].rearrange("j b (u g h q) -> j u h b g q", u=2, g=HEADS, h=2)[:, t // 2, t % 2],
                                 den[t][:].rearrange("j (b g q) -> j b g q", b=BLOCKS, g=HEADS), ACT.Square, bias=1.0)

        num = {}

        def add_to_num(t, b, term, first=False, last=False):
            if first:
                num[b] = psum.tile([P, S], F32, name=f"num{b}", tag=f"num{b}")
            nc.tensor.matmul(num[b][:].rearrange("j (u g h q) -> j u h g q", u=2, g=HEADS, h=2)[:, t // 2, t % 2], term, ident[:], start=first, stop=last, is_transpose=True)

        val_acc = {}

        def multiply_val(t):
            val_acc[t] = product_with_x(W2, t, 0, S, "acc", 2)

        def make_val(t):
            nc.scalar.copy(val[t][:, :S], val_acc[t])
            if t + 2 < TILES:
                multiply_val(t + 2)

        def add_val(t):
            for b in range(BLOCKS):
                add_to_num(t, b, val[t][:, b * P : (b + 1) * P], first=(t == 0))

        def make_term(t, n, b0, b1, tag):
            j0, j1 = b0 * P, b1 * P
            term = keep.tile([P, j1 - j0], F32, name=f"term{t}_{b0}_{n}", tag=tag, align_bytes=64)
            nc.vector.tensor_tensor(term[:], val[t][:].indirect(entries(p_sb[n], j0, j1)), e[t][n][:, j0:j1], ALU.mult)
            for b in range(b0, b1):
                add_to_num(t, b, term[:, block(b - b0)], last=(t == TILES - 1 and n == 1))

        inv = {}

        def make_inv(b, part=lambda row: row):
            if b not in inv:
                inv[b] = keep.tile([P, H], F32, name=f"inv{b}", tag=f"inv{b}" if b else "last_square", align_bytes=64)
            nc.scalar.activation(part(inv[b][:]), part(den_sq[:, b, :]), ACT.Abs_reciprocal_sqrt)

        def tile_columns(t):
            return lambda row: row.rearrange("j (u g h q) -> j u h g q", u=2, g=HEADS, h=2)[:, t // 2, t % 2]

        z_word = keep.tile([P, S], U32, name="z_word", align_bytes=64)
        z_scale = keep.tile([P, S], U8, name="z_scale", align_bytes=64)
        z_bf16 = [keep.tile([P, P * PACK], BF16, name=f"z_bf16_{b}", align_bytes=64) for b in range(BLOCKS)]
        back = {}

        def make_z(b, pieces):
            z_rows = keep.tile([P, H], BF16, name=f"z_rows{b}", tag=f"z_rows{b}", align_bytes=64)
            back[b] = psum.tile([P, 2, P], F32, name="back", tag="den" if b < 2 else "acc", bufs=2)
            width = H // pieces
            for i0 in range(0, H, width):
                nc.vector.tensor_tensor(z_rows[:, i0 : i0 + width], num[b][:, i0 : i0 + width], inv[b][:, i0 : i0 + width], ALU.mult)
                for u in range(i0 // (2 * P), (i0 + width) // (2 * P)):
                    nc.tensor.transpose(back[b][:, u, :], z_rows[:].bitcast(F32)[:, u * P : (u + 1) * P], ident[:])

        def interleave_z(b):
            nc.scalar.copy(z_bf16[b][:].bitcast(F32).rearrange("p (j u) -> p j u", u=2), back[b][:].rearrange("p u j -> p j u"))

        def quantise_z(b):
            nc.vector.quantize_mx(out=z_word[:, b * P : (b + 1) * P].bitcast(FP8X4), scales=z_scale[:, b * P : (b + 1) * P], in_=z_bf16[b][:])

        out_acc = {}
        w3_word = {}

        def multiply_out(j0, banks):
            per_bank = TILES // len(banks)
            out_acc[j0] = []
            for k, bank in enumerate(banks):
                acc = psum.tile([P, per_bank, HALF], F32, name="out_acc", tag=bank, bufs=2 if bank in ("den", "acc") else 1)
                for a in range(per_bank):
                    m = per_bank * k + a
                    nc.tensor.matmul_mx(out=acc[:, a, :], lhsT=w3_word[m].bitcast(FP8X4), lhsT_scale=w_scale[W3][:, m * P : (m + 1) * P],
                                        rhs=z_word[:, j0 : j0 + HALF].bitcast(FP8X4), rhs_scale=z_scale[:, j0 : j0 + HALF], start=True, stop=True)
                out_acc[j0].append(acc)

        def store_out(j0, copies):
            per_bank = TILES // len(copies)
            for k, copy in enumerate(copies):
                res = keep.tile([P, per_bank, HALF], F32, name=f"res{j0}_{k}")
                copy(res[:], out_acc[j0][k][:])
                nc.sync.dma_start(out.rearrange("(a p) j -> p a j", p=P)[:, per_bank * k : per_bank * (k + 1), j0 : j0 + HALF], res[:])

        halves = [product_with_x(W1, 0, j0, j0 + HALF, "acc", 2) for j0 in range(0, S, HALF)]
        nc.scalar.copy(c_win[0][:, :HALF], halves[0])
        nc.scalar.copy(c_win[0][:, HALF:S], halves[1])
        for t in range(TILES):
            cast_tile_columns(W2, nc.vector.tensor_copy, t, w2_raw[0], 0, HEADS // 2)
        fetch_negated(0, 0)
        fetch_negated(0, 1)
        def cast_w2_on_gpsimd(u):
            nc.gpsimd.tensor_scalar(w_bf16[W2][:].rearrange("p (u h g q s) -> p u g h q s", u=2, h=2, g=HEADS, s=PACK)[:, u, HEADS // 2 :],
                                    w2_raw[1][:].rearrange("p s (g h u q) -> p u g h q s", g=HEADS // 2, h=2, u=2)[:, u], 1.0, 0.0, ALU.mult, ALU.add)

        w3_first = keep.tile([P, P * PACK], BF16, name="w3_first", tag="w2_raw0", align_bytes=64)
        nc.gpsimd.tensor_scalar(w3_first[:].rearrange("p (c s) -> p c s", s=PACK), w3_raw_first[:].rearrange("p s c -> p c s"), 1.0, 0.0, ALU.mult, ALU.add)
        cast_w2_on_gpsimd(0)
        cast_w2_on_gpsimd(1)
        make_c(2, "den", 2)
        make_c(1, "den", 2)
        make_c(3, "num0", 1)
        fetch_negated(1, 0)
        fetch_negated(1, 1, on_scalar=True)
        quantise_weights(W2, 0, TILES)
        make_diff(2, 0, "w2_raw1")
        make_diff(2, 1, "w_bf16_1")
        make_diff(3, 0, None)
        make_diff(3, 1, None)
        nc.vector.tensor_tensor(last_square[:, :HALF], last_diff[:, :HALF], last_diff[:, :HALF], ALU.mult)
        turn_diff(0, 0, "num1")
        turn_diff(0, 1, "num2")
        turn_diff(1, 1, "num3")
        make_square(0, 0)
        turn_square_back(0, 0, "den", 2)
        make_square(0, 1)
        turn_square_back(0, 1, "den", 2)
        multiply_val(0)
        turn_diff(1, 0, "num1")
        make_square(1, 1)
        turn_square_back(1, 1, "num0", 1)
        multiply_val(1)
        make_e(0, 0)
        make_square(2, 0, "square0_0")
        make_e(0, 1)
        make_val(0)

        w3_raw = load_w3("w3_raw", P, N, "square0_1")

        def quantise_w3(words, values, m0, m1, base):
            nc.vector.quantize_mx(out=words[:, (m0 - base) * P : (m1 - base) * P].bitcast(FP8X4), scales=w_scale[W3][:, m0 * P : m1 * P],
                                  in_=values[:, (m0 - base) * P * PACK : (m1 - base) * P * PACK])
            for m in range(m0, m1):
                w3_word[m] = words[:, (m - base) * P : (m - base + 1) * P]

        make_square(1, 0)
        turn_square_back(1, 0, "num2", 1)
        make_square(2, 1, "w2_raw1")
        make_e(1, 1)
        add_to_den(0, 0)
        add_to_den(0, 1)
        add_to_den(1, 1)
        make_e(2, 0)
        make_e(2, 1)
        make_val(1)
        make_e(1, 0)
        add_to_den(1, 0)
        add_val(0)
        add_val(1)
        square_den(0)
        add_to_den(2, 0)
        add_to_den(2, 1)
        make_term(0, 0, 0, BLOCKS, "term0_0")
        make_term(0, 1, 0, BLOCKS, "term0_1")
        nc.scalar.activation(last_square[:, HALF:], last_diff[:, HALF:], ACT.Square)
        make_val(2)
        add_val(2)
        make_term(1, 0, 0, BLOCKS, "term1_0")
        square_den(1)
        nc.scalar.activation(last_e[:], last_square[:], ACT.Exp, scale=-0.5)
        add_to_den(3, 0)
        add_to_den(3, 1)
        make_val(3)
        add_val(3)
        make_term(1, 1, 0, BLOCKS, "term1_1")
        quantise_w3(keep.tile([P, P], U32, name="w3_word_first", tag="last_diff", align_bytes=64), w3_first, 0, 1, 0)
        make_term(2, 0, 0, BLOCKS, "term2_0")
        make_term(2, 1, 0, BLOCKS, "term2_1")
        make_inv(0, lambda row: row[:, : H // 2])
        square_den(2)
        square_den(TILES - 1)
        make_inv(0, tile_columns(2))
        make_inv(0, tile_columns(3))
        for b0 in (0, 2):
            for n in range(2):
                make_term(TILES - 1, n, b0, b0 + 2, f"term3_{b0}_{n}")

        sc, vc = nc.scalar.copy, nc.vector.tensor_copy
        for b in range(1, BLOCKS):
            make_inv(b)
        w3_rest = keep.tile([P, N // 2 * PACK], BF16, name="w3_rest", tag="last_e", align_bytes=64)
        nc.gpsimd.tensor_scalar(w3_rest[:].rearrange("p (c s) -> p c s", s=PACK), w3_raw[:, :, : N // 2].rearrange("p s c -> p c s"), 1.0, 0.0, ALU.mult, ALU.add)
        make_z(0, 1)
        make_z(1, 1)
        interleave_z(0)
        make_z(2, 1)
        interleave_z(1)
        w3_last = keep.tile([P, P * PACK], BF16, name="w3_last", tag="z_rows1", align_bytes=64)
        nc.scalar.copy(w3_last[:].rearrange("p (c i s) -> p c s i", i=LINE, s=PACK), w3_raw[:, :, N // 2 :].rearrange("p s (c i) -> p c s i", i=LINE))
        make_z(3, 2)
        interleave_z(2)
        interleave_z(3)
        quantise_z(0)
        quantise_z(1)
        quantise_w3(keep.tile([P, N // 2], U32, name="w3_word_rest", tag="inv2", align_bytes=64), w3_rest, 1, TILES - 1, 1)
        quantise_w3(keep.tile([P, P], U32, name="w3_word_last", align_bytes=64), w3_last, TILES - 1, TILES, TILES - 1)
        quantise_z(2)
        quantise_z(3)
        multiply_out(0, ["num0", "num1", "num2", "num3"])
        multiply_out(HALF, ["den", "den", "acc", "acc"])
        store_out(0, [sc, sc, sc, sc])
        store_out(HALF, [sc, vc, sc, vc])
